import numpy as np, ml_dtypes
CORES = [8,136,40,168]
N = 4
BF = ml_dtypes.bfloat16
def gentries(a):
    return np.ascontiguousarray(a.reshape(8, 16, -1).transpose(0, 2, 1)).reshape(8, -1)
def gtable(e):
    e = np.asarray(e); return np.ascontiguousarray(e.reshape(8, -1, 16).transpose(0, 2, 1)).reshape(128, -1).astype(np.int32)
M, L, T, H, A, R = 896, 128, 3, 2048, 9, 512
W = M + L * T; NONE = 4095
def hashes(w, a):
    u = np.matmul(w.transpose(0, 2, 1), a) & 4095
    return (((u[:, 0] * u[:, 1]) >> 5) + u[:, 1]) & (H - 1)
def some(rng, n, tops):
    return (rng.random((N, 8, 16, n)) * rng.choice(np.array(tops), (N, 8, 1, n))).astype(np.int64)
def places(rng, sizes):
    v = np.zeros((N, 8, L), np.int64)
    for r in range(N):
        for g in range(8):
            pool = rng.permutation(M)[:int(sizes[r, g])]; v[r, g] = pool[rng.integers(0, len(pool), L)]
    return v
def flat(a):
    return np.ascontiguousarray(a.reshape(N, 128, -1)).astype(np.float32).astype(BF)
def pack(X, B, E, x, v, w):
    return {"nodes": flat(X), "book": flat(B), "kids": np.ascontiguousarray(E.reshape(N, 128, M)).astype(np.int32), "cand": flat(x),
            "spot": np.stack([gtable(a) for a in v]), "wts": flat(w)}
def setup_inputs(rng):
    X = some(rng, M, (48, 96, 160, 256)); B = some(rng, H, (96, 160, 256)); x = some(rng, L, (96, 192, 256))
    k = np.minimum(rng.integers(0, 17, (N, 8, 16, M)), rng.integers(0, 17, (N, 8, 16, M)))
    fill = rng.choice(np.array([0.3, 0.6, 0.9, 1.0]), (N, 8, 1, M))
    E = 4096 * k + np.where(rng.random((N, 8, 16, M)) < fill, rng.integers(0, M, (N, 8, 16, M)), NONE)
    v = places(rng, rng.choice(np.array([8, 32, 128, M]), (N, 8)))
    return pack(X, B, E, x, v, rng.integers(0, 16, (N, 8, 16, 2)))
def setup_inputs_spread(rng):
    X = (np.exp2(8 * rng.random((N, 8, 1, M))) * rng.random((N, 8, 16, M))).astype(np.int64)
    x = (np.exp2(8 * rng.random((N, 8, 1, L))) * rng.random((N, 8, 16, L))).astype(np.int64); B = rng.integers(0, 256, (N, 8, 16, H))
    E = 4096 * rng.integers(0, 17, (N, 8, 16, M)) + np.where(rng.random((N, 8, 16, M)) < rng.random((N, 8, 1, M)), rng.integers(0, M, (N, 8, 16, M)), NONE)
    v = np.minimum((M * rng.random((N, 8, L)) ** 3).astype(np.int64), M - 1); w = np.minimum((16 * rng.random((N, 8, 16, 2)) ** 2).astype(np.int64), 15)
    return pack(X, B, E, x, v, w)
def setup_inputs_ends(rng):
    X = 255 * rng.integers(0, 2, (N, 8, 16, M)); B = 255 * rng.integers(0, 2, (N, 8, 16, H)); x = 255 * rng.integers(0, 2, (N, 8, 16, L))
    a = rng.random((N, 8, 1, L)); x = np.where(a < 0.15, 0, np.where(a < 0.4, 255, x))
    X[..., 0] = 0; X[..., M - 1] = 255
    w = 15 * rng.integers(0, 2, (N, 8, 16, 2)); w[:, ::2, 13] = 15; w[:, ::2, 14] = 1; w[:, ::2, 15] = 15; w[:, 7] = 15
    E = 69631 * rng.integers(0, 2, (N, 8, 16, M)); o = rng.random(E.shape)
    E = np.where(o < 0.35, rng.choice(np.array([65536, M - 1, M - 1 + 65536]), E.shape), E)
    E = np.where(o < 0.1, rng.integers(1, M - 16, E.shape) + 65536 * rng.integers(0, 2, E.shape), E)
    E[..., M - 1] = 69631 * rng.integers(0, 2, (N, 8, 16)); E[:, :, 15, M - 1] = M - 1 + 65536; low = rng.integers(0, 8, (N, 8))
    E[:, :, :15, M - 2] = 0; E[:, :, 15, M - 2] = 69631
    for j in range(1, T): E[:, :, :, M - 2 - j] = 65536 + M - 1 - j
    E[:, :, :15, M - 2 - T] = 69631; E[:, :, 15, M - 2 - T] = 0
    v = np.where(rng.random((N, 8, L)) < 0.68, (M - 1) * rng.integers(0, 2, (N, 8, L)), rng.integers(1, M - 16, (N, 8, L)))
    v[:, :, L - 1] = M - 1 - T; x[..., L - 1] = 255
    v[:, :, L - 17] = M - 1; x[..., L - 17] = 255
    v[:, :, L - 33] = M - 2 - T; x[..., L - 33] = 255
    v[:, :, L - 2] = M - 1; x[:, ::2, :, L - 2] = 0; x[:, ::2, 14:, L - 2] = 255; x[:, ::2, 13, L - 2] = 1
    s = rng.integers(0, 2, (N, 8)); s[:, 7] = 1; s[:, 1] = 0
    for r in range(N):
        h = hashes(w[r], np.full((8, 16, 1), 255))[:, 0]
        for g in range(8):
            B[r, g, :, h[g]] = 255 * s[r, g]; E[r, g, low[r, g], M - 1] = 65536
    return pack(X, B, E, x, v, w)
def setup_inputs_corners(rng):
    X = some(rng, M, (2, 64, 256)); B = some(rng, H, (2, 128, 256))
    kind = rng.integers(0, 9, (N, 8, 1, M)); kind[..., 5:6 + T] = 4
    own = np.arange(M); one = rng.integers(0, 16, (N, 8, 1, M)); line = np.arange(16)[:, None]
    c = rng.integers(0, M, (N, 8, 16, M))
    c = np.where(kind == 3, own, np.where(kind == 4, (own + 1) % M, np.where(kind == 5, 0, np.where(kind == 6, M - 1, c))))
    hide = (kind == 0) | ((kind == 2) & (line != one)) | ((kind == 7) & (line == one)) | ((kind == 8) & (rng.random(c.shape) < 0.5))
    m = rng.integers(0, 4, (N, 8, 1, M)); m = np.where(kind == 4, 1, m)
    k = np.where(m == 0, 0, np.where(m == 1, 16, np.where(m == 2, 15, rng.integers(0, 17, c.shape))))
    E = 4096 * k + np.where(hide, NONE, c)
    v = rng.integers(0, M, (N, 8, L)); w = rng.integers(0, 16, (N, 8, 16, 2))
    for r in range(N):
        o = rng.permutation(8); q = rng.permutation(M)
        v[r, o[0]] = 0; v[r, o[1]] = M - 1; v[r, o[2]] = q[:L]; v[r, o[3]] = rng.permutation(np.repeat(q[:L // 2], 2))
        v[r, o[4]] = rng.choice(np.array([5, 0, M - 1, 6]), L); v[r, o[5], ::2] = 5; v[r, o[5], L - 1] = 5
        b = rng.permutation(8)
        w[r, b[0]] = 0; w[r, b[1]] = 15; w[r, b[2], 1:] = 0; w[r, b[2], 0] = 15; w[r, b[3], :15] = 0; w[r, b[3], 15] = 15; w[r, b[4], :, 0] = 0; w[r, b[5], :, 1] = 0
    d = rng.integers(0, 4, (N, 8, 1, L)); x = some(rng, L, (64, 256))
    x = np.where(d == 0, 0, np.where(d == 1, 255, np.where(d == 2, np.take_along_axis(X, v[:, :, None, :], 3), x)))
    return pack(X, B, E, x, v, w)
def full(rng, X, B, E, x, v, r, late):
    n = T - 1 if late else 0; half = rng.permutation(8)
    for g in range(8):
        u = rng.permutation(M)[:L * T].reshape(T, L); e = E[r, g]; v[r, g] = u[0]
        for j in range(n): e[:, u[j]] = 65536 + u[j + 1][None, :]
        if half[g] < 4:
            e[:, u[n]] = NONE + 4096 * rng.integers(0, 17, (16, L))
        else:
            X[r, g] = rng.integers(0, 8, (16, M)); x[r, g] = rng.integers(8, 24, (16, L)); B[r, g] = rng.integers(24, 256, (16, H))
            e[:, u[n]] = rng.integers(0, M, (16, L)) + 4096 * rng.integers(0, 16, (16, L))
def setup_inputs_crowd(rng):
    X = some(rng, M, (16, 64, 128)); B = some(rng, H, (160, 256)); x = np.minimum(some(rng, L, (128, 256)) + rng.integers(0, 64, (N, 8, 1, L)), 255)
    k = rng.integers(0, 17, (N, 8, 16, M)) * (rng.random((N, 8, 16, M)) < 0.3); fill = rng.choice(np.array([0.5, 1.0]), (N, 8, 1, M))
    E = 4096 * k + np.where(rng.random((N, 8, 16, M)) < fill, rng.integers(0, M, (N, 8, 16, M)), NONE)
    v = places(rng, rng.choice(np.array([1, 2, 3, 16]), (N, 8))); v[:, 0] = 0; v[:, 7] = M - 1
    o = rng.permutation(N); full(rng, X, B, E, x, v, int(o[0]), False); full(rng, X, B, E, x, v, int(o[1]), True)
    return pack(X, B, E, x, v, rng.integers(0, 16, (N, 8, 16, 2)))
def setup_inputs_ties(rng):
    X = 100 + rng.integers(0, 3, (N, 8, 16, M)); x = 100 + rng.integers(0, 3, (N, 8, 16, L)); B = rng.integers(0, 3, (N, 8, 16, H))
    c = rng.integers(0, M, (N, 8, 16, M)); c[:, ::2, 8:] = c[:, ::2, :8]
    E = 4096 * rng.integers(8, 15, c.shape) + np.where(rng.random(c.shape) < 0.8, c, NONE)
    v = places(rng, rng.choice(np.array([4, 16, 64, M]), (N, 8)))
    return pack(X, B, E, x, v, rng.integers(0, 16, (N, 8, 16, 2)))
def check_inputs(d):
    bad = []
    for k, lo, hi in (("nodes", 0, 255), ("book", 0, 255), ("kids", 0, 69631), ("cand", 0, 255), ("spot", 0, M - 1), ("wts", 0, 15)):
        a = np.asarray(d[k]).astype(np.float32)
        if not (np.min(a) >= lo and np.max(a) <= hi and np.all(a == np.floor(a))): bad.append("range of " + k)
    c = np.asarray(d["kids"]).astype(np.int64) & 4095
    if np.any((c >= M) & (c != NONE)): bad.append("children in kids")
    return bad
def reference(nodes, book, kids, cand, spot, wts):
    X = np.zeros((N, 8, 16, W), np.int64); X[..., :M] = nodes.astype(np.float32).astype(np.int64).reshape(N, 8, 16, M)
    E = np.full((N, 8, 16, W), NONE, np.int64); E[..., :M] = kids.astype(np.int64).reshape(N, 8, 16, M)
    B = book.astype(np.float32).astype(np.int64).reshape(N, 8, 16, H); w = wts.astype(np.float32).astype(np.int64).reshape(N, 8, 16, 2)
    xs = cand.astype(np.float32).astype(np.int64).reshape(N, 8, 16, L).copy(); vs = np.stack([gentries(a) for a in spot]).astype(np.int64)
    lane = np.arange(L); p = lane & 15; gr = np.arange(8)[:, None]
    for t in range(T):
        for r in range(N):
            x, v, q = xs[r], vs[r], (r + 1 + t % (N - 1)) % N
            ev = np.take_along_axis(E[r], v[:, None, :], 2)
            c = ev & 4095; thr = ev >> 12; filled = c != NONE
            xc = np.take_along_axis(X[r], np.where(filled, c, 0).reshape(8, 1, 16 * L), 2).reshape(8, 16, 16, L)
            dif = np.abs(x[:, :, None, :] - xc); fd = dif.reshape(8, 16, 16 * L)
            bc = np.take_along_axis(B[r], hashes(w[r], fd)[:, None, :], 2)
            s = np.add.reduce((bc >= fd).astype(np.int64), axis=1).reshape(8, 16, L)
            over = np.add.reduce((x[:, :, None, :] >= xc).astype(np.int64), axis=1)
            cap = filled & (over >= A) & (s > thr); stay = filled & ~cap
            go = stay[:, p, lane]
            best = np.argmax(np.where(stay, s, -1), axis=1)
            down = np.take_along_axis(c, best[:, None, :], 1)[:, 0]
            first = np.full((8, W), L); np.minimum.at(first, (gr, v), np.where(go, L, lane[None, :]))
            win = ~go & (first[gr, v] == lane[None, :]); wb = win[:, None, :]
            z = np.abs(np.take_along_axis(X[r], v[:, None, :], 2) - x)
            y = np.take_along_axis(B[q], hashes(w[q], z)[:, None, :], 2)
            n = M + L * t + lane
            X[r][:, :, M + L * t:M + L * t + L] = np.where(wb, x, 0)
            E[r][:, :, M + L * t:M + L * t + L] = np.where(wb & cap, c + 4096 * s, NONE)
            col = np.where(cap, NONE, ev); col[:, p, lane] = n[None, :] + 4096 * np.max(np.where(cap, s, 0), axis=1)
            gi, li = np.nonzero(win)
            E[r][gi, :, v[gi, li]] = col[gi, :, li]
            x = np.where(wb, np.abs(x - y), x)
            back = np.add.reduce(w[r][:, :, 0:1] * x, axis=1) & (R - 1)
            xs[r] = x; vs[r] = np.where(win, back, np.where(go, down, v))
    return {"ykids": E.reshape(N, 128, W).astype(np.float32), "ynodes": np.ascontiguousarray(X[..., M:]).reshape(N, 128, L * T).astype(np.float32).astype(BF),
            "ycand": xs.reshape(N, 128, L).astype(np.float32).astype(BF), "yspot": np.stack([gtable(a) for a in vs]).astype(np.float32)}

@@ -1,0 +1,594 @@
+import numpy as np
+from concourse.mybir import AluOpType as A, ActivationFunctionType as F
+
+M, L, STEPS, H, R, NB = 896, 128, 3, 2048, 512, 4
+XW = 1296
+SBANKS = (2, 3)
+XS = (1, 2)
+
+BF, F32, I32, U16 = "bfloat16", "float32", "int32", "uint16"
+_S = {
+    "spi": (8, I32), "E": (128 + 1280, I32), "EF": (128 + 1280, F32), "X": (XW, BF), "bk": (3 * H, BF), "XX": (2 * L, BF),
+    "wt": (2, BF), "wl0": (2, BF), "wl1": (2, BF), "wl2": (2, BF),
+    "qs": (8 * STEPS, U16), "ql": (8 * STEPS, U16), "ys": (L * STEPS, BF), "yl": (L * STEPS, BF),
+    "one": (128, BF), "zer": (256, BF), "pk": (128, I32), "Id": (128, BF), "nId": (128, BF), "IF": (256, F32), "JJ": (256, BF), "CA": (256, BF),
+    "BD0": (128, BF), "BD": (128, BF), "BDf": (8, F32), "P": (128, BF), "Pb": (128, BF), "P4": (128, F32), "P128": (128, BF), "TPm": (128, BF),
+    "NEG": (256, BF), "I4": (128, BF), "Iq": (128, BF), "I14": (256, BF), "nIh": (128, BF), "BDq": (128, BF), "BD16": (128, BF), "CH2": (16, BF),
+    "RB": (16, BF), "WO": (128, BF), "WI": (128, BF), "Ex": (2048, BF), "Mh": (128, BF), "W": (16, BF), "Wz": (48, BF),
+    "LW": (2048, BF), "lwo": (2, U16), "wrep": (16, BF), "chp": (8, BF),
+    "ni": (128, F32), "Pn": (128, F32), "pt": (128, I32), "ptb": (256, BF), "lowb": (128, BF), "hib": (16, F32), "CODE": (1280, BF),
+    "lst": (16, U16), "e2": (16, F32), "BW": (16, F32), "BB": (16, F32),
+    "Ci": (128, I32), "C16": (128, U16), "XC": (2048, BF), "D": (2048, BF), "xT": (128, BF), "XV": (128, BF), "z": (128, BF), "zh": (128, F32),
+    "Ui": (256, I32), "U2": (256, I32), "h1": (128, I32), "h2": (128, I32), "hf": (128, F32), "H16": (128, U16), "BC": (2048, BF),
+    "CG": (128, BF), "CGm": (256, BF), "EQ": (1024, BF), "evf": (128, F32), "d4": (128, BF), "fe": (128, BF), "d4P": (128, BF), "feP": (128, BF),
+    "Cf": (128, F32), "AA": (256, F32), "evP": (128, F32), "Kc": (256, F32), "ov": (256, F32), "xm": (256, BF),
+    "wr": (128, BF), "wd": (128, BF), "cap": (128, BF), "nc": (128, F32), "mk": (128, F32), "sc": (128, F32), "zc": (128, F32),
+    "scap": (128, BF), "scs": (128, F32), "sp": (128, BF), "wP": (128, BF), "wL": (128, BF),
+    "mm": (256, F32), "VC": (128, F32), "n1": (128, F32), "n2": (128, F32),
+    "i8": (128, I32), "f8": (128, F32),
+}
+SCRATCH = {k: ("sbuf", [128, w], d) for k, (w, d) in _S.items()}
+for _k in ("OV", "IN"):
+    SCRATCH[_k] = ("sbuf", [128, 8, 256], BF)
+for _k in ("PD0", "PD1", "PD2", "PD3", "PB4", "PB5", "PB6", "PB7"):
+    SCRATCH[_k] = ("psum", [128, 512], F32)
+_I8 = {"uz": (0, 16), "uz2": (16, 16), "hz1": (32, 8), "hz2": (40, 8), "bk1": (48, 8), "bk2": (56, 8), "ch1": (64, 8), "ch2": (72, 8),
+       "ip": (80, 1), "p15": (84, 1), "mi": (88, 1), "g8": (96, 8)}
+_F8 = {"hz": (0, 8), "ch3": (8, 8), "ch4": (16, 8), "il": (24, 8), "c128": (32, 8), "e1": (40, 16), "lwi": (56, 1), "colk": (60, 1), "m0": (64, 1),
+       "m1": (68, 1), "lwf": (72, 1), "cb": (76, 1)}
+SLICED = set("pt Ex W JJ I14 CH2 RB RBh CK CA ptb zh zc sp IF WI CGm Wz CODE IN0 IN1 IN2 IN3 PB7".split())
+DUR = {"V": 0.13, "S": 0.19, "P": 0.13, "G": 0.4, "Y": 0.1, "A": 0.0}
+COST = {"VCi": 0.24, "VXC": 0.82, "Vevf": 0.24, "VXV": 0.24, "VE": 0.43, "VEF": 0.43, "VUi": 0.26, "VU": 0.26, "Vh": 0.26, "Vhf": 0.26, "VIN": 0.47,
+        "Vd": 0.26, "VKc": 0.26, "VLW": 0.1, "SD": 0.57, "SOV": 0.57, "SEQ": 0.57, "SXC": 0.82, "SBC": 0.82, "Sov": 0.32, "Sxm": 0.32, "SCG": 0.25,
+        "Sys": 0.25, "PPD": 0.26, "PPDw": 0.38, "PPB": 0.4, "PPBu": 0.5, "PPBh": 0.26, "PPBo": 0.3, "PPBk": 0.26, "PPBv": 0.3, "PPDb": 0.52}
+for _k in ("uz", "uz2", "hz1", "hz2", "hz", "zh", "qs", "zc", "sp", "ch1", "ch2", "ch3", "ch4", "BBb", "BWa", "BWb", "bk1", "bk2", "e1", "e2", "lst", "WI", "WO",
+           "CODE", "Ex", "W", "Wz", "RB", "CH2", "nId", "pt", "ptb", "CGm", "lwi", "lwf", "lwo", "il", "c128", "BBa", "BDf", "p15", "colk", "m0", "m1", "mi",
+           "chp", "wrep", "Pb"):
+    COST["V" + _k.rstrip("0123456789")] = 0.065
+COST["Sspk"] = COST["Spsk"] = 0.13
+TUNE = {"wake": 0.13, "remote": 2.5, "look": 0.02, "noise": 0.1, "seed": 9594}
+ORDERS = {}
+DMAS = ["spi", "E", "x", "X", "wt", "bk0", "bk1", "bk2", "out", "out0"]
+SEMAPHORES = (["sV", "sS", "sP", "sG", "wloc", "wrem"] + ["d_" + k for k in DMAS]
+              + [k + str(t) for k in ("qa", "qo", "ya", "yo") for t in range(STEPS)])
+
+
+def rank_program(g, core, T, topo):
+    rank = T.rank_of(core)
+    if rank is None:
+        return
+    Q = {"V": g.vector, "S": g.scalar, "P": g.tensor, "G": g, "Y": g.sync}
+    cnt = {k: 0 for k in "VSPG"}
+    known = {k: {} for k in Q}
+    snap = {}
+    lastw, readers, banks = {}, {}, {}
+    B = {k: T[k] for k in SCRATCH}
+
+    def sm(k, a=0, b=None):
+        buf, (o, w) = ("i8", _I8[k]) if k in _I8 else ("f8", _F8[k])
+        return B[buf][:, o + a:o + (w if b is None else b)]
+
+    def wait(eng, toks):
+        best = {}
+        for s, v in toks:
+            if known[eng].get(s, 0) < v:
+                best[s] = max(best.get(s, 0), v)
+        for s, v in sorted(best.items(), key=lambda a: -len(snap.get(a, ()))):
+            if known[eng].get(s, 0) >= v:
+                continue
+            Q[eng].wait_ge(T.sem[s], v)
+            known[eng][s] = v
+            for a, b in snap.get((s, v), {}).items():
+                known[eng][a] = max(known[eng].get(a, 0), b)
+
+    calls = []
+
+    def note(eng, rd, wr, fn, kind="c", dur=None, lat=0.0, tok=None):
+        rd, wr = rd.split(), wr.split()
+        n, pre = len(calls), {}
+
+        def edge(m, w):
+            pre[m] = pre.get(m, False) or w
+        for k in rd:
+            for m in lastw.get(k, ()):
+                edge(m, True)
+        for k in wr:
+            old, rs = lastw.get(k, []), readers.get(k, [])
+            if k in SLICED and old and not rs and calls[old[0]]["eng"] == eng:
+                lastw[k] = old + [n]
+                for m in calls[old[0]]["pre"]:
+                    if calls[old[0]]["pre"][m]:
+                        edge(m, True)
+                continue
+            for m in old:
+                edge(m, not (eng == "P" and calls[m]["eng"] == "P"))
+            for m in rs:
+                edge(m, not (eng == "P" and calls[m]["eng"] == "P"))
+            lastw[k], readers[k] = [n], []
+        for k in rd:
+            readers.setdefault(k, []).append(n)
+        for k in sorted(set(k[:3] for k in rd + wr if k[:2] in ("PD", "PB"))):
+            cur, prev = banks.get(k, (None, [])), None
+            if cur[0] != eng:
+                banks[k] = cur = (eng, [], cur[1])
+            for m in cur[2]:
+                edge(m, True)
+            if eng == "P":
+                for m in cur[1]:
+                    edge(m, False)
+            cur[1].append(n)
+        calls.append({"eng": eng, "pre": pre, "fn": fn, "kind": kind, "lat": lat, "tok": tok, "n": n,
+                      "dur": dur if dur is not None else COST.get(eng + wr[0].rstrip("0123456789"), DUR[eng])})
+        return n
+
+    def op(eng, rd, wr, fn, dur=None):
+        return note(eng, rd, wr, fn, dur=dur)
+
+    dcount = {}
+
+    def dma(eng, rd, wr, sem, out, in_, lat=3.0):
+        dcount[sem] = dcount.get(sem, 0) + 16
+        note(eng, rd, wr, lambda: Q[eng].dma_start(out, in_).then_inc(T.sem["d_" + sem], 16), "d", 0.1, lat, ("d_" + sem, dcount[sem]))
+
+    def send(rd, wr, out, in_, dst, arrive, left, lands):
+        rid, pid = topo.addr(dst, core)
+        m = note("G", rd, "", lambda: g.remote_dma(out, in_, T.sem[arrive], T.sem[left], pid, rid, topo.mask(core, dst)), "r", 0.4)
+        if wr:
+            n = note("A", "", wr, None, "a", 0.0, TUNE["remote"], (arrive, lands))
+            calls[n]["pre"][m] = True
+
+    V, S, PE = g.vector, g.scalar, g.tensor
+
+    def tt(rd, wr, out, a, b, o):
+        op("V", rd, wr, lambda: V.tensor_tensor(out, a, b, o))
+
+    def ts(rd, wr, out, a, s1, s2, o0, o1=None):
+        if o1 is None:
+            op("V", rd, wr, lambda: V.tensor_scalar(out, a, s1, s2, o0))
+        else:
+            op("V", rd, wr, lambda: V.tensor_scalar(out, a, s1, s2, o0, o1))
+
+    def cp(rd, wr, out, a):
+        op("V", rd, wr, lambda: V.tensor_copy(out, a))
+
+    def act(rd, wr, out, a, f, **kw):
+        op("S", rd, wr, lambda: S.activation(out, a, f, **kw))
+
+    def mms(rd, wr, lst):
+        def go():
+            i = None
+            for out, l, r, st, sp in lst:
+                i = PE.matmul(out, l, r, st, sp)
+            return i
+        op("P", rd, wr, go)
+
+    def memset(wr, ap, c):
+        op("V", "", wr, lambda: V.memset(ap, c))
+
+    nx, x = B["XX"][:, 0:L], B["XX"][:, L:2 * L]
+    dma("Y", "", "spi", "spi", B["spi"][:], T.spot[:])
+    dma("Y", "", "E", "E", B["E"][:, 128:128 + M], T.kids[:])
+    dma("S", "", "wt", "wt", B["wt"][:], T.wts[:])
+    dma("S", "", "x", "x", x, T.cand[:])
+    dma("S", "", "X", "X", B["X"][:, 0:M], T.nodes[:])
+    for j in range(3):
+        dma("Y", "", "bk%d" % j, "bk%d" % j, B["bk"][:, H * j:H * j + H], T.book[:])
+
+    memset("one", B["one"][:], 1.0)
+    memset("zer", B["zer"][:], 0.0)
+    op("G", "one", "Id", lambda: g.affine_select(B["Id"][:], B["one"][:], [[-1, 128]], A.is_equal, 0.0, 0, 1))
+    op("G", "one", "BD0", lambda: g.affine_select(B["BD0"][:], B["one"][:], [[-16, 8], [0, 16]], A.is_ge, 0.0, 0, 1))
+    op("G", "BD0", "BD", lambda: g.affine_select(B["BD"][:], B["BD0"][:], [[16, 8], [0, 16]], A.is_ge, 0.0, 15, -1))
+    op("G", "", "pk", lambda: g.iota(B["pk"][:], [[0, 8], [-1, 16]], 16, 1))
+    op("G", "", "ip", lambda: g.iota(sm("ip"), [[0, 1]], 0, 1))
+    op("G", "", "g8", lambda: g.iota(sm("g8"), [[0, 8]], 0, 1))
+    neng = len(topo.engines(core, T.cores[(rank + 1) % NB]))
+    for j in range(NB - 1):
+        send("wt", "wl0 wl1 wl2" if j == NB - 2 else "", B["wl%d" % j][:], B["wt"][:], T.cores[(rank - 1 - j) % NB], "wrem", "wloc", neng * (NB - 1))
+    op("G", "zer", "NEG", lambda: g.affine_select(B["NEG"][:], B["zer"][:], [[0, 2], [1, 128]], A.is_gt, -100.0, 0, -1))
+    op("G", "", "ni", lambda: g.iota(B["ni"][:], [[1, 128]], M, 0, allow_small_or_imprecise_dtypes=True))
+    op("G", "", "LW", lambda: g.iota(B["LW"][:], [[0, 2048]], 0, 0, allow_small_or_imprecise_dtypes=True))
+
+    memset("Xz", B["X"][:, M:XW], 0.0)
+    memset("ptb0", B["ptb"][:, 128:256], 0.0)
+    memset("pt0", B["pt"][:], 0)
+    memset("Mh", B["Mh"][:], 1.0)
+    memset("Mh", B["Mh"][:, 0:128:16], 0.0)
+    memset("IF", B["IF"][:, 128:256], 0.0)
+    memset("CA", B["CA"][:, 0:128], -2.0)
+    memset("CA", B["CA"][:, 128:256], 0.0)
+    bd8 = B["BD"][:, 0:128:16]
+    ts("Id", "nId", B["nId"][:], B["Id"][:], -1.0, None, A.mult)
+    mms("x Id", "PB4x", [(B["PB4"][:, 384:512], x, B["Id"][:], True, True)])
+    act("PB4x", "xT", B["xT"][:], B["PB4"][:, 384:512], F.Copy)
+    EXR = "Ex"
+    for k in range(16):
+        if k % 3 == 2:
+            act("Id", "Ex%d" % k, B["Ex"][:, k:2048:16], B["Id"][:], F.Copy)
+            EXR += " Ex%d" % k
+        else:
+            cp("Id", "Ex", B["Ex"][:, k:2048:16], B["Id"][:])
+    ts("pk", "Ci", B["Ci"][:], B["pk"][:], 15, None, A.bitwise_and)
+    ts("Ci", "P", B["P"][:], B["Ci"][:], 0, None, A.is_equal)
+    cp("Id", "IF", B["IF"][:, 0:128], B["Id"][:])
+    cp("BD", "BDf", B["BDf"][:], bd8)
+    ts("ip", "p15", sm("p15"), sm("ip"), 15, None, A.bitwise_and)
+    ts("p15", "colk", sm("colk"), sm("p15"), -2048.0, 30720.0, A.mult, A.add)
+    ts("P", "Pb", B["Pb"][:], B["P"][:], -1.0, 1.0, A.mult, A.add)
+    CP, CPb, CP4 = (B["PB7"][:, 128 * j:128 * j + 128] for j in range(3))
+    cp("P", "PB7", CP, B["P"][:])
+    cp("Pb", "PB7", CPb, B["Pb"][:])
+    ts("Pb", "PB7", CP4, B["Pb"][:], 4095.0, None, A.mult)
+    act("P", "TPm", B["TPm"][:], B["P"][:], F.Copy, scale=1000.0, bias=-1000.0)
+    act("colk", "cb", sm("cb"), sm("colk"), F.Copy, scale=-1.0, bias=-4095.0)
+    for k, src, f in (("nIh", "Id", -0.5), ("I4", "Id", 4096.0), ("Iq", "Id", 1.0 / 4096), ("P128", "P", 128.0), ("BDq", "BD", 1.0 / 4096),
+                      ("BD16", "BD", -16.0)):
+        act(src, k, B[k][:], B[src][:], F.Copy, scale=f)
+    memset("I14z", B["I14"][:, 128:256], 0.0)
+    act("Id", "I14", B["I14"][:, 0:128], B["Id"][:], F.Copy, scale=-16384.0)
+    for j in range(2):
+        act("Id", "JJ", B["JJ"][:, 128 * j:128 * j + 128], B["Id"][:], F.Copy, scale=(256.0, -256.0)[j])
+        cp("BD", "CH2", B["CH2"][:, 8 * j:8 * j + 8], bd8)
+        ts("BD", "RB", B["RB"][:, 8 * j:8 * j + 8], bd8, (32768.0, 1.0)[j], None, A.mult)
+    pt = B["pt"]
+    for b in range(7):
+        ts("g8 pt0", "pt", pt[:, b:128:16], sm("g8"), b, 1, A.logical_shift_right, A.bitwise_and)
+    ts("pt", "ptb", B["ptb"][:, 0:128], pt[:], 2.0, -1.0, A.mult, A.add)
+    for b in range(7, 11):
+        ts("ptb0 pt", "ptb", B["ptb"][:, 128 + b:256:16], pt[:, b - 7:128:16], 2.0, None, A.mult)
+    mms("ptb Id", "PB6c", [(B["PB6"][:, 256:384], B["ptb"][:, 0:128], B["Id"][:], True, True),
+                           (B["PB6"][:, 384:400], B["ptb"][:, 128:256], B["Id"][:, 0:16], True, True)])
+    act("PB6c", "hib", B["hib"][:], B["PB6"][:, 384:400], F.Copy)
+    act("PB6c", "lowb", B["lowb"][:], B["PB6"][:, 256:384], F.Copy)
+    ts("ip", "mi", sm("mi"), sm("ip"), 4, 1, A.logical_shift_right, A.bitwise_and)
+    cp("mi", "m1", sm("m1"), sm("mi"))
+    ts("m1", "m0", sm("m0"), sm("m1"), -1.0, 1.0, A.mult, A.add)
+    cp("ip", "lwi", sm("lwi"), sm("ip"))
+    ts("BD lwi", "chp", B["chp"][:], bd8, sm("lwi"), None, A.mult)
+    mms("P chp", "PD3i", [(B["PD3"][:, 0:8], B["P"][:], B["chp"][:], True, True)])
+    cp("PD3i", "il", sm("il"), B["PD3"][:, 0:8])
+    ts("il", "c128", sm("c128"), sm("il"), -1.0, 128.0, A.mult, A.add)
+    cp("il", "BBa", B["BB"][:, 0:8], sm("il"))
+    for u in range(2):
+        ts("BD wt", "W", B["W"][:, 8 * u:8 * u + 8], bd8, B["wt"][:, u:u + 1], None, A.mult)
+    cp("spi", "lst", B["lst"][:, 8:16], B["spi"][:])
+    cp("spi", "e2", B["e2"][:, 8:16], B["spi"][:])
+
+    def code_blocks():
+        for h in range(10):
+            ts("lowb hib", "CODE", B["CODE"][:, 128 * h:128 * h + 128], B["lowb"][:], B["hib"][:, h:h + 1], None, A.add)
+
+    def late_consts():
+        tt("P ni", "Pn", B["Pn"][:], B["P"][:], B["ni"][:], A.mult)
+        ts("p15 lwi", "lwf", sm("lwf"), sm("p15"), 128.0, sm("lwi"), A.mult, A.add)
+        cp("lwf", "lwo", B["lwo"][:, 0:1], sm("lwf"))
+        ts("one wt", "wrep", B["wrep"][:], B["one"][:, 0:16], B["wt"][:, 0:1], None, A.mult)
+        op("V", "lwo wrep LW", "LW", lambda: V.tensor_copy(B["LW"][:].indirect(B["lwo"][:, 0:1]), B["wrep"][:]))
+
+    PD = [B["PD%d" % b] for b in range(4)]
+    U, KS, PB6 = B["PB4"], B["PB5"], B["PB6"]
+    v16, vf = B["lst"][:, 8:16], B["e2"][:, 8:16]
+    sb = list(SBANKS)
+    vbk = [b for b in range(4) if b not in sb]
+    vb = [b for b in range(4) if b not in XS]
+    order = list(range(4))
+    dorder = list(XS) + vb
+    ch = [slice(512 * b, 512 * b + 512) for b in range(4)]
+    c32 = [slice(32 * b, 32 * b + 32) for b in range(4)]
+
+    def newcols(t):
+        tt("PB5n AAa", "mma", B["mm"][:, 0:128], KS[:, 0:128], B["AA"][:, 0:128], A.mult)
+        tt("PB5n mma", "n1", B["n1"][:], KS[:, 128:256], B["mm"][:, 0:128], A.add)
+        tt("PB5n n1", "n2", B["n2"][:], KS[:, 256:384], B["n1"][:], A.mult)
+        k = "EF" if t == STEPS - 1 else "E"
+        c = 128 + M + L * t
+        ts("n2", k + str(t), B[k][:, c:c + L], B["n2"][:], 4095.0, None, A.add)
+
+    def nodes_at(t):
+        op("V", "X lst " + " ".join("X%d" % j for j in range(t - 1)), "XV",
+           lambda: V.tensor_copy(B["XV"][:], B["X"][:, 0:M + L * max(0, t - 1)].indirect(v16)))
+
+    def newx():
+        mms("xm Id", "PB4x", [(U[:, 256:384], B["Id"][:], B["xm"][:, 0:128], True, False), (U[:, 256:384], B["Id"][:], B["xm"][:, 128:256], False, True)])
+        act("PB4x", "x", x, U[:, 256:384], F.Copy)
+
+    for t in range(STEPS):
+        last = t == STEPS - 1
+        wg = M + L * max(0, t - 1)
+        XR = "X Xz " + " ".join("X%d" % j for j in range(t))
+        ER = "E " + " ".join("E%d" % j for j in range(t - 1))
+        qb = (rank + 1 + t) % NB
+        qf = (rank - 1 - t) % NB
+        ts(ER + " lst", "Ci", B["Ci"][:], B["E"][:, 128:128 + wg].indirect(v16), 4095, None, A.bitwise_and)
+        ts("Ci", "C16", B["C16"][:], B["Ci"][:], 1280.0, None, A.min)
+        if t == 0:
+            nodes_at(t)
+        mms("XV xm Id nId x", "PB5z", [(KS[:, 384:512], B["Id"][:], B["XV"][:], True, False)]
+            + ([(KS[:, 384:512], B["nId"][:], x, False, True)] if t == 0 else
+               [(KS[:, 384:512], B["nId"][:], B["xm"][:, L * j:L * j + L], False, j == 1) for j in range(2)]))
+        act("PB5z", "z", B["z"][:], KS[:, 384:512], F.Abs)
+        if t:
+            mms("z Wz", "PB5u", [(KS[:, 384:400], B["z"][:], B["Wz"][:, 16 * t:16 * t + 16], True, True)])
+        for b in order:
+            mms("%s xT" % EXR, "PD%d" % b, [(PD[b][:], B["xT"][:], B["Ex"][:, ch[b]], True, False)])
+
+        def diff(b):
+            mms("nId XC%d" % b, "PD%d" % b, [(PD[b][:], B["nId"][:], B["XC"][:, ch[b]], False, True)])
+
+        def hashsum(b0, b1):
+            mms(" ".join("D%d" % b for b in range(b0, b1)) + " W", "PB4u",
+                [(U[32 * b0:32 * b1, k:256:16], B["D"][:, 512 * b0 + k:512 * b1:16], B["W"][:], True, True) for k in range(16)])
+
+        for b in XS:
+            act(XR + " C16", "XC%d" % b, B["XC"][:, ch[b]], B["X"][:].indirect(B["C16"][:, c32[b]]), F.Copy)
+        if t:
+            newx()
+        if t == 0:
+            for b in vb[:-1]:
+                cp(XR + " C16", "XC%d" % b, B["XC"][:, ch[b]], B["X"][:].indirect(B["C16"][:, c32[b]]))
+            for b in dorder[:-1]:
+                diff(b)
+            for j in range(3):
+                for u in range(2):
+                    ts("BD wl%d" % j, "Wz", B["Wz"][:, 16 * j + 8 * u:16 * j + 8 * u + 8], bd8, B["wl%d" % j][:, u:u + 1], None, A.mult)
+            mms("z Wz", "PB5u", [(KS[:, 384:400], B["z"][:], B["Wz"][:, 16 * t:16 * t + 16], True, True)])
+        cp("PB5u", "uz", sm("uz"), KS[:, 384:400])
+        ts("uz", "uz2", sm("uz2"), sm("uz"), 4095, None, A.bitwise_and)
+        tt("uz2", "hz1", sm("hz1"), sm("uz2", 0, 8), sm("uz2", 8, 16), A.mult)
+        ts("hz1", "hz2", sm("hz2"), sm("hz1"), 5, H - 1, A.logical_shift_right, A.bitwise_and)
+        if t:
+            tt("hz2 uz2", "hz", sm("hz"), sm("hz2"), sm("uz2", 8, 16), A.add)
+        else:
+            tt("hz2 uz2", "hz1", sm("hz1"), sm("hz2"), sm("uz2", 8, 16), A.add)
+            ts("hz1", "hz2", sm("hz2"), sm("hz1"), H - 1, None, A.bitwise_and)
+            cp("hz2", "hz", sm("hz"), sm("hz2"))
+        for k in range(8):
+            ts("P hz", "zh", B["zh"][:, 16 * k:16 * k + 16], B["P"][:, 0:16], sm("hz", k, k + 1), None, A.mult)
+        mms("zh BDf", "PB5q", [(KS[:, 400:408], B["zh"][:], B["BDf"][:], True, True)])
+        if t:
+            for b in XS:
+                diff(b)
+        ts("Ci", "fe", B["fe"][:], B["Ci"][:], 4095.0, 128.0, A.is_ge, A.mult)
+        ts("Ci colk", "Cf", B["Cf"][:], B["Ci"][:], sm("colk"), None, A.add)
+        cp("PB5q", "qs%d" % t, B["qs"][:, 8 * t:8 * t + 8], KS[:, 400:408])
+        send("qs%d" % t, "ql%d" % t, B["ql"][:, 8 * t:8 * t + 8], B["qs"][:, 8 * t:8 * t + 8], T.cores[qb], "qa%d" % t, "qo%d" % t,
+             len(topo.engines(T.cores[qf], core)))
+        for b in vb if t else vb[-1:]:
+            cp(XR + " C16", "XC%d" % b, B["XC"][:, ch[b]], B["X"][:].indirect(B["C16"][:, c32[b]]))
+            if b != 3:
+                diff(b)
+        for n, b in enumerate(dorder):
+            act("PD%d" % b, "D%d" % b, B["D"][:, ch[b]], PD[b][:], F.Abs)
+            if n == 0 and t:
+                act("CODE lst", "CG", B["CG"][:], B["CODE"][:].indirect(v16), F.Copy)
+            if n == 1:
+                diff(3)
+            if n == 2:
+                hashsum(0, 3)
+        hashsum(3, 4)
+        if t == 0:
+            code_blocks()
+            act("CODE lst", "CG", B["CG"][:], B["CODE"][:].indirect(v16), F.Copy)
+        op("V", ER + " lst", "evf", lambda wg=wg: V.tensor_copy(B["evf"][:], B["E"][:, 128:128 + wg].indirect(v16)))
+        tt("evf Ci", "d4", B["d4"][:], B["evf"][:], B["Ci"][:], A.subtract)
+        tt("d4 PB7", "d4P", B["d4P"][:], B["d4"][:], CP, A.mult)
+        tt("fe PB7", "feP", B["feP"][:], B["fe"][:], CP, A.mult)
+        for j in range(2):
+            ts("CG m%d" % j, "CGm", B["CGm"][:, 128 * j:128 * j + 128], B["CG"][:], sm("m%d" % j), None, A.mult)
+        cp("PB4u", "Ui", B["Ui"][:], U[:, 0:256])
+        ts("Ui", "U2", B["U2"][:], B["Ui"][:], 4095, None, A.bitwise_and)
+        tt("U2", "h1", B["h1"][:], B["U2"][:, 0:128], B["U2"][:, 128:256], A.mult)
+        ts("h1", "h2", B["h2"][:], B["h1"][:], 5, H - 1, A.logical_shift_right, A.bitwise_and)
+        tt("h2 U2", "hf", B["hf"][:], B["h2"][:], B["U2"][:, 128:256], A.add)
+        if t:
+            newcols(t - 1)
+
+
+        def eqmat(h):
+            for a in (2 * h, 2 * h + 1):
+                o = PD[h][:, 256 * (a % 2):256 * (a % 2) + 256]
+                mms("CG CGm NEG Id", "PD%d" % h, [(o, B["Id"][:], B["NEG"][:], True, False)])
+                mms("CG CGm" + (" rt%d" % h if a % 2 else ""), "PD%d" % h + ("" if a % 2 else " rt%d" % h), [(o, B["CG"][32 * a:32 * a + 32, :], B["CGm"][32 * a:32 * a + 32, :], False, True)])
+
+        def eqact(h):
+            act("PD%d" % h, "EQ%d" % h, B["EQ"][:, 512 * h:512 * h + 512], PD[h][:], F.Relu, bias=-15.0)
+        for n, b in enumerate(order):
+            act("PD%d" % b, "OV%d" % b, B["OV"][:, 2 * b:2 * b + 2, :], PD[b][:], F.Sign, bias=0.5)
+        eqmat(0)
+        op("P", "hf IF", "PB4h", lambda: PE.transpose(U[:, 256:384], B["hf"][:], B["IF"][:, 0:128]))
+        if t:
+            cp("PB4h", "H16", B["H16"][:], U[:, 256:384])
+        else:
+            cp("PB4h", "h1", B["h1"][:], U[:, 256:384])
+            ts("h1", "h2", B["h2"][:], B["h1"][:], H - 1, None, A.bitwise_and)
+            cp("h2", "H16", B["H16"][:], B["h2"][:])
+        bk = B["bk"][:] if t else B["bk"][:, 0:H]
+        BK = "bk0 bk1 bk2" if t else "bk0"
+        eqmat(1)
+        mms("OV0 OV1 OV2 OV3 BD", "PB6o", [(PB6[:, k:128:16], B["OV"][:, :, k:256:16], bd8, True, True) for k in range(16)])
+        cp("OV0 OV1 OV2 OV3", "WO", B["WO"][:], B["OV"][:, :, 0:256:17])
+        mms("WO BD", "PB6o", [(PB6[:, 128:256], B["WO"][:], B["BD"][:], True, True)])
+        mms("Cf IF", "PB5", [(KS[:, 0:256], B["Cf"][:], B["IF"][:], True, False)])
+        def sbook(b):
+            act(BK + " H16", "BC%d" % b, B["BC"][:, ch[b]], bk.indirect(B["H16"][:, c32[b]]), F.Copy)
+
+        def vbook(b):
+            for c in (2 * b, 2 * b + 1):
+                tt(BK + " H16 D%d" % b, "IN%d" % b, B["IN"][:, c, :], bk.indirect(B["H16"][:, 16 * c:16 * c + 16]), B["D"][:, 256 * c:256 * c + 256], A.is_ge)
+
+        def bdiff(b):
+            mms("Id nId BC%d D%d" % (b, b), "PD%d" % b, [(PD[b][:], B["Id"][:], B["BC"][:, ch[b]], True, False), (PD[b][:], B["nId"][:], B["D"][:, ch[b]], False, True)])
+
+        def count(b0, b1):
+            mms(" ".join("IN%d" % b for b in range(b0, b1)) + " RB", "PB5",
+                [(KS[32 * b0:32 * b1, k:256:16], B["IN"][:, 2 * b0:2 * b1, k:256:16], B["RB"][:], False, False) for k in range(16)])
+        def answer():
+            act(BK + " ql%d" % t, "ys%d" % t, B["ys"][:, L * t:L * t + L], bk.indirect(B["ql"][:, 8 * t:8 * t + 8]), F.Copy)
+            send("ys%d" % t, "yl%d" % t, B["yl"][:, L * t:L * t + L], B["ys"][:, L * t:L * t + L], T.cores[qf], "ya%d" % t, "yo%d" % t,
+                 len(topo.engines(T.cores[qb], core)))
+        if t:
+            answer()
+        sbook(sb[0])
+        act("PB6o", "ov", B["ov"][:], PB6[:, 0:256], F.Relu, scale=-64.0, bias=128.0)
+        if t == 0:
+            answer()
+        for b in sb[1:]:
+            sbook(b)
+        eqact(0)
+        vbook(vbk[0])
+        bdiff(sb[0])
+        if t == 0:
+            late_consts()
+        mms("d4 Iq fe Id d4P BDq feP BD16", "PB6k",
+            [(PB6[:, 256:384], B["d4"][:], B["Iq"][:], True, False), (PB6[:, 256:384], B["fe"][:], B["Id"][:], False, True),
+             (PB6[:, 384:512], B["d4P"][:], B["BDq"][:], True, False), (PB6[:, 384:512], B["feP"][:], B["BD16"][:], False, True)])
+        for b in vbk[1:]:
+            vbook(b)
+        for b in sb[1:]:
+            bdiff(b)
+        tt("PB6k ov", "Kc", B["Kc"][:], PB6[:, 256:512], B["ov"][:], A.add)
+        tt("evf PB7", "evP", B["evP"][:], B["evf"][:], CPb, A.mult)
+        tt("PB7 evP", "AAb", B["AA"][:, 128:256], CP4, B["evP"][:], A.subtract)
+        tt("c128 e2", "BWa", B["BW"][:, 0:8], sm("c128"), vf, A.add)
+        if last:
+            c = 128 + wg
+            cp("E1", "EFb", B["EF"][:, c:c + L], B["E"][:, c:c + L])
+            cp("E E0", "EF", B["EF"][:, 128:c], B["E"][:, 128:c])
+            dma("Y", "EFb", "", "out0", T.ykids[:, c - 128:c - 128 + L], B["EF"][:, c:c + L])
+        count(0, 2)
+        for b in sb:
+            ts("PD%d" % b, "IN%d" % b, B["IN"][:, 2 * b:2 * b + 2, :], PD[b][:], 0.0, None, A.is_ge)
+        eqact(1)
+        act("Cf cb", "AAa", B["AA"][:, 0:128], B["Cf"][:], F.Identity, bias=sm("cb"))
+        count(2, 3)
+        cp("IN0 IN1 IN2 IN3", "WI", B["WI"][:], B["IN"][:, :, 0:256:17])
+        mms("WI BD", "PD2s", [(PD[2][:, 128:256], B["WI"][:], B["BD"][:], True, True)])
+        count(3, 4)
+        mms("fe I14 I14z", "PB5", [(KS[:, 0:256], B["fe"][:], B["I14"][:], False, True)])
+        tt("PD2s Kc", "wr", B["wr"][:], PD[2][:, 128:256], B["Kc"][:, 128:256], A.is_gt)
+        mms("nIh wr EQ0 EQ1", "PD0w", [(PD[0][:, 0:128], B["nIh"][:], B["wr"][:], True, False)]
+            + [(PD[0][:, 16 * k:16 * k + 16], B["EQ"][:, 128 * k:128 * k + 128], B["wr"][:, 16 * k:16 * k + 16], False, False) for k in range(8)]
+            + [(PD[0][:, 0:128], B["nIh"][:], B["wr"][:], False, True)])
+        sK = KS[:, 128:256]
+        tt("PB5 Kc", "cap", B["cap"][:], sK, B["Kc"][:, 0:128], A.is_gt)
+        tt("PB5 cap", "scap", B["scap"][:], sK, B["cap"][:], A.mult)
+        tt("PB5 Kc", "nc", B["nc"][:], sK, B["Kc"][:, 0:128], A.is_le)
+        op("V", "Mh scap", "scs", lambda: V.tensor_tensor_scan(B["scs"][:], B["Mh"][:], B["scap"][:], 0.0, A.mult, A.max))
+        for k in range(4):
+            ts("P scs", "sp", B["sp"][:, 16 * k:16 * k + 16], B["P"][:, 0:16], B["scs"][:, 16 * k + 15:16 * k + 16], None, A.mult)
+        tt("PB5 nc", "mk", B["mk"][:], KS[:, 0:128], B["nc"][:], A.mult)
+        tt("PD0w TPm", "wP", B["wP"][:], PD[0][:, 0:128], B["TPm"][:], A.is_lt)
+        op("V", "Mh mk", "sc", lambda: V.tensor_tensor_scan(B["sc"][:], B["Mh"][:], B["mk"][:], 0.0, A.mult, A.max))
+        for k in range(8):
+            ts("P sc", "zc", B["zc"][:, 16 * k:16 * k + 16], B["P"][:, 0:16], B["sc"][:, 16 * k + 15:16 * k + 16], None, A.mult)
+        tt("wr PB7", "wd", B["wd"][:], B["wr"][:], CP, A.mult)
+        mms("Id nId x yl%d" % t, "PB4d", [(U[:, 256:384], B["Id"][:], x, True, False), (U[:, 256:384], B["nId"][:], B["yl"][:, L * t:L * t + L], False, True)])
+        act("PB4d", "nx", nx, U[:, 256:384], F.Abs)
+        for k in range(4, 8):
+            act("P scs", "sp4", B["sp"][:, 16 * k:16 * k + 16], B["P"][:, 0:16], F.Copy, scale=B["scs"][:, 16 * k + 15:16 * k + 16])
+        act("PD0w", "wL", B["wL"][:], PD[0][:, 0:128], F.Relu, scale=-1.0)
+        mms("IF evP Pn P128 Id", "PB6v", [(PB6[:, 0:128], B["IF"][:, 0:128], B["evP"][:], True, False), (PB6[:, 0:128], B["IF"][:, 0:128], B["Pn"][:], False, False)]
+            + [(PB6[:, 0:128], B["Id"][:], B["P128"][:], False, False)] * t)
+        mms("cap Id", "PD3c", [(PD[3][:, 0:128], B["cap"][:], B["Id"][:], True, True)])
+        mms("sp sp4 I4", "PB6v", [(PB6[:, 0:128], B["sp"][:], B["I4"][:], False, True)])
+        mms("wP CH2", "PD2l", [(PD[2][:, 0:16], B["wP"][:], B["CH2"][:], True, True)])
+        mms("zc BDf", "PD2l", [(PD[2][:, 24:32], B["zc"][:], B["BDf"][:], True, True)])
+        mms("wd CH2", "PD2l", [(PD[2][:, 16:24], B["wd"][:], B["CH2"][:, 0:8], True, True)])
+        cp("PD2l", "ch1", sm("ch1"), PD[2][:, 24:32])
+        ts("ch1", "ch2", sm("ch2"), sm("ch1"), 2047, None, A.bitwise_and)
+        tt("e2 ch2", "ch3", sm("ch3"), vf, sm("ch2"), A.subtract)
+        tt("PD2l ch3", "ch4", sm("ch4"), PD[2][:, 16:24], sm("ch3"), A.mult)
+        tt("ch2 ch4", "BBb", B["BB"][:, 8:16], sm("ch2"), sm("ch4"), A.add)
+        tt("PD3c AAb", "mmb", B["mm"][:, 128:256], PD[3][:, 0:128], B["AA"][:, 128:256], A.mult)
+        tt("PB6v mmb", "VC", B["VC"][:], PB6[:, 0:128], B["mm"][:, 128:256], A.add)
+        mms("LW nx", "PD1b", [(PD[1][:, 128:136], B["LW"][:, 128 * r:128 * r + 128], B["XX"][:, r:128:16], r == 0, r == 15) for r in range(16)])
+        cp("PD1b", "bk1", sm("bk1"), PD[1][:, 128:136])
+        ts("bk1", "bk2", sm("bk2"), sm("bk1"), R - 1, None, A.bitwise_and)
+        tt("bk2 e2", "BWb", B["BW"][:, 8:16], sm("bk2"), vf, A.subtract)
+        mms("Id nx x one CA", "PB4a", [(U[:, 0:256], B["Id"][:], B["XX"][:], True, False), (U[:, 0:256], B["one"][:], B["CA"][:], False, False)])
+        mms("wL JJ", "PB4a", [(U[:, 0:256], B["wL"][:], B["JJ"][:], False, True)])
+        mms("x Id one CA wL JJ", "PD1x", [(PD[1][:, 0:128], B["Id"][:], x, True, False), (PD[1][:, 0:128], B["one"][:], B["CA"][:, 0:128], False, False),
+                                          (PD[1][:, 0:128], B["wL"][:], B["JJ"][:, 0:128], False, True)])
+        mms("cap scap wL Id I4", "PB5n", [(KS[:, 0:128], B["cap"][:], B["Id"][:], True, True), (KS[:, 128:256], B["scap"][:], B["I4"][:], True, True),
+                                          (KS[:, 256:384], B["wL"][:], B["Id"][:], True, True)])
+        act("PB4a", "xm", B["xm"][:], U[:, 0:256], F.Relu)
+        act("PD1x", "Xz X%d" % t, B["X"][:, M + L * t:M + L * t + L], PD[1][:, 0:128], F.Relu)
+        if not last:
+            mms("xm Id", "PB4y", [(U[:, 384:512], B["xm"][:, 0:128], B["Id"][:], True, False), (U[:, 384:512], B["xm"][:, 128:256], B["Id"][:], False, True)])
+            act("PB4y", "xT", B["xT"][:], U[:, 384:512], F.Copy)
+        else:
+            newx()
+        tt("PD2l BWa BWb", "e1", sm("e1"), PD[2][:, 0:16], B["BW"][:], A.mult)
+        tt("e1 BBa BBb", "e2", B["e2"][:], sm("e1"), B["BB"][:], A.add)
+        cp("e2", "lst", B["lst"][:], B["e2"][:])
+        if not last:
+            nodes_at(t + 1)
+        if not last:
+            op("V", "lst VC", ER, lambda wg=wg: V.tensor_copy(B["E"][:, 0:128 + wg].indirect(B["lst"][:, 0:8]), B["VC"][:]))
+        else:
+            op("V", "lst VC EF", "EF", lambda: V.tensor_copy(B["EF"][:, 0:128 + wg].indirect(B["lst"][:, 0:8]), B["VC"][:]))
+            dma("Y", "EF", "", "out", T.ykids[:, 0:wg], B["EF"][:, 128:128 + wg])
+            newcols(t)
+            dma("Y", "EF%d" % t, "", "out", T.ykids[:, M + L * t:M + L * t + L], B["EF"][:, 128 + M + L * t:128 + M + L * t + L])
+            dma("S", XR + " X%d" % t, "", "out", T.ynodes[:], B["X"][:, M:M + L * STEPS])
+            dma("S", "x", "", "out", T.ycand[:], x)
+            dma("S", "e2", "", "out", T.yspot[:], vf)
+    def schedule():
+        N = len(calls)
+        WAKE, LOOK = TUNE["wake"], TUNE["look"]
+        noise = np.random.RandomState(TUNE["seed"]).rand(N) * TUNE["noise"]
+        succ = [[] for _ in range(N)]
+        left = [len(c["pre"]) for c in calls]
+        for c in calls:
+            for m in c["pre"]:
+                succ[m].append(c["n"])
+        prio = [0.0] * N
+        for n in range(N - 1, -1, -1):
+            c = calls[n]
+            prio[n] = c["dur"] + c["lat"] + max([prio[m] + (WAKE if calls[m]["pre"][n] else 0.0) for m in succ[n]] or [0.0])
+        for n in range(N):
+            prio[n] += float(noise[n])
+        free, end, start, est = {}, [0.0] * N, [0.0] * N, {}
+        for n in range(N):
+            if not left[n]:
+                est[n] = 0.0
+        out = []
+        while est:
+            at = {n: max(e, free.get(calls[n]["eng"], 0.0)) for n, e in est.items()}
+            lo = min(at.values())
+            n = max((m for m in at if at[m] <= lo + LOOK), key=lambda m: (prio[m], -m))
+            c = calls[n]
+            start[n] = at[n]
+            if c["eng"] != "A":
+                free[c["eng"]] = at[n] + c["dur"]
+            end[n] = at[n] + c["dur"] + c["lat"]
+            del est[n]
+            out.append(n)
+            for m in succ[n]:
+                left[m] -= 1
+                if not left[m]:
+                    est[m] = max(end[q] + WAKE if w else start[q] + calls[q]["dur"] for q, w in calls[m]["pre"].items())
+        return out
+
+    if "order" not in ORDERS:
+        ORDERS["order"] = schedule()
+    for n in ORDERS["order"]:
+        c = calls[n]
+        eng = c["eng"]
+        if eng == "A":
+            snap[c["tok"]] = {}
+            continue
+        wait(eng, [calls[m]["tok"] for m, w in c["pre"].items() if w])
+        i = c["fn"]()
+        if c["kind"] == "c":
+            cnt[eng] += 1
+            i.then_inc(T.sem["s" + eng], 1)
+            c["tok"] = ("s" + eng, cnt[eng])
+        if c["tok"]:
+            snap[c["tok"]] = dict(known[eng])
+    for t in range(STEPS):
+        for s in ("qo", "yo"):
+            g.wait_ge(T.sem[s + str(t)], neng)
+    g.wait_ge(T.sem.wloc, neng * (NB - 1))
+    wait("G", [("sV", cnt["V"]), ("sS", cnt["S"]), ("sP", cnt["P"]), ("sG", cnt["G"])] + [("d_" + k, n) for k, n in dcount.items()]
+         + [("wrem", neng * (NB - 1))] + [(k + str(t), neng) for k in ("qa", "ya") for t in range(STEPS)])

@@ -1,56 +1,45 @@
 import numpy as np
-from concourse.mybir import AluOpType as A, ActivationFunctionType as F
+from concourse.bass import DstId, RemoteDMATransfer
+from concourse.mybir import AluOpType as A, ActivationFunctionType as F, AxisListType as AX
 
 M, L, STEPS, H, R, NB = 896, 128, 3, 2048, 512, 4
 XW = 1296
-SBANKS = (2, 3)
-XS = (1, 2)
-
-BF, F32, I32, U16 = "bfloat16", "float32", "int32", "uint16"
+BF, F32, I32, U16, F16 = "bfloat16", "float32", "int32", "uint16", "float16"
+BIG, TOP, MAGIC = 2.0 ** 22, 2.0 ** 21, 1.5 * 2.0 ** 35
 _S = {
-    "spi": (8, I32), "E": (128 + 1280, I32), "EF": (128 + 1280, F32), "X": (XW, BF), "bk": (3 * H, BF), "XX": (2 * L, BF),
-    "wt": (2, BF), "wl0": (2, BF), "wl1": (2, BF), "wl2": (2, BF),
-    "qs": (8 * STEPS, U16), "ql": (8 * STEPS, U16), "ys": (L * STEPS, BF), "yl": (L * STEPS, BF),
-    "one": (128, BF), "zer": (256, BF), "pk": (128, I32), "Id": (128, BF), "nId": (128, BF), "IF": (256, F32), "JJ": (256, BF), "CA": (256, BF),
-    "BD0": (128, BF), "BD": (128, BF), "BDf": (8, F32), "P": (128, BF), "Pb": (128, BF), "P4": (128, F32), "P128": (128, BF), "TPm": (128, BF),
-    "NEG": (256, BF), "I4": (128, BF), "Iq": (128, BF), "I14": (256, BF), "nIh": (128, BF), "BDq": (128, BF), "BD16": (128, BF), "CH2": (16, BF),
-    "RB": (16, BF), "WO": (128, BF), "WI": (128, BF), "Ex": (2048, BF), "Mh": (128, BF), "W": (16, BF), "Wz": (48, BF),
-    "LW": (2048, BF), "lwo": (2, U16), "wrep": (16, BF), "chp": (8, BF),
-    "ni": (128, F32), "Pn": (128, F32), "pt": (128, I32), "ptb": (256, BF), "lowb": (128, BF), "hib": (16, F32), "CODE": (1280, BF),
-    "lst": (16, U16), "e2": (16, F32), "BW": (16, F32), "BB": (16, F32),
-    "Ci": (128, I32), "C16": (128, U16), "XC": (2048, BF), "D": (2048, BF), "xT": (128, BF), "XV": (128, BF), "z": (128, BF), "zh": (128, F32),
-    "Ui": (256, I32), "U2": (256, I32), "h1": (128, I32), "h2": (128, I32), "hf": (128, F32), "H16": (128, U16), "BC": (2048, BF),
-    "CG": (128, BF), "CGm": (256, BF), "EQ": (1024, BF), "evf": (128, F32), "d4": (128, BF), "fe": (128, BF), "d4P": (128, BF), "feP": (128, BF),
-    "Cf": (128, F32), "AA": (256, F32), "evP": (128, F32), "Kc": (256, F32), "ov": (256, F32), "xm": (256, BF),
-    "wr": (128, BF), "wd": (128, BF), "cap": (128, BF), "nc": (128, F32), "mk": (128, F32), "sc": (128, F32), "zc": (128, F32),
-    "scap": (128, BF), "scs": (128, F32), "sp": (128, BF), "wP": (128, BF), "wL": (128, BF),
-    "mm": (256, F32), "VC": (128, F32), "n1": (128, F32), "n2": (128, F32),
-    "i8": (128, I32), "f8": (128, F32),
+    "spi": (8, I32), "E": (128 + 1280, I32), "EF": (128 + 1280, F32), "X": (XW, BF), "bk": (3 * H, BF), "x": (L, BF), "xT": (L, BF), "nx": (L, BF),
+    "wt": (2, BF), "wl": (24, BF), "qs": (8 * STEPS, U16), "ql": (8 * STEPS, U16), "ys": (L * STEPS, BF), "yl": (L * STEPS, BF),
+    "one": (128, BF), "pk": (128, I32), "pa": (128, I32), "Id": (128, BF), "nId": (128, BF), "n2Id": (128, BF), "IF": (128, F32), "IFq": (128, F32),
+    "BD0": (128, BF), "BD": (128, BF), "BDs": (128, BF), "BDf": (32, F32), "P": (128, BF), "Pb": (128, BF), "PJ": (64, BF), "Q4": (32, BF),
+    "Mv": (32, BF), "I16": (128, F16), "il": (8, BF), "Mvf": (32, F32), "rt": (128, F32), "TR": (128, F32), "zer": (128, F32), "wsc": (128, F32), "sg": (16, F32), "CODE": (1024, BF),
+    "col": (16, F32), "KC": (384, BF), "cT": (128, BF), "c1": (128, BF), "cN": (256, BF), "T1": (128, BF), "T2": (128, BF), "P128": (128, BF), "ni": (128, BF),
+    "I4": (128, BF), "I2k": (128, BF), "I256": (128, BF), "c256": (128, BF), "nIs": (128, BF), "FE": (256, BF), "NC": (256, BF), "NW": (256, BF),
+    "RB": (24, BF), "W": (16, BF), "Wz": (192, BF), "spf": (8, F32), "sv": (128, F32),
+    "lst": (16, U16), "e2": (8, F32), "Ci": (128, I32), "C16": (128, U16), "A1": (128, F32), "Cf": (128, F32), "fe": (128, BF), "AA": (128, F32),
+    "Zs": (128, BF), "ZP": (128, BF), "XC": (2048, BF), "D": (2048, BF), "XV": (128, BF), "z": (128, BF),
+    "uz": (64, I32), "uy": (64, I32), "hz": (64, I32), "ZH": (132, F32), "Ui": (256, I32), "U2": (256, I32), "h1": (128, I32), "h2": (128, I32),
+    "H16": (128, U16), "BC": (2048, BF), "CG": (128, BF), "CGm": (256, BF), "EQ": (1024, BF), "WO": (128, BF), "ov": (256, BF),
+    "wr": (128, BF), "cap": (128, BF), "wL": (128, BF), "ZL": (144, F16), "ZS": (144, BF), "ZW": (132, BF), "b1": (8, I32), "b2": (8, I32),
+    "MK": (128, F32), "SK": (128, BF), "sc": (128, F32), "ss": (128, BF), "Mh": (128, BF),
+    "mm": (128, F32), "VC": (128, F32), "Bq": (128, F32), "YW": (128, BF),
 }
-SCRATCH = {k: ("sbuf", [128, w], d) for k, (w, d) in _S.items()}
-for _k in ("OV", "IN"):
-    SCRATCH[_k] = ("sbuf", [128, 8, 256], BF)
-for _k in ("PD0", "PD1", "PD2", "PD3", "PB4", "PB5", "PB6", "PB7"):
-    SCRATCH[_k] = ("psum", [128, 512], F32)
-_I8 = {"uz": (0, 16), "uz2": (16, 16), "hz1": (32, 8), "hz2": (40, 8), "bk1": (48, 8), "bk2": (56, 8), "ch1": (64, 8), "ch2": (72, 8),
-       "ip": (80, 1), "p15": (84, 1), "mi": (88, 1), "g8": (96, 8)}
-_F8 = {"hz": (0, 8), "ch3": (8, 8), "ch4": (16, 8), "il": (24, 8), "c128": (32, 8), "e1": (40, 16), "lwi": (56, 1), "colk": (60, 1), "m0": (64, 1),
-       "m1": (68, 1), "lwf": (72, 1), "cb": (76, 1)}
-SLICED = set("pt Ex W JJ I14 CH2 RB RBh CK CA ptb zh zc sp IF WI CGm Wz CODE IN0 IN1 IN2 IN3 PB7".split())
-DUR = {"V": 0.13, "S": 0.19, "P": 0.13, "G": 0.4, "Y": 0.1, "A": 0.0}
-COST = {"VCi": 0.24, "VXC": 0.82, "Vevf": 0.24, "VXV": 0.24, "VE": 0.43, "VEF": 0.43, "VUi": 0.26, "VU": 0.26, "Vh": 0.26, "Vhf": 0.26, "VIN": 0.47,
-        "Vd": 0.26, "VKc": 0.26, "VLW": 0.1, "SD": 0.57, "SOV": 0.57, "SEQ": 0.57, "SXC": 0.82, "SBC": 0.82, "Sov": 0.32, "Sxm": 0.32, "SCG": 0.25,
-        "Sys": 0.25, "PPD": 0.26, "PPDw": 0.38, "PPB": 0.4, "PPBu": 0.5, "PPBh": 0.26, "PPBo": 0.3, "PPBk": 0.26, "PPBv": 0.3, "PPDb": 0.52}
-for _k in ("uz", "uz2", "hz1", "hz2", "hz", "zh", "qs", "zc", "sp", "ch1", "ch2", "ch3", "ch4", "BBb", "BWa", "BWb", "bk1", "bk2", "e1", "e2", "lst", "WI", "WO",
-           "CODE", "Ex", "W", "Wz", "RB", "CH2", "nId", "pt", "ptb", "CGm", "lwi", "lwf", "lwo", "il", "c128", "BBa", "BDf", "p15", "colk", "m0", "m1", "mi",
-           "chp", "wrep", "Pb"):
-    COST["V" + _k.rstrip("0123456789")] = 0.065
-COST["Sspk"] = COST["Spsk"] = 0.13
-TUNE = {"wake": 0.13, "remote": 2.5, "look": 0.02, "noise": 0.1, "seed": 9594}
+_IN = {}
+for _buf, _w, _d, _names in (("KB", 128, BF, "nId n2Id BDs P Pb cT c1 T1 T2 P128 I4 I2k I256 c256 nIs"), ("KF", 8, F32, "BDf hi vB bv wB t1 mt m1 of vo")):
+    for _j, _k in enumerate(_names.split()):
+        _IN[_k] = (_buf, _w * _j, _w)
+    _S[_buf] = (_w * len(_names.split()), _d)
+SCRATCH = {k: ("sbuf", [128, w], d) for k, (w, d) in _S.items() if k not in _IN}
+for _k, _s, _d in (("OV", [8, 256], BF), ("IN", [4, 512], BF), ("WI", [4, 32], BF), ("Ex", [128, 16], BF), ("HB0", [18, 8], F32), ("HB1", [18, 8], F32)):
+    SCRATCH[_k] = ("sbuf", [128] + _s, _d)
+for _k in range(8):
+    SCRATCH["PB%d" % _k] = ("psum", [128, 512], F32)
+SIZE = {BF: 2, F16: 2, U16: 2, F32: 4, I32: 4}
+TUNE = {"wake": 0.15, "remote": 2.0, "load": 2.0, "tries": 3000, "noise": 0.3, "seed": 0, "xs": (1, 3), "sb": (), "sel": "SS"}
 ORDERS = {}
 DMAS = ["spi", "E", "x", "X", "wt", "bk0", "bk1", "bk2", "out", "out0"]
 SEMAPHORES = (["sV", "sS", "sP", "sG", "wloc", "wrem"] + ["d_" + k for k in DMAS]
               + [k + str(t) for k in ("qa", "qo", "ya", "yo") for t in range(STEPS)])
+CYC, PEC = 0.00083, 0.00042
 
 
 def rank_program(g, core, T, topo):
@@ -58,15 +47,32 @@ def rank_program(g, core, T, topo):
     if rank is None:
         return
     Q = {"V": g.vector, "S": g.scalar, "P": g.tensor, "G": g, "Y": g.sync}
+    V, S, PE = g.vector, g.scalar, g.tensor
     cnt = {k: 0 for k in "VSPG"}
     known = {k: {} for k in Q}
     snap = {}
-    lastw, readers, banks = {}, {}, {}
-    B = {k: T[k] for k in SCRATCH}
 
-    def sm(k, a=0, b=None):
-        buf, (o, w) = ("i8", _I8[k]) if k in _I8 else ("f8", _F8[k])
-        return B[buf][:, o + a:o + (w if b is None else b)]
+    def b(name, *idx, p=None):
+        if name in _IN:
+            name, o, w = _IN[name]
+            i = idx[0] if idx else (0, w)
+            idx = ((o + i[0], o + i[1]) + i[2:],)
+        shape = SCRATCH[name][1]
+        ix = tuple(slice(*i) if isinstance(i, tuple) else i for i in idx)
+        cols = np.arange(int(np.prod(shape[1:]))).reshape(shape[1:])[ix].reshape(-1)
+        bits = np.zeros(int(np.prod(shape[1:])), np.uint8)
+        bits[cols] = 1
+        mask = int.from_bytes(np.packbits(bits, bitorder="little").tobytes(), "little")
+        return (T[name][(slice(*p) if p else slice(None),) + ix], [(name, mask)], len(cols), SCRATCH[name][2], False)
+
+    def ind(win, off):
+        return (win[0].indirect(off[0]), win[1], 16 * off[2], win[3], off[1])
+
+    def a_(v):
+        return v[0] if isinstance(v, tuple) else v
+
+    def psum(v):
+        return v[1][0][0][:2] == "PB"
 
     def wait(eng, toks):
         best = {}
@@ -78,497 +84,428 @@ def rank_program(g, core, T, topo):
                 continue
             Q[eng].wait_ge(T.sem[s], v)
             known[eng][s] = v
-            for a, b in snap.get((s, v), {}).items():
-                known[eng][a] = max(known[eng].get(a, 0), b)
+            for k, n in snap.get((s, v), {}).items():
+                known[eng][k] = max(known[eng].get(k, 0), n)
 
-    calls = []
+    calls, touched, banks = [], {}, {}
 
-    def note(eng, rd, wr, fn, kind="c", dur=None, lat=0.0, tok=None):
-        rd, wr = rd.split(), wr.split()
+    def note(eng, rd, wr, fn, dur, kind="c", lat=0.0, tok=None):
         n, pre = len(calls), {}
-
-        def edge(m, w):
-            pre[m] = pre.get(m, False) or w
-        for k in rd:
-            for m in lastw.get(k, ()):
-                edge(m, True)
-        for k in wr:
-            old, rs = lastw.get(k, []), readers.get(k, [])
-            if k in SLICED and old and not rs and calls[old[0]]["eng"] == eng:
-                lastw[k] = old + [n]
-                for m in calls[old[0]]["pre"]:
-                    if calls[old[0]]["pre"][m]:
-                        edge(m, True)
-                continue
-            for m in old:
-                edge(m, not (eng == "P" and calls[m]["eng"] == "P"))
-            for m in rs:
-                edge(m, not (eng == "P" and calls[m]["eng"] == "P"))
-            lastw[k], readers[k] = [n], []
-        for k in rd:
-            readers.setdefault(k, []).append(n)
-        for k in sorted(set(k[:3] for k in rd + wr if k[:2] in ("PD", "PB"))):
-            cur, prev = banks.get(k, (None, [])), None
+        rd = [v for v in rd if isinstance(v, tuple)]
+        rs = [r for v in rd for r in v[1]] + [r for v in rd + wr if v[4] for r in v[4]]
+        ws = [r for v in wr for r in v[1]]
+        for regs, w in ((rs, False), (ws, True)):
+            for k, mask in regs:
+                for m, mk, mw in touched.get(k, ()):
+                    if mk & mask and (w or mw):
+                        pre[m] = pre.get(m, False) or not (w and eng == "P" and calls[m]["eng"] == "P")
+        for k, mask in ws:
+            touched[k] = [(m, mk & ~mask, mw) for m, mk, mw in touched.get(k, ()) if mk & ~mask] + [(n, mask, True)]
+        for k, mask in rs:
+            touched.setdefault(k, []).append((n, mask, False))
+        for k in sorted(set(k for k, _ in rs + ws if k[:2] == "PB")):
+            cur = banks.get(k, (None, [], []))
             if cur[0] != eng:
                 banks[k] = cur = (eng, [], cur[1])
             for m in cur[2]:
-                edge(m, True)
+                pre[m] = True
             if eng == "P":
-                for m in cur[1]:
-                    edge(m, False)
+                for m in cur[1][-1:]:
+                    pre[m] = pre.get(m, False)
             cur[1].append(n)
-        calls.append({"eng": eng, "pre": pre, "fn": fn, "kind": kind, "lat": lat, "tok": tok, "n": n,
-                      "dur": dur if dur is not None else COST.get(eng + wr[0].rstrip("0123456789"), DUR[eng])})
+        calls.append({"eng": eng, "pre": pre, "fn": fn, "kind": kind, "lat": lat, "tok": tok, "n": n, "dur": dur})
         return n
 
-    def op(eng, rd, wr, fn, dur=None):
-        return note(eng, rd, wr, fn, dur=dur)
+    def cost(eng, out, ins, two=False):
+        vs = [out] + ins
+        n = ins[0][2] if ins else out[2]
+        if out[4]:
+            return 0.05 + 3.8 * n * CYC
+        if any(v[4] for v in ins):
+            return 0.06 + 1.56 * n * CYC
+        if eng == "S":
+            return 0.06 + max(64, n) * CYC
+        r = (1.0 if any(psum(v) for v in ins) else 2.0) if two else 0.5 if all(SIZE[v[3]] == 2 for v in vs) else 1.0
+        return max(64, n * r) * CYC
 
-    dcount = {}
+    dcount, loads = {}, {}
 
-    def dma(eng, rd, wr, sem, out, in_, lat=3.0):
+    def dma(eng, sem, out, in_, lat):
         dcount[sem] = dcount.get(sem, 0) + 16
-        note(eng, rd, wr, lambda: Q[eng].dma_start(out, in_).then_inc(T.sem["d_" + sem], 16), "d", 0.1, lat, ("d_" + sem, dcount[sem]))
+        n = note(eng, [in_], [out] if isinstance(out, tuple) else [], lambda: Q[eng].dma_start(a_(out), a_(in_)).then_inc(T.sem["d_" + sem], 16),
+                 0.06, "d", lat, ("d_" + sem, dcount[sem]))
+        if isinstance(out, tuple):
+            if eng in loads:
+                calls[n]["pre"][loads[eng]] = False
+            loads[eng] = n
 
-    def send(rd, wr, out, in_, dst, arrive, left, lands):
+    def lands(m, out, arrive, n):
+        k = note("A", [], out, None, 0.0, "a", TUNE["remote"], (arrive, n))
+        calls[k]["pre"][m] = True
+
+    def send(out, in_, dst, src, arrive, left):
         rid, pid = topo.addr(dst, core)
-        m = note("G", rd, "", lambda: g.remote_dma(out, in_, T.sem[arrive], T.sem[left], pid, rid, topo.mask(core, dst)), "r", 0.4)
-        if wr:
-            n = note("A", "", wr, None, "a", 0.0, TUNE["remote"], (arrive, lands))
-            calls[n]["pre"][m] = True
+        m = note("G", [in_], [], lambda: g.remote_dma(out[0], in_[0], T.sem[arrive], T.sem[left], pid, rid, topo.mask(core, dst)), 0.3, "r")
+        lands(m, [out], arrive, len(topo.engines(src, core)))
 
-    V, S, PE = g.vector, g.scalar, g.tensor
+    def tt(out, x0, x1, o):
+        note("V", [x0, x1], [out], lambda: V.tensor_tensor(out[0], x0[0], x1[0], o), cost("V", out, [x0, x1], True))
 
-    def tt(rd, wr, out, a, b, o):
-        op("V", rd, wr, lambda: V.tensor_tensor(out, a, b, o))
+    def ts(out, x0, s1, o0, s2=None, o1=None):
+        more = () if o1 is None else (o1,)
+        note("V", [x0, s1, s2], [out], lambda: V.tensor_scalar(out[0], x0[0], a_(s1), a_(s2), o0, *more), cost("V", out, [x0]))
 
-    def ts(rd, wr, out, a, s1, s2, o0, o1=None):
-        if o1 is None:
-            op("V", rd, wr, lambda: V.tensor_scalar(out, a, s1, s2, o0))
+    def cp(out, x0):
+        note("V", [x0], [out], lambda: V.tensor_copy(out[0], x0[0]), cost("V", out, [x0]))
+
+    def scan(out, d0, d1, init, o0, o1):
+        note("V", [d0, d1], [out], lambda: V.tensor_tensor_scan(out[0], d0[0], d1[0], init, o0, o1), cost("V", out, [d0, d1]))
+
+    def fill(out, c):
+        note("V", [], [out], lambda: V.memset(out[0], c), cost("V", out, []))
+
+    def act(out, x0, f, bias=0.0, scale=1.0):
+        note("S", [x0, bias, scale], [out], lambda: S.activation(out[0], x0[0], f, bias=a_(bias), scale=a_(scale)), cost("S", out, [x0]))
+
+    def mul(eng, out, x0, c):
+        if eng == "S":
+            act(out, x0, F.Copy, scale=c)
         else:
-            op("V", rd, wr, lambda: V.tensor_scalar(out, a, s1, s2, o0, o1))
+            ts(out, x0, c, A.mult)
 
-    def cp(rd, wr, out, a):
-        op("V", rd, wr, lambda: V.tensor_copy(out, a))
-
-    def act(rd, wr, out, a, f, **kw):
-        op("S", rd, wr, lambda: S.activation(out, a, f, **kw))
-
-    def mms(rd, wr, lst):
+    def mm(lst, start=True, stop=True, apart=False, more=()):
         def go():
             i = None
-            for out, l, r, st, sp in lst:
-                i = PE.matmul(out, l, r, st, sp)
+            for n, (o, l, r) in enumerate(lst):
+                i = PE.matmul(o[0], l[0], r[0], apart or (start and n == 0), apart or (stop and n == len(lst) - 1))
             return i
-        op("P", rd, wr, go)
+        m = note("P", [v for _, l, r in lst for v in (l, r)], [o for o, _, _ in lst], go,
+                 sum(max(min(64, l[2]), r[2]) * SIZE[l[3]] ** 2 / 4 * PEC for _, l, r in lst))
+        for k in more:
+            calls[m]["pre"][k] = True
+        return m
 
-    def memset(wr, ap, c):
-        op("V", "", wr, lambda: V.memset(ap, c))
+    def gp(out, ins, fn):
+        note("G", ins, [out], fn, 0.15 + 2 * out[2] * CYC)
 
-    nx, x = B["XX"][:, 0:L], B["XX"][:, L:2 * L]
-    dma("Y", "", "spi", "spi", B["spi"][:], T.spot[:])
-    dma("Y", "", "E", "E", B["E"][:, 128:128 + M], T.kids[:])
-    dma("S", "", "wt", "wt", B["wt"][:], T.wts[:])
-    dma("S", "", "x", "x", x, T.cand[:])
-    dma("S", "", "X", "X", B["X"][:, 0:M], T.nodes[:])
+    def c_(a, n):
+        return (a, a + n)
+
+    one, Id, nId, IF, BD, P, PJ = (b(k) for k in ("one", "Id", "nId", "IF", "BD", "P", "PJ"))
+    x, xT = b("x"), b("xT")
+    bd8, bd32, pj = b("BD", (0, 128, 16)), b("BD", (0, 128, 4)), b("PJ", (0, 32))
+
+    def pad(k):
+        return b(k, (3, 131, 4))
+
+    def tolist(out, k, mv):
+        return [(out, b(k, c_(3 - kk, 128)), b(mv, (kk, 32, 4))) for kk in range(4)]
+
+    ld = TUNE["load"]
+    dma("Y", "spi", b("spi"), T.spot[:], ld - 0.6)
+    dma("Y", "E", b("E", c_(128, M)), T.kids[:], ld + 0.6)
+    dma("S", "wt", b("wt"), T.wts[:], ld - 0.6)
+    dma("S", "x", x, T.cand[:], ld - 0.5)
+    dma("Y", "X", b("X", (0, M)), T.nodes[:], ld + 1.4)
     for j in range(3):
-        dma("Y", "", "bk%d" % j, "bk%d" % j, B["bk"][:, H * j:H * j + H], T.book[:])
+        dma("Y", "bk%d" % j, b("bk", c_(H * j, H)), T.book[:], ld + 3.2 + 1.8 * j)
 
-    memset("one", B["one"][:], 1.0)
-    memset("zer", B["zer"][:], 0.0)
-    op("G", "one", "Id", lambda: g.affine_select(B["Id"][:], B["one"][:], [[-1, 128]], A.is_equal, 0.0, 0, 1))
-    op("G", "one", "BD0", lambda: g.affine_select(B["BD0"][:], B["one"][:], [[-16, 8], [0, 16]], A.is_ge, 0.0, 0, 1))
-    op("G", "BD0", "BD", lambda: g.affine_select(B["BD"][:], B["BD0"][:], [[16, 8], [0, 16]], A.is_ge, 0.0, 15, -1))
-    op("G", "", "pk", lambda: g.iota(B["pk"][:], [[0, 8], [-1, 16]], 16, 1))
-    op("G", "", "ip", lambda: g.iota(sm("ip"), [[0, 1]], 0, 1))
-    op("G", "", "g8", lambda: g.iota(sm("g8"), [[0, 8]], 0, 1))
-    neng = len(topo.engines(core, T.cores[(rank + 1) % NB]))
-    for j in range(NB - 1):
-        send("wt", "wl0 wl1 wl2" if j == NB - 2 else "", B["wl%d" % j][:], B["wt"][:], T.cores[(rank - 1 - j) % NB], "wrem", "wloc", neng * (NB - 1))
-    op("G", "zer", "NEG", lambda: g.affine_select(B["NEG"][:], B["zer"][:], [[0, 2], [1, 128]], A.is_gt, -100.0, 0, -1))
-    op("G", "", "ni", lambda: g.iota(B["ni"][:], [[1, 128]], M, 0, allow_small_or_imprecise_dtypes=True))
-    op("G", "", "LW", lambda: g.iota(B["LW"][:], [[0, 2048]], 0, 0, allow_small_or_imprecise_dtypes=True))
+    fill(one, 1.0)
+    gp(b("pk"), [], lambda: g.iota(T.pk[:], [[0, 8], [-1, 16]], 16, 1))
+    gp(Id, [one], lambda: g.affine_select(T.Id[:], T.one[:], [[-1, 128]], A.is_equal, 0.0, 0, 1))
+    gp(b("BD0"), [one], lambda: g.affine_select(T.BD0[:], T.one[:], [[-16, 8], [0, 16]], A.is_ge, 0.0, 0, 1))
+    gp(BD, [b("BD0")], lambda: g.affine_select(T.BD[:], T.BD0[:], [[16, 8], [0, 16]], A.is_ge, 0.0, 15, -1))
+    others = [T.cores[(rank - 1 - j) % NB] for j in range(NB - 1)]
+    neng = len(topo.engines(core, others[0]))
 
-    memset("Xz", B["X"][:, M:XW], 0.0)
-    memset("ptb0", B["ptb"][:, 128:256], 0.0)
-    memset("pt0", B["pt"][:], 0)
-    memset("Mh", B["Mh"][:], 1.0)
-    memset("Mh", B["Mh"][:, 0:128:16], 0.0)
-    memset("IF", B["IF"][:, 128:256], 0.0)
-    memset("CA", B["CA"][:, 0:128], -2.0)
-    memset("CA", B["CA"][:, 128:256], 0.0)
-    bd8 = B["BD"][:, 0:128:16]
-    ts("Id", "nId", B["nId"][:], B["Id"][:], -1.0, None, A.mult)
-    mms("x Id", "PB4x", [(B["PB4"][:, 384:512], x, B["Id"][:], True, True)])
-    act("PB4x", "xT", B["xT"][:], B["PB4"][:, 384:512], F.Copy)
-    EXR = "Ex"
-    for k in range(16):
-        if k % 3 == 2:
-            act("Id", "Ex%d" % k, B["Ex"][:, k:2048:16], B["Id"][:], F.Copy)
-            EXR += " Ex%d" % k
-        else:
-            cp("Id", "Ex", B["Ex"][:, k:2048:16], B["Id"][:])
-    ts("pk", "Ci", B["Ci"][:], B["pk"][:], 15, None, A.bitwise_and)
-    ts("Ci", "P", B["P"][:], B["Ci"][:], 0, None, A.is_equal)
-    cp("Id", "IF", B["IF"][:, 0:128], B["Id"][:])
-    cp("BD", "BDf", B["BDf"][:], bd8)
-    ts("ip", "p15", sm("p15"), sm("ip"), 15, None, A.bitwise_and)
-    ts("p15", "colk", sm("colk"), sm("p15"), -2048.0, 30720.0, A.mult, A.add)
-    ts("P", "Pb", B["Pb"][:], B["P"][:], -1.0, 1.0, A.mult, A.add)
-    CP, CPb, CP4 = (B["PB7"][:, 128 * j:128 * j + 128] for j in range(3))
-    cp("P", "PB7", CP, B["P"][:])
-    cp("Pb", "PB7", CPb, B["Pb"][:])
-    ts("Pb", "PB7", CP4, B["Pb"][:], 4095.0, None, A.mult)
-    act("P", "TPm", B["TPm"][:], B["P"][:], F.Copy, scale=1000.0, bias=-1000.0)
-    act("colk", "cb", sm("cb"), sm("colk"), F.Copy, scale=-1.0, bias=-4095.0)
-    for k, src, f in (("nIh", "Id", -0.5), ("I4", "Id", 4096.0), ("Iq", "Id", 1.0 / 4096), ("P128", "P", 128.0), ("BDq", "BD", 1.0 / 4096),
-                      ("BD16", "BD", -16.0)):
-        act(src, k, B[k][:], B[src][:], F.Copy, scale=f)
-    memset("I14z", B["I14"][:, 128:256], 0.0)
-    act("Id", "I14", B["I14"][:, 0:128], B["Id"][:], F.Copy, scale=-16384.0)
+    def weights():
+        ids = [DstId(rid=topo.addr(d, core)[0], pnc=topo.addr(d, core)[1]) for d in others]
+        return g.remote_dma_fused([RemoteDMATransfer(dst_ids=ids, dma_engine_mask=topo.mask(core, others[0]), remote_sem=T.sem.wrem, srcs=[T.wt[:]],
+                                                     dsts=[T.wl[:, 8 * j:8 * j + 2] for j in range(NB - 1)])], local_sem=T.sem.wloc)
+    lands(note("G", [b("wt")], [], weights, 0.5, "r"), [b("wl")], "wrem", neng * (NB - 1))
+    fill(b("rt"), 0.35)
+    fill(b("zer"), 0.0)
+    gp(b("TR"), [b("rt")], lambda: g.affine_select(T.TR[:], T.rt[:], [[-1, 128]], A.is_gt, 1.0, 0, 1))
+    gp(b("ni"), [], lambda: g.iota(T.ni[:], [[1, 128]], 1, 0, allow_small_or_imprecise_dtypes=True))
+    scan(b("wsc"), b("TR"), b("zer"), 2.0 ** 96, A.mult, A.add)
+    wcol = b("wsc", (127, 128))
+
+    fill(b("X", (M, XW)), 0.0)
+    for k in ("ZS", "ZW", "ZH", "HB0", "HB1"):
+        fill(b(k), 0.0)
+    cp(b("ZL"), b("ZS"))
+    fill(b("Mh"), 1.0)
+    fill(b("Mh", (0, 128, 16)), 0.0)
+    fill(b("KC", (128, 256)), -0.5 / 128)
+    fill(b("KC", (256, 384)), 0.0)
+    fill(b("cT"), -BIG / 128)
+    fill(b("c1"), 1.0 / 128)
+    fill(b("c256"), -2.0)
+    fill(b("cN", (0, 128)), (4096.0 - 2.0 ** 19) / 128)
+    fill(b("cN", (128, 256)), 2.0 / 128)
+    cp(b("Ex", (0, 128), (0, 1)), Id)
+    for n in (1, 2, 4, 8):
+        cp(b("Ex", (0, 128), c_(n, n)), b("Ex", (0, 128), (0, n)))
+    mul("V", nId, Id, -1.0)
+    mm([(b("PB7", (384, 512)), x, Id)])
+    act(xT, b("PB7", (384, 512)), F.Copy)
+    ts(b("pa"), b("pk"), 15, A.bitwise_and)
+    ts(P, b("pa"), 0, A.is_equal)
+    ts(b("uz", (0, 32)), b("pk", (0, 128, 4)), 12, A.bitwise_and)
     for j in range(2):
-        act("Id", "JJ", B["JJ"][:, 128 * j:128 * j + 128], B["Id"][:], F.Copy, scale=(256.0, -256.0)[j])
-        cp("BD", "CH2", B["CH2"][:, 8 * j:8 * j + 8], bd8)
-        ts("BD", "RB", B["RB"][:, 8 * j:8 * j + 8], bd8, (32768.0, 1.0)[j], None, A.mult)
-    pt = B["pt"]
-    for b in range(7):
-        ts("g8 pt0", "pt", pt[:, b:128:16], sm("g8"), b, 1, A.logical_shift_right, A.bitwise_and)
-    ts("pt", "ptb", B["ptb"][:, 0:128], pt[:], 2.0, -1.0, A.mult, A.add)
-    for b in range(7, 11):
-        ts("ptb0 pt", "ptb", B["ptb"][:, 128 + b:256:16], pt[:, b - 7:128:16], 2.0, None, A.mult)
-    mms("ptb Id", "PB6c", [(B["PB6"][:, 256:384], B["ptb"][:, 0:128], B["Id"][:], True, True),
-                           (B["PB6"][:, 384:400], B["ptb"][:, 128:256], B["Id"][:, 0:16], True, True)])
-    act("PB6c", "hib", B["hib"][:], B["PB6"][:, 384:400], F.Copy)
-    act("PB6c", "lowb", B["lowb"][:], B["PB6"][:, 256:384], F.Copy)
-    ts("ip", "mi", sm("mi"), sm("ip"), 4, 1, A.logical_shift_right, A.bitwise_and)
-    cp("mi", "m1", sm("m1"), sm("mi"))
-    ts("m1", "m0", sm("m0"), sm("m1"), -1.0, 1.0, A.mult, A.add)
-    cp("ip", "lwi", sm("lwi"), sm("ip"))
-    ts("BD lwi", "chp", B["chp"][:], bd8, sm("lwi"), None, A.mult)
-    mms("P chp", "PD3i", [(B["PD3"][:, 0:8], B["P"][:], B["chp"][:], True, True)])
-    cp("PD3i", "il", sm("il"), B["PD3"][:, 0:8])
-    ts("il", "c128", sm("c128"), sm("il"), -1.0, 128.0, A.mult, A.add)
-    cp("il", "BBa", B["BB"][:, 0:8], sm("il"))
+        ts(b("PJ", c_(32 * j, 32)), b("uz", (0, 32)), 0, A.is_equal)
+    ts(b("uz", (32, 64)), b("pk", (0, 32)), 3, A.bitwise_and)
+    ts(b("Q4"), b("uz", (32, 64)), 0, A.is_equal)
+    tt(b("Mvf"), bd32, b("Q4"), A.mult)
+    ts(b("Pb"), P, -1.0, A.mult, 1.0, A.add)
+    kcol, slot, m0, m1 = (b("col", c_(j, 1)) for j in (0, 2, 6, 8))
+    ts(kcol, b("pa", (0, 1)), -512.0, A.mult, 8192.0, A.add)
+    ts(slot, b("pa", (0, 1)), -1.0, A.add)
+    ts(b("il"), b("ni", (0, 128, 16)), slot, A.add)
+    for j, m in enumerate((m0, m1)):
+        note("V", [BD], [m], lambda j=j, m=m: V.tensor_reduce(m[0], T.BD[:, 16 * j:128:32], AX.X, A.add), 64 * CYC)
+    for eng, out, src, f in (("S", IF, Id, 1.0), ("S", b("IFq"), Id, 1.0 / 4096), ("S", b("KC", (0, 128)), P, kcol), ("S", b("BDs"), BD, 2 * BIG),
+                             ("V", b("n2Id"), Id, -2.0), ("V", b("I4"), Id, 4096.0), ("V", b("I2k"), Id, 2048.0), ("V", b("I256"), Id, 256.0),
+                             ("V", b("nIs"), Id, -2 * BIG), ("V", b("FE", (0, 128)), Id, -TOP), ("V", b("FE", (128, 256)), Id, -4096.0),
+                             ("V", b("NC", (0, 128)), Id, 2.0 ** 18 / BIG), ("V", b("NC", (128, 256)), Id, -1.0 / BIG),
+                             ("V", b("NW", (0, 128)), Id, 2.0 ** 18), ("V", b("NW", (128, 256)), Id, -1.0), ("V", b("P128"), P, 128.0),
+                             ("S", b("BDf"), bd8, 1.0), ("V", b("I16"), Id, 1.0), ("V", b("Mv"), b("Mvf"), 4096.0), ("V", b("RB", (0, 8)), bd8, 65536.0), ("V", b("RB", (8, 16)), bd8, 1.0),
+                             ("V", b("RB", (16, 24)), bd8, 1.0)):
+        mul(eng, out, src, f)
+    ts(b("T1"), P, M - 4096.0, A.mult, 4096.0, A.add)
+    tt(b("YW"), P, b("ni"), A.mult)
+    ts(b("T2"), b("YW"), -1.0, A.add)
+    ts(b("sg"), b("P", (0, 16)), -2.0, A.mult, 1.0, A.add)
+    fill(b("CODE", (0, 1)), -1.0)
+    for j in range(10):
+        ts(b("CODE", c_(2 ** j, 2 ** j)), b("CODE", (0, 2 ** j)), b("sg", c_(j, 1)), A.mult)
     for u in range(2):
-        ts("BD wt", "W", B["W"][:, 8 * u:8 * u + 8], bd8, B["wt"][:, u:u + 1], None, A.mult)
-    cp("spi", "lst", B["lst"][:, 8:16], B["spi"][:])
-    cp("spi", "e2", B["e2"][:, 8:16], B["spi"][:])
+        ts(b("W", c_(8 * u, 8)), bd8, b("wt", c_(u, 1)), A.mult)
+    for j in range(3):
+        for u in range(2):
+            ts(b("Wz", c_(64 * j + 32 * u, 32)), bd32, b("wl", c_(8 * j + u, 1)), A.mult)
+    v16, o16 = b("lst", (8, 16)), b("lst", (0, 8))
+    cp(v16, b("spi"))
+    cp(b("spf"), b("spi"))
+    for c in range(8):
+        mul("S", b("sv", c_(16 * c, 16)), b("P", (0, 16)), b("spf", c_(c, 1)))
+    mm([(b("PB7", (0, 8)), b("sv"), b("BDf"))])
+    vl = b("ZL", (15, 143, 16))
+    cp(vl, b("PB7", (0, 8)))
+    ts(b("vo"), b("spi"), 128.0, A.add)
 
-    def code_blocks():
-        for h in range(10):
-            ts("lowb hib", "CODE", B["CODE"][:, 128 * h:128 * h + 128], B["lowb"][:], B["hib"][:, h:h + 1], None, A.add)
+    def PB(k, a=0, n=512, s=1):
+        return b("PB%d" % k, (a, a + n, s))
 
-    def late_consts():
-        tt("P ni", "Pn", B["Pn"][:], B["P"][:], B["ni"][:], A.mult)
-        ts("p15 lwi", "lwf", sm("lwf"), sm("p15"), 128.0, sm("lwi"), A.mult, A.add)
-        cp("lwf", "lwo", B["lwo"][:, 0:1], sm("lwf"))
-        ts("one wt", "wrep", B["wrep"][:], B["one"][:, 0:16], B["wt"][:, 0:1], None, A.mult)
-        op("V", "lwo wrep LW", "LW", lambda: V.tensor_copy(B["LW"][:].indirect(B["lwo"][:, 0:1]), B["wrep"][:]))
+    def ch(k, c):
+        return b(k, c_(512 * c, 512))
 
-    PD = [B["PD%d" % b] for b in range(4)]
-    U, KS, PB6 = B["PB4"], B["PB5"], B["PB6"]
-    v16, vf = B["lst"][:, 8:16], B["e2"][:, 8:16]
-    sb = list(SBANKS)
-    vbk = [b for b in range(4) if b not in sb]
-    vb = [b for b in range(4) if b not in XS]
-    order = list(range(4))
-    dorder = list(XS) + vb
-    ch = [slice(512 * b, 512 * b + 512) for b in range(4)]
-    c32 = [slice(32 * b, 32 * b + 32) for b in range(4)]
-
-    def newcols(t):
-        tt("PB5n AAa", "mma", B["mm"][:, 0:128], KS[:, 0:128], B["AA"][:, 0:128], A.mult)
-        tt("PB5n mma", "n1", B["n1"][:], KS[:, 128:256], B["mm"][:, 0:128], A.add)
-        tt("PB5n n1", "n2", B["n2"][:], KS[:, 256:384], B["n1"][:], A.mult)
-        k = "EF" if t == STEPS - 1 else "E"
-        c = 128 + M + L * t
-        ts("n2", k + str(t), B[k][:, c:c + L], B["n2"][:], 4095.0, None, A.add)
-
-    def nodes_at(t):
-        op("V", "X lst " + " ".join("X%d" % j for j in range(t - 1)), "XV",
-           lambda: V.tensor_copy(B["XV"][:], B["X"][:, 0:M + L * max(0, t - 1)].indirect(v16)))
-
-    def newx():
-        mms("xm Id", "PB4x", [(U[:, 256:384], B["Id"][:], B["xm"][:, 0:128], True, False), (U[:, 256:384], B["Id"][:], B["xm"][:, 128:256], False, True)])
-        act("PB4x", "x", x, U[:, 256:384], F.Copy)
+    def ch3(k, c):
+        return b(k, c_(2 * c, 2))
 
     for t in range(STEPS):
         last = t == STEPS - 1
         wg = M + L * max(0, t - 1)
-        XR = "X Xz " + " ".join("X%d" % j for j in range(t))
-        ER = "E " + " ".join("E%d" % j for j in range(t - 1))
-        qb = (rank + 1 + t) % NB
-        qf = (rank - 1 - t) % NB
-        ts(ER + " lst", "Ci", B["Ci"][:], B["E"][:, 128:128 + wg].indirect(v16), 4095, None, A.bitwise_and)
-        ts("Ci", "C16", B["C16"][:], B["Ci"][:], 1280.0, None, A.min)
-        if t == 0:
-            nodes_at(t)
-        mms("XV xm Id nId x", "PB5z", [(KS[:, 384:512], B["Id"][:], B["XV"][:], True, False)]
-            + ([(KS[:, 384:512], B["nId"][:], x, False, True)] if t == 0 else
-               [(KS[:, 384:512], B["nId"][:], B["xm"][:, L * j:L * j + L], False, j == 1) for j in range(2)]))
-        act("PB5z", "z", B["z"][:], KS[:, 384:512], F.Abs)
+        asked, asker = T.cores[(rank + 1 + t) % NB], T.cores[(rank - 1 - t) % NB]
+        Ev = ind(b("E", c_(128, wg)), v16)
+        bk = b("bk") if t else b("bk", (0, H))
+        yl = b("yl", c_(L * t, L))
+        ts(b("Ci"), Ev, 4095, A.bitwise_and)
+        ts(b("C16"), b("Ci"), 1280.0, A.min)
+        cp(b("XV"), ind(b("X", (0, wg)), v16))
+        mm([(PB(7, 384, 128), Id, b("XV")), (PB(7, 384, 128), nId, x)])
+        act(b("z"), PB(7, 384, 128), F.Abs)
+        mm([(PB(7, 384, 64), b("z"), b("Wz", c_(64 * t, 64)))])
+        tt(b("uz"), PB(7, 384, 64), PJ, A.mult)
+        ts(b("uy"), b("uz"), 4095, A.bitwise_and)
+        tt(b("hz", (0, 32)), b("uy", (0, 32)), b("uy", (32, 64)), A.mult)
+        ts(b("hz", (32, 64)), b("hz", (0, 32)), 5, A.logical_shift_right, H - 1, A.bitwise_and)
         if t:
-            mms("z Wz", "PB5u", [(KS[:, 384:400], B["z"][:], B["Wz"][:, 16 * t:16 * t + 16], True, True)])
-        for b in order:
-            mms("%s xT" % EXR, "PD%d" % b, [(PD[b][:], B["xT"][:], B["Ex"][:, ch[b]], True, False)])
-
-        def diff(b):
-            mms("nId XC%d" % b, "PD%d" % b, [(PD[b][:], B["nId"][:], B["XC"][:, ch[b]], False, True)])
-
-        def hashsum(b0, b1):
-            mms(" ".join("D%d" % b for b in range(b0, b1)) + " W", "PB4u",
-                [(U[32 * b0:32 * b1, k:256:16], B["D"][:, 512 * b0 + k:512 * b1:16], B["W"][:], True, True) for k in range(16)])
-
-        for b in XS:
-            act(XR + " C16", "XC%d" % b, B["XC"][:, ch[b]], B["X"][:].indirect(B["C16"][:, c32[b]]), F.Copy)
-        if t:
-            newx()
-        if t == 0:
-            for b in vb[:-1]:
-                cp(XR + " C16", "XC%d" % b, B["XC"][:, ch[b]], B["X"][:].indirect(B["C16"][:, c32[b]]))
-            for b in dorder[:-1]:
-                diff(b)
-            for j in range(3):
-                for u in range(2):
-                    ts("BD wl%d" % j, "Wz", B["Wz"][:, 16 * j + 8 * u:16 * j + 8 * u + 8], bd8, B["wl%d" % j][:, u:u + 1], None, A.mult)
-            mms("z Wz", "PB5u", [(KS[:, 384:400], B["z"][:], B["Wz"][:, 16 * t:16 * t + 16], True, True)])
-        cp("PB5u", "uz", sm("uz"), KS[:, 384:400])
-        ts("uz", "uz2", sm("uz2"), sm("uz"), 4095, None, A.bitwise_and)
-        tt("uz2", "hz1", sm("hz1"), sm("uz2", 0, 8), sm("uz2", 8, 16), A.mult)
-        ts("hz1", "hz2", sm("hz2"), sm("hz1"), 5, H - 1, A.logical_shift_right, A.bitwise_and)
-        if t:
-            tt("hz2 uz2", "hz", sm("hz"), sm("hz2"), sm("uz2", 8, 16), A.add)
+            tt(pad("ZH"), b("hz", (32, 64)), b("uy", (32, 64)), A.add)
         else:
-            tt("hz2 uz2", "hz1", sm("hz1"), sm("hz2"), sm("uz2", 8, 16), A.add)
-            ts("hz1", "hz2", sm("hz2"), sm("hz1"), H - 1, None, A.bitwise_and)
-            cp("hz2", "hz", sm("hz"), sm("hz2"))
-        for k in range(8):
-            ts("P hz", "zh", B["zh"][:, 16 * k:16 * k + 16], B["P"][:, 0:16], sm("hz", k, k + 1), None, A.mult)
-        mms("zh BDf", "PB5q", [(KS[:, 400:408], B["zh"][:], B["BDf"][:], True, True)])
-        if t:
-            for b in XS:
-                diff(b)
-        ts("Ci", "fe", B["fe"][:], B["Ci"][:], 4095.0, 128.0, A.is_ge, A.mult)
-        ts("Ci colk", "Cf", B["Cf"][:], B["Ci"][:], sm("colk"), None, A.add)
-        cp("PB5q", "qs%d" % t, B["qs"][:, 8 * t:8 * t + 8], KS[:, 400:408])
-        send("qs%d" % t, "ql%d" % t, B["ql"][:, 8 * t:8 * t + 8], B["qs"][:, 8 * t:8 * t + 8], T.cores[qb], "qa%d" % t, "qo%d" % t,
-             len(topo.engines(T.cores[qf], core)))
-        for b in vb if t else vb[-1:]:
-            cp(XR + " C16", "XC%d" % b, B["XC"][:, ch[b]], B["X"][:].indirect(B["C16"][:, c32[b]]))
-            if b != 3:
-                diff(b)
-        for n, b in enumerate(dorder):
-            act("PD%d" % b, "D%d" % b, B["D"][:, ch[b]], PD[b][:], F.Abs)
-            if n == 0 and t:
-                act("CODE lst", "CG", B["CG"][:], B["CODE"][:].indirect(v16), F.Copy)
-            if n == 1:
-                diff(3)
-            if n == 2:
-                hashsum(0, 3)
-        hashsum(3, 4)
-        if t == 0:
-            code_blocks()
-            act("CODE lst", "CG", B["CG"][:], B["CODE"][:].indirect(v16), F.Copy)
-        op("V", ER + " lst", "evf", lambda wg=wg: V.tensor_copy(B["evf"][:], B["E"][:, 128:128 + wg].indirect(v16)))
-        tt("evf Ci", "d4", B["d4"][:], B["evf"][:], B["Ci"][:], A.subtract)
-        tt("d4 PB7", "d4P", B["d4P"][:], B["d4"][:], CP, A.mult)
-        tt("fe PB7", "feP", B["feP"][:], B["fe"][:], CP, A.mult)
-        for j in range(2):
-            ts("CG m%d" % j, "CGm", B["CGm"][:, 128 * j:128 * j + 128], B["CG"][:], sm("m%d" % j), None, A.mult)
-        cp("PB4u", "Ui", B["Ui"][:], U[:, 0:256])
-        ts("Ui", "U2", B["U2"][:], B["Ui"][:], 4095, None, A.bitwise_and)
-        tt("U2", "h1", B["h1"][:], B["U2"][:, 0:128], B["U2"][:, 128:256], A.mult)
-        ts("h1", "h2", B["h2"][:], B["h1"][:], 5, H - 1, A.logical_shift_right, A.bitwise_and)
-        tt("h2 U2", "hf", B["hf"][:], B["h2"][:], B["U2"][:, 128:256], A.add)
-        if t:
-            newcols(t - 1)
-
-
-        def eqmat(h):
+            tt(b("hz", (0, 32)), b("hz", (32, 64)), b("uy", (32, 64)), A.add)
+            ts(b("hz", (32, 64)), b("hz", (0, 32)), H - 1, A.bitwise_and)
+            cp(pad("ZH"), b("hz", (32, 64)))
+        mm(tolist(PB(7, 448, 8), "ZH", "Mvf"))
+        cp(b("qs", c_(8 * t, 8)), PB(7, 448, 8))
+        send(b("ql", c_(8 * t, 8)), b("qs", c_(8 * t, 8)), asked, asker, "qa%d" % t, "qo%d" % t)
+        for c in range(4):
+            mm([(PB(c), xT, b("Ex", c_(32 * c, 32)))], stop=False)
+            src = ind(b("X"), b("C16", c_(32 * c, 32)))
+            if c in TUNE["xs"]:
+                act(ch("XC", c), src, F.Copy)
+            else:
+                cp(ch("XC", c), src)
+            mm([(PB(c), nId, ch("XC", c))], start=False)
+            act(ch("D", c), PB(c), F.Abs)
+            act(ch3("OV", c), PB(c), F.Sign, bias=0.5)
+        ts(b("A1"), Ev, -1.0, A.mult, 4095.0, A.add)
+        ts(b("Cf"), b("Ci"), -4096.0, A.add)
+        act(b("fe"), b("Cf"), F.Relu, bias=2.0)
+        tt(b("AA"), b("A1"), b("Pb"), A.mult)
+        mm([(PB(7, 256, 128), b("IFq"), b("A1")), (PB(7, 256, 128), b("IFq"), b("Cf")), (PB(7, 256, 128), b("I2k"), b("fe"))])
+        act(b("Zs"), PB(7, 256, 128), F.Copy)
+        tt(b("ZP"), PB(7, 256, 128), P, A.mult)
+        ts(b("vB"), vl, TOP, A.add)
+        act(b("CG"), ind(b("CODE"), v16), F.Copy)
+        for j, m in enumerate((m0, m1)):
+            ts(b("CGm", c_(128 * j, 128)), b("CG"), m, A.mult)
+        for h in range(2):
+            u, hb = 4 + h, "HB%d" % h
+            mm([(PB(u, k, 128 - k, 8), b("D", (1024 * h + k, 1024 * h + 1024, 8)), b("W")) for k in range(8)], apart=True)
+            u1, u2, h1, h2 = b("U2", c_(128 * h, 64)), b("U2", c_(128 * h + 64, 64)), b("h1", c_(64 * h, 64)), b("h2", c_(64 * h, 64))
+            cp(b("Ui", c_(128 * h, 128)), PB(u, 0, 128))
+            ts(b("U2", c_(128 * h, 128)), b("Ui", c_(128 * h, 128)), 4095, A.bitwise_and)
+            tt(h1, u1, u2, A.mult)
+            ts(h2, h1, 5, A.logical_shift_right, H - 1, A.bitwise_and)
+            if t:
+                tt(b(hb, (1, 17, 2)), h2, u2, A.add)
+            else:
+                tt(h1, h2, u2, A.add)
+                ts(h2, h1, H - 1, A.bitwise_and)
+                cp(b(hb, (1, 17, 2)), h2)
+            mm([(PB(u, 128, 64), b(hb, c_(1 - kk, 16)), b("IF", (kk, 128, 2))) for kk in range(2)])
+            cp(b("H16", c_(64 * h, 64)), PB(u, 128, 64))
+        act(b("ys", c_(L * t, L)), ind(bk, b("ql", c_(8 * t, 8))), F.Copy)
+        send(yl, b("ys", c_(L * t, L)), asker, asked, "ya%d" % t, "yo%d" % t)
+        mm([(PB(7, k, 128 - k, 16), b("OV", (0, 8), (k, 256, 16)), bd8) for k in range(16)], apart=True)
+        cp(b("WO"), b("OV", (0, 8), (0, 256, 17)))
+        mm([(PB(7, 128, 128), b("WO"), BD)])
+        act(b("ov"), PB(7, 0, 256), F.Relu, scale=-64.0, bias=128.0)
+        for h in range(2):
+            more = ()
             for a in (2 * h, 2 * h + 1):
-                o = PD[h][:, 256 * (a % 2):256 * (a % 2) + 256]
-                mms("CG CGm NEG Id", "PD%d" % h, [(o, B["Id"][:], B["NEG"][:], True, False)])
-                mms("CG CGm" + (" rt%d" % h if a % 2 else ""), "PD%d" % h + ("" if a % 2 else " rt%d" % h), [(o, B["CG"][32 * a:32 * a + 32, :], B["CGm"][32 * a:32 * a + 32, :], False, True)])
-
-        def eqact(h):
-            act("PD%d" % h, "EQ%d" % h, B["EQ"][:, 512 * h:512 * h + 512], PD[h][:], F.Relu, bias=-15.0)
-        for n, b in enumerate(order):
-            act("PD%d" % b, "OV%d" % b, B["OV"][:, 2 * b:2 * b + 2, :], PD[b][:], F.Sign, bias=0.5)
-        eqmat(0)
-        op("P", "hf IF", "PB4h", lambda: PE.transpose(U[:, 256:384], B["hf"][:], B["IF"][:, 0:128]))
-        if t:
-            cp("PB4h", "H16", B["H16"][:], U[:, 256:384])
-        else:
-            cp("PB4h", "h1", B["h1"][:], U[:, 256:384])
-            ts("h1", "h2", B["h2"][:], B["h1"][:], H - 1, None, A.bitwise_and)
-            cp("h2", "H16", B["H16"][:], B["h2"][:])
-        bk = B["bk"][:] if t else B["bk"][:, 0:H]
-        BK = "bk0 bk1 bk2" if t else "bk0"
-        eqmat(1)
-        mms("OV0 OV1 OV2 OV3 BD", "PB6o", [(PB6[:, k:128:16], B["OV"][:, :, k:256:16], bd8, True, True) for k in range(16)])
-        cp("OV0 OV1 OV2 OV3", "WO", B["WO"][:], B["OV"][:, :, 0:256:17])
-        mms("WO BD", "PB6o", [(PB6[:, 128:256], B["WO"][:], B["BD"][:], True, True)])
-        mms("Cf IF", "PB5", [(KS[:, 0:256], B["Cf"][:], B["IF"][:], True, False)])
-        def sbook(b):
-            act(BK + " H16", "BC%d" % b, B["BC"][:, ch[b]], bk.indirect(B["H16"][:, c32[b]]), F.Copy)
-
-        def vbook(b):
-            for c in (2 * b, 2 * b + 1):
-                tt(BK + " H16 D%d" % b, "IN%d" % b, B["IN"][:, c, :], bk.indirect(B["H16"][:, 16 * c:16 * c + 16]), B["D"][:, 256 * c:256 * c + 256], A.is_ge)
-
-        def bdiff(b):
-            mms("Id nId BC%d D%d" % (b, b), "PD%d" % b, [(PD[b][:], B["Id"][:], B["BC"][:, ch[b]], True, False), (PD[b][:], B["nId"][:], B["D"][:, ch[b]], False, True)])
-
-        def count(b0, b1):
-            mms(" ".join("IN%d" % b for b in range(b0, b1)) + " RB", "PB5",
-                [(KS[32 * b0:32 * b1, k:256:16], B["IN"][:, 2 * b0:2 * b1, k:256:16], B["RB"][:], False, False) for k in range(16)])
-        def answer():
-            act(BK + " ql%d" % t, "ys%d" % t, B["ys"][:, L * t:L * t + L], bk.indirect(B["ql"][:, 8 * t:8 * t + 8]), F.Copy)
-            send("ys%d" % t, "yl%d" % t, B["yl"][:, L * t:L * t + L], B["ys"][:, L * t:L * t + L], T.cores[qf], "ya%d" % t, "yo%d" % t,
-                 len(topo.engines(T.cores[qb], core)))
-        if t:
-            answer()
-        sbook(sb[0])
-        act("PB6o", "ov", B["ov"][:], PB6[:, 0:256], F.Relu, scale=-64.0, bias=128.0)
-        if t == 0:
-            answer()
-        for b in sb[1:]:
-            sbook(b)
-        eqact(0)
-        vbook(vbk[0])
-        bdiff(sb[0])
-        if t == 0:
-            late_consts()
-        mms("d4 Iq fe Id d4P BDq feP BD16", "PB6k",
-            [(PB6[:, 256:384], B["d4"][:], B["Iq"][:], True, False), (PB6[:, 256:384], B["fe"][:], B["Id"][:], False, True),
-             (PB6[:, 384:512], B["d4P"][:], B["BDq"][:], True, False), (PB6[:, 384:512], B["feP"][:], B["BD16"][:], False, True)])
-        for b in vbk[1:]:
-            vbook(b)
-        for b in sb[1:]:
-            bdiff(b)
-        tt("PB6k ov", "Kc", B["Kc"][:], PB6[:, 256:512], B["ov"][:], A.add)
-        tt("evf PB7", "evP", B["evP"][:], B["evf"][:], CPb, A.mult)
-        tt("PB7 evP", "AAb", B["AA"][:, 128:256], CP4, B["evP"][:], A.subtract)
-        tt("c128 e2", "BWa", B["BW"][:, 0:8], sm("c128"), vf, A.add)
+                more = (mm([(PB(h, 256 * (a % 2), 256), b("CG", p=c_(32 * a, 32)), b("CGm", p=c_(32 * a, 32)))], more=more),)
+            act(ch("EQ", h), PB(h), F.Relu, bias=-15.0)
+        key, TT, sK, Tp = PB(6, 0, 128), PB(6, 128, 128), PB(6, 256, 128), PB(4, 256, 128)
+        mm([(PB(6, 0, 384), one, b("KC")), (key, b("Cf"), IF), (PB(6, 0, 256), b("fe"), b("FE")), (TT, b("Zs"), Id)], stop=False)
+        mm([(TT, nId, b("ov", (0, 128)))], start=False, stop=False)
+        mm([(Tp, one, b("cT")), (Tp, b("ZP"), b("BDs")), (Tp, b("nIs"), b("ov", (128, 256)))], stop=False)
+        for c in range(4):
+            src = ind(bk, b("H16", c_(32 * c, 32)))
+            if c in TUNE["sb"]:
+                act(ch("BC", c), src, F.Copy)
+                mm([(PB(c), Id, ch("BC", c)), (PB(c), nId, ch("D", c))])
+                ts(b("IN", c), PB(c), 0.0, A.is_ge)
+            else:
+                tt(b("IN", c), src, ch("D", c), A.is_ge)
+        for j in range(2):
+            cp(b("WI", (0, 4), c_(16 * j, 16)), b("IN", (0, 4), (256 * j, 256 * j + 256, 17)))
+        mm([(Tp, b("WI"), b("BDs"))], start=False)
+        mm([(PB(6, k, 384 - k, 16), b("IN", (0, 4), (k, 512, 16)), b("RB")) for k in range(16)], start=False)
+        mm([(PB(5, 256, 128), Id, x), (PB(5, 256, 128), nId, yl)])
+        act(b("nx"), PB(5, 256, 128), F.Abs)
+        mm([(PB(5, 256, 8), b("nx"), b("W", (0, 8)))])
+        cp(b("b1"), PB(5, 256, 8))
+        ts(b("b2"), b("b1"), R - 1, A.bitwise_and)
+        tt(b("bv"), b("b2"), vl, A.subtract)
         if last:
-            c = 128 + wg
-            cp("E1", "EFb", B["EF"][:, c:c + L], B["E"][:, c:c + L])
-            cp("E E0", "EF", B["EF"][:, 128:c], B["E"][:, 128:c])
-            dma("Y", "EFb", "", "out0", T.ykids[:, c - 128:c - 128 + L], B["EF"][:, c:c + L])
-        count(0, 2)
-        for b in sb:
-            ts("PD%d" % b, "IN%d" % b, B["IN"][:, 2 * b:2 * b + 2, :], PD[b][:], 0.0, None, A.is_ge)
-        eqact(1)
-        act("Cf cb", "AAa", B["AA"][:, 0:128], B["Cf"][:], F.Identity, bias=sm("cb"))
-        count(2, 3)
-        cp("IN0 IN1 IN2 IN3", "WI", B["WI"][:], B["IN"][:, :, 0:256:17])
-        mms("WI BD", "PD2s", [(PD[2][:, 128:256], B["WI"][:], B["BD"][:], True, True)])
-        count(3, 4)
-        mms("fe I14 I14z", "PB5", [(KS[:, 0:256], B["fe"][:], B["I14"][:], False, True)])
-        tt("PD2s Kc", "wr", B["wr"][:], PD[2][:, 128:256], B["Kc"][:, 128:256], A.is_gt)
-        mms("nIh wr EQ0 EQ1", "PD0w", [(PD[0][:, 0:128], B["nIh"][:], B["wr"][:], True, False)]
-            + [(PD[0][:, 16 * k:16 * k + 16], B["EQ"][:, 128 * k:128 * k + 128], B["wr"][:, 16 * k:16 * k + 16], False, False) for k in range(8)]
-            + [(PD[0][:, 0:128], B["nIh"][:], B["wr"][:], False, True)])
-        sK = KS[:, 128:256]
-        tt("PB5 Kc", "cap", B["cap"][:], sK, B["Kc"][:, 0:128], A.is_gt)
-        tt("PB5 cap", "scap", B["scap"][:], sK, B["cap"][:], A.mult)
-        tt("PB5 Kc", "nc", B["nc"][:], sK, B["Kc"][:, 0:128], A.is_le)
-        op("V", "Mh scap", "scs", lambda: V.tensor_tensor_scan(B["scs"][:], B["Mh"][:], B["scap"][:], 0.0, A.mult, A.max))
-        for k in range(4):
-            ts("P scs", "sp", B["sp"][:, 16 * k:16 * k + 16], B["P"][:, 0:16], B["scs"][:, 16 * k + 15:16 * k + 16], None, A.mult)
-        tt("PB5 nc", "mk", B["mk"][:], KS[:, 0:128], B["nc"][:], A.mult)
-        tt("PD0w TPm", "wP", B["wP"][:], PD[0][:, 0:128], B["TPm"][:], A.is_lt)
-        op("V", "Mh mk", "sc", lambda: V.tensor_tensor_scan(B["sc"][:], B["Mh"][:], B["mk"][:], 0.0, A.mult, A.max))
-        for k in range(8):
-            ts("P sc", "zc", B["zc"][:, 16 * k:16 * k + 16], B["P"][:, 0:16], B["sc"][:, 16 * k + 15:16 * k + 16], None, A.mult)
-        tt("wr PB7", "wd", B["wd"][:], B["wr"][:], CP, A.mult)
-        mms("Id nId x yl%d" % t, "PB4d", [(U[:, 256:384], B["Id"][:], x, True, False), (U[:, 256:384], B["nId"][:], B["yl"][:, L * t:L * t + L], False, True)])
-        act("PB4d", "nx", nx, U[:, 256:384], F.Abs)
-        for k in range(4, 8):
-            act("P scs", "sp4", B["sp"][:, 16 * k:16 * k + 16], B["P"][:, 0:16], F.Copy, scale=B["scs"][:, 16 * k + 15:16 * k + 16])
-        act("PD0w", "wL", B["wL"][:], PD[0][:, 0:128], F.Relu, scale=-1.0)
-        mms("IF evP Pn P128 Id", "PB6v", [(PB6[:, 0:128], B["IF"][:, 0:128], B["evP"][:], True, False), (PB6[:, 0:128], B["IF"][:, 0:128], B["Pn"][:], False, False)]
-            + [(PB6[:, 0:128], B["Id"][:], B["P128"][:], False, False)] * t)
-        mms("cap Id", "PD3c", [(PD[3][:, 0:128], B["cap"][:], B["Id"][:], True, True)])
-        mms("sp sp4 I4", "PB6v", [(PB6[:, 0:128], B["sp"][:], B["I4"][:], False, True)])
-        mms("wP CH2", "PD2l", [(PD[2][:, 0:16], B["wP"][:], B["CH2"][:], True, True)])
-        mms("zc BDf", "PD2l", [(PD[2][:, 24:32], B["zc"][:], B["BDf"][:], True, True)])
-        mms("wd CH2", "PD2l", [(PD[2][:, 16:24], B["wd"][:], B["CH2"][:, 0:8], True, True)])
-        cp("PD2l", "ch1", sm("ch1"), PD[2][:, 24:32])
-        ts("ch1", "ch2", sm("ch2"), sm("ch1"), 2047, None, A.bitwise_and)
-        tt("e2 ch2", "ch3", sm("ch3"), vf, sm("ch2"), A.subtract)
-        tt("PD2l ch3", "ch4", sm("ch4"), PD[2][:, 16:24], sm("ch3"), A.mult)
-        tt("ch2 ch4", "BBb", B["BB"][:, 8:16], sm("ch2"), sm("ch4"), A.add)
-        tt("PD3c AAb", "mmb", B["mm"][:, 128:256], PD[3][:, 0:128], B["AA"][:, 128:256], A.mult)
-        tt("PB6v mmb", "VC", B["VC"][:], PB6[:, 0:128], B["mm"][:, 128:256], A.add)
-        mms("LW nx", "PD1b", [(PD[1][:, 128:136], B["LW"][:, 128 * r:128 * r + 128], B["XX"][:, r:128:16], r == 0, r == 15) for r in range(16)])
-        cp("PD1b", "bk1", sm("bk1"), PD[1][:, 128:136])
-        ts("bk1", "bk2", sm("bk2"), sm("bk1"), R - 1, None, A.bitwise_and)
-        tt("bk2 e2", "BWb", B["BW"][:, 8:16], sm("bk2"), vf, A.subtract)
-        mms("Id nx x one CA", "PB4a", [(U[:, 0:256], B["Id"][:], B["XX"][:], True, False), (U[:, 0:256], B["one"][:], B["CA"][:], False, False)])
-        mms("wL JJ", "PB4a", [(U[:, 0:256], B["wL"][:], B["JJ"][:], False, True)])
-        mms("x Id one CA wL JJ", "PD1x", [(PD[1][:, 0:128], B["Id"][:], x, True, False), (PD[1][:, 0:128], B["one"][:], B["CA"][:, 0:128], False, False),
-                                          (PD[1][:, 0:128], B["wL"][:], B["JJ"][:, 0:128], False, True)])
-        mms("cap scap wL Id I4", "PB5n", [(KS[:, 0:128], B["cap"][:], B["Id"][:], True, True), (KS[:, 128:256], B["scap"][:], B["I4"][:], True, True),
-                                          (KS[:, 256:384], B["wL"][:], B["Id"][:], True, True)])
-        act("PB4a", "xm", B["xm"][:], U[:, 0:256], F.Relu)
-        act("PD1x", "Xz X%d" % t, B["X"][:, M + L * t:M + L * t + L], PD[1][:, 0:128], F.Relu)
+            cp(b("EF", c_(128 + wg, L)), b("E", c_(128 + wg, L)))
+            cp(b("EF", c_(128, wg)), b("E", c_(128, wg)))
+            dma("Y", "out0", T.ykids[:, wg:wg + L], b("EF", c_(128 + wg, L)), 1.5)
+        ts(b("wr"), Tp, 0.0, A.is_gt, wcol, A.mult)
+        tt(b("wB"), PB(4, 256, 128, 16), b("vB"), A.min)
+        mm([(PB(0, 0, 128), b("n2Id"), b("wr"))] + [(PB(0, 16 * k, 16), b("EQ", c_(128 * k, 128)), b("wr", c_(16 * k, 16))) for k in range(8)])
+        ts(b("wL"), PB(0, 0, 128), 0.0, A.is_lt)
+        tt(pad("ZW"), b("wL", (0, 128, 4)), pj, A.mult)
+        tt(b("t1"), b("wL", (0, 128, 16)), b("bv"), A.mult)
+        ts(b("cap"), TT, 0.0, A.is_gt, BIG, A.mult)
+        tt(b("MK"), key, b("cap"), A.subtract)
+        tt(b("SK"), sK, b("cap"), A.min)
+        scan(b("sc"), b("Mh"), b("MK"), 0.0, A.mult, A.max)
+        scan(b("ss"), b("Mh"), b("SK"), 0.0, A.mult, A.max)
+        cp(b("ZS", (15, 143, 16)), b("ss", (15, 128, 16)))
+        tt(b("mt"), b("sc", (15, 128, 16)), b("wB"), A.max)
+        ts(b("hi"), b("mt"), MAGIC, A.add, -MAGIC, A.add)
+        tt(b("m1"), b("mt"), b("t1"), A.add)
+        tt(vl, b("m1"), b("hi"), A.subtract)
+        mm([(PB(1, 0, 8), Id, b("il"))] + tolist(PB(1, 0, 8), "ZW", "Mv"))
+        tt(b("of"), PB(1, 0, 8), b("vo"), A.min)
+        cp(o16, b("of"))
+        mm([(PB(5, 384, 8), b("ZL", c_(15 - k, 128)), b("I16", (k, 128, 16))) for k in range(16)])
+        cp(b("e2") if last else v16, PB(5, 384, 8))
         if not last:
-            mms("xm Id", "PB4y", [(U[:, 384:512], B["xm"][:, 0:128], B["Id"][:], True, False), (U[:, 384:512], B["xm"][:, 128:256], B["Id"][:], False, True)])
-            act("PB4y", "xT", B["xT"][:], U[:, 384:512], F.Copy)
-        else:
-            newx()
-        tt("PD2l BWa BWb", "e1", sm("e1"), PD[2][:, 0:16], B["BW"][:], A.mult)
-        tt("e1 BBa BBb", "e2", B["e2"][:], sm("e1"), B["BB"][:], A.add)
-        cp("e2", "lst", B["lst"][:], B["e2"][:])
+            ts(b("vo"), PB(5, 384, 8), 128.0, A.add)
+        mm([(PB(2, 0, 128), one, b("c1")), (PB(2, 0, 128), b("cap"), b("NC", (128, 256)))])
+        tt(b("mm"), PB(2, 0, 128), b("AA"), A.mult)
+        mm([(PB(3, 0, 128), Id, b("T1")), (PB(3, 0, 128), Id, b("T2"))] + [(PB(3, 0, 128), Id, b("P128"))] * t, stop=False)
+        mm([(PB(3, k, 128 - k, 16), b("ZS", c_(15 - k, 128)), b("I4", (k, 128, 16))) for k in range(16)], start=False)
+        tt(b("VC"), PB(3, 0, 128), b("mm"), A.subtract)
+        ek = "EF" if last else "E"
+        cp(ind(b(ek, (0, 128 + wg)), o16), b("VC"))
+        if last:
+            dma("Y", "out", T.ykids[:, 0:wg], b("EF", c_(128, wg)), 3.0)
+        new = b("X", c_(M + L * t, L))
+        for out, src, k, eng in ((b("YW"), yl, 4, TUNE["sel"][0]), (new, x, 0, TUNE["sel"][1])):
+            if eng == "S":
+                mm([(PB(k, 384, 128), Id, src), (PB(k, 384, 128), one, b("c256")), (PB(k, 384, 128), b("wL"), b("I256"))])
+                act(out, PB(k, 384, 128), F.Relu)
+            else:
+                mm([(PB(k, 384, 128), b("wL"), Id)])
+                tt(out, PB(k, 384, 128), src, A.mult)
         if not last:
-            nodes_at(t + 1)
-        if not last:
-            op("V", "lst VC", ER, lambda wg=wg: V.tensor_copy(B["E"][:, 0:128 + wg].indirect(B["lst"][:, 0:8]), B["VC"][:]))
-        else:
-            op("V", "lst VC EF", "EF", lambda: V.tensor_copy(B["EF"][:, 0:128 + wg].indirect(B["lst"][:, 0:8]), B["VC"][:]))
-            dma("Y", "EF", "", "out", T.ykids[:, 0:wg], B["EF"][:, 128:128 + wg])
-            newcols(t)
-            dma("Y", "EF%d" % t, "", "out", T.ykids[:, M + L * t:M + L * t + L], B["EF"][:, 128 + M + L * t:128 + M + L * t + L])
-            dma("S", XR + " X%d" % t, "", "out", T.ynodes[:], B["X"][:, M:M + L * STEPS])
-            dma("S", "x", "", "out", T.ycand[:], x)
-            dma("S", "e2", "", "out", T.yspot[:], vf)
+            mm([(PB(4, 0, 128), x, Id), (PB(4, 0, 128), b("YW"), nId)])
+            act(xT, PB(4, 0, 128), F.Abs)
+        mm([(PB(5, 0, 128), Id, x), (PB(5, 0, 128), nId, b("YW"))])
+        act(x, PB(5, 0, 128), F.Abs)
+        mm([(PB(6, 0, 256), one, b("cN")), (PB(6, 0, 128), IF, b("Cf")), (PB(6, 0, 128), b("SK"), b("I4")),
+            (PB(6, 0, 256), b("cap"), b("NC")), (PB(6, 0, 256), b("wL"), b("NW"))])
+        ts(b("Bq"), PB(6, 128, 128), 4095.0, A.mult, 4095.0, A.min)
+        tt(b(ek, c_(128 + M + L * t, L)), PB(6, 0, 128), b("Bq"), A.max)
+        if last:
+            dma("Y", "out", T.ykids[:, M + L * t:M + L * t + L], b("EF", c_(128 + M + L * t, L)), 1.5)
+            dma("S", "out", T.ynodes[:], b("X", c_(M, L * STEPS)), 1.5)
+            dma("S", "out", T.ycand[:], x, 1.5)
+            dma("S", "out", T.yspot[:], b("e2"), 1.5)
+
     def schedule():
         N = len(calls)
-        WAKE, LOOK = TUNE["wake"], TUNE["look"]
-        noise = np.random.RandomState(TUNE["seed"]).rand(N) * TUNE["noise"]
+        WAKE = TUNE["wake"]
         succ = [[] for _ in range(N)]
-        left = [len(c["pre"]) for c in calls]
         for c in calls:
-            for m in c["pre"]:
-                succ[m].append(c["n"])
-        prio = [0.0] * N
+            for m, w in c["pre"].items():
+                succ[m].append((c["n"], WAKE + calls[m]["lat"] if w else 0.0))
+        dur, eng = [c["dur"] for c in calls], [c["eng"] for c in calls]
+        rest = [0.0] * N
         for n in range(N - 1, -1, -1):
-            c = calls[n]
-            prio[n] = c["dur"] + c["lat"] + max([prio[m] + (WAKE if calls[m]["pre"][n] else 0.0) for m in succ[n]] or [0.0])
-        for n in range(N):
-            prio[n] += float(noise[n])
-        free, end, start, est = {}, [0.0] * N, [0.0] * N, {}
-        for n in range(N):
-            if not left[n]:
-                est[n] = 0.0
-        out = []
-        while est:
-            at = {n: max(e, free.get(calls[n]["eng"], 0.0)) for n, e in est.items()}
-            lo = min(at.values())
-            n = max((m for m in at if at[m] <= lo + LOOK), key=lambda m: (prio[m], -m))
-            c = calls[n]
-            start[n] = at[n]
-            if c["eng"] != "A":
-                free[c["eng"]] = at[n] + c["dur"]
-            end[n] = at[n] + c["dur"] + c["lat"]
-            del est[n]
-            out.append(n)
-            for m in succ[n]:
-                left[m] -= 1
-                if not left[m]:
-                    est[m] = max(end[q] + WAKE if w else start[q] + calls[q]["dur"] for q, w in calls[m]["pre"].items())
-        return out
+            rest[n] = dur[n] + max([rest[m] + d for m, d in succ[n]] or [calls[n]["lat"]])
+
+        def place(prio):
+            left = [len(c["pre"]) for c in calls]
+            est, at, used = [0.0] * N, [0.0] * N, {k: [] for k in eng}
+            ready = [n for n in range(N) if not left[n]]
+            while ready:
+                n = max(ready, key=lambda m: prio[m])
+                ready.remove(n)
+                t0, slots = est[n], used[eng[n]]
+                j = len(slots)
+                while j and slots[j - 1][1] > t0:
+                    j -= 1
+                while j < len(slots) and slots[j][0] < t0 + dur[n]:
+                    t0 = max(t0, slots[j][1])
+                    j += 1
+                if dur[n]:
+                    slots.insert(j, (t0, t0 + dur[n]))
+                at[n] = t0
+                for m, d in succ[n]:
+                    est[m] = max(est[m], t0 + dur[n] + d)
+                    left[m] -= 1
+                    if not left[m]:
+                        ready.append(m)
+            return max(at[n] + dur[n] + calls[n]["lat"] for n in range(N)), at
+
+        rng = np.random.RandomState(TUNE["seed"])
+        best, at = place(rest)
+        prio = rest
+        for _ in range(TUNE["tries"]):
+            new = list(prio)
+            for n in rng.randint(0, N, 12):
+                new[n] += TUNE["noise"] * float(rng.randn())
+            span, at2 = place(new)
+            if span <= best:
+                best, at, prio = span, at2, new
+        ORDERS["span"] = best
+        return sorted(range(N), key=lambda n: (at[n], n))
 
     if "order" not in ORDERS:
         ORDERS["order"] = schedule()
@@ -589,6 +526,6 @@ def rank_program(g, core, T, topo):
     for t in range(STEPS):
         for s in ("qo", "yo"):
             g.wait_ge(T.sem[s + str(t)], neng)
-    g.wait_ge(T.sem.wloc, neng * (NB - 1))
+    g.wait_ge(T.sem.wloc, neng)
     wait("G", [("sV", cnt["V"]), ("sS", cnt["S"]), ("sP", cnt["P"]), ("sG", cnt["G"])] + [("d_" + k, n) for k, n in dcount.items()]
          + [("wrem", neng * (NB - 1))] + [(k + str(t), neng) for k in ("qa", "ya") for t in range(STEPS)])

@@ -19,12 +19,13 @@ _S = {
     "Zs": (128, BF), "ZP": (128, BF), "XC": (2048, BF), "D": (2048, BF), "XV": (128, BF), "z": (128, BF),
     "uz": (64, I32), "uy": (64, I32), "hz": (64, I32), "ZH": (132, F32), "Ui": (256, I32), "U2": (256, I32), "h1": (128, I32), "h2": (128, I32),
     "H16": (128, U16), "BC": (2048, BF), "CG": (128, BF), "CGm": (256, BF), "EQ": (1024, BF), "WO": (128, BF), "ov": (256, BF),
-    "wr": (128, BF), "cap": (128, BF), "wL": (128, BF), "ZL": (144, F16), "ZS": (144, BF), "ZW": (132, BF), "b1": (8, I32), "b2": (8, I32),
+    "wr": (128, BF), "cap": (128, BF), "wL": (128, BF), "ZL": (144, F16), "ZS": (144, BF), "ZW": (132, BF), "b1": (32, I32), "b2": (32, I32),
+    "W1": (32, BF), "M16": (32, F16), "ZB": (132, F16),
     "MK": (128, F32), "SK": (128, BF), "sc": (128, F32), "ss": (128, BF), "Mh": (128, BF),
     "mm": (128, F32), "VC": (128, F32), "Bq": (128, F32), "YW": (128, BF),
 }
 _IN = {}
-for _buf, _w, _d, _names in (("KB", 128, BF, "nId n2Id BDs P Pb cT c1 T1 T2 P128 I4 I2k I256 c256 nIs"), ("KF", 8, F32, "BDf hi vB bv wB t1 mt m1 of vo")):
+for _buf, _w, _d, _names in (("KB", 128, BF, "nId n2Id BDs P Pb cT c1 T1 T2 P128 I4 I2k I256 c256 nIs"), ("KF", 8, F32, "BDf hi vB vn wB t1 mt m1 of vo")):
     for _j, _k in enumerate(_names.split()):
         _IN[_k] = (_buf, _w * _j, _w)
     _S[_buf] = (_w * len(_names.split()), _d)
@@ -34,7 +35,7 @@ for _k, _s, _d in (("OV", [8, 256], BF), ("IN", [4, 512], BF), ("WI", [4, 32], B
 for _k in range(8):
     SCRATCH["PB%d" % _k] = ("psum", [128, 512], F32)
 SIZE = {BF: 2, F16: 2, U16: 2, F32: 4, I32: 4}
-TUNE = {"wake": 0.15, "remote": 2.0, "load": 2.0, "tries": 3000, "noise": 0.3, "seed": 0, "xs": (1, 3), "sb": (), "sel": "SS"}
+TUNE = {"wake": 0.15, "remote": 2.5, "load": 2.0, "tries": 1500, "noise": 0.15, "seed": 0, "xs": (0, 2), "sb": (2,), "sel": "SS"}
 ORDERS = {}
 DMAS = ["spi", "E", "x", "X", "wt", "bk0", "bk1", "bk2", "out", "out0"]
 SEMAPHORES = (["sV", "sS", "sP", "sG", "wloc", "wrem"] + ["d_" + k for k in DMAS]
@@ -291,7 +292,11 @@ def rank_program(g, core, T, topo):
         mul("S", b("sv", c_(16 * c, 16)), b("P", (0, 16)), b("spf", c_(c, 1)))
     mm([(b("PB7", (0, 8)), b("sv"), b("BDf"))])
     vl = b("ZL", (15, 143, 16))
-    cp(vl, b("PB7", (0, 8)))
+    act(b("vn"), b("PB7", (0, 8)), F.Copy)
+    act(b("vB"), b("PB7", (0, 8)), F.Copy, bias=TOP)
+    ts(b("W1"), bd32, b("wt", (0, 1)), A.mult)
+    cp(b("M16"), b("Mvf"))
+    cp(b("ZB"), b("ZW"))
     ts(b("vo"), b("spi"), 128.0, A.add)
 
     def PB(k, a=0, n=512, s=1):
@@ -312,9 +317,8 @@ def rank_program(g, core, T, topo):
         yl = b("yl", c_(L * t, L))
         ts(b("Ci"), Ev, 4095, A.bitwise_and)
         ts(b("C16"), b("Ci"), 1280.0, A.min)
-        cp(b("XV"), ind(b("X", (0, wg)), v16))
-        mm([(PB(7, 384, 128), Id, b("XV")), (PB(7, 384, 128), nId, x)])
-        act(b("z"), PB(7, 384, 128), F.Abs)
+        tt(b("XV"), ind(b("X", (0, wg)), v16), x, A.subtract)
+        act(b("z"), b("XV"), F.Abs)
         mm([(PB(7, 384, 64), b("z"), b("Wz", c_(64 * t, 64)))])
         tt(b("uz"), PB(7, 384, 64), PJ, A.mult)
         ts(b("uy"), b("uz"), 4095, A.bitwise_and)
@@ -346,7 +350,6 @@ def rank_program(g, core, T, topo):
         mm([(PB(7, 256, 128), b("IFq"), b("A1")), (PB(7, 256, 128), b("IFq"), b("Cf")), (PB(7, 256, 128), b("I2k"), b("fe"))])
         act(b("Zs"), PB(7, 256, 128), F.Copy)
         tt(b("ZP"), PB(7, 256, 128), P, A.mult)
-        ts(b("vB"), vl, TOP, A.add)
         act(b("CG"), ind(b("CODE"), v16), F.Copy)
         for j, m in enumerate((m0, m1)):
             ts(b("CGm", c_(128 * j, 128)), b("CG"), m, A.mult)
@@ -395,10 +398,9 @@ def rank_program(g, core, T, topo):
         mm([(PB(6, k, 384 - k, 16), b("IN", (0, 4), (k, 512, 16)), b("RB")) for k in range(16)], start=False)
         mm([(PB(5, 256, 128), Id, x), (PB(5, 256, 128), nId, yl)])
         act(b("nx"), PB(5, 256, 128), F.Abs)
-        mm([(PB(5, 256, 8), b("nx"), b("W", (0, 8)))])
-        cp(b("b1"), PB(5, 256, 8))
+        mm([(PB(5, 256, 32), b("nx"), b("W1"))])
+        tt(b("b1"), PB(5, 256, 32), pj, A.mult)
         ts(b("b2"), b("b1"), R - 1, A.bitwise_and)
-        tt(b("bv"), b("b2"), vl, A.subtract)
         if last:
             cp(b("EF", c_(128 + wg, L)), b("E", c_(128 + wg, L)))
             cp(b("EF", c_(128, wg)), b("E", c_(128, wg)))
@@ -408,7 +410,8 @@ def rank_program(g, core, T, topo):
         mm([(PB(0, 0, 128), b("n2Id"), b("wr"))] + [(PB(0, 16 * k, 16), b("EQ", c_(128 * k, 128)), b("wr", c_(16 * k, 16))) for k in range(8)])
         ts(b("wL"), PB(0, 0, 128), 0.0, A.is_lt)
         tt(pad("ZW"), b("wL", (0, 128, 4)), pj, A.mult)
-        tt(b("t1"), b("wL", (0, 128, 16)), b("bv"), A.mult)
+        tt(pad("ZB"), b("wL", (0, 128, 4)), b("b2"), A.mult)
+        tt(b("t1"), b("wL", (0, 128, 16)), b("vn"), A.mult)
         ts(b("cap"), TT, 0.0, A.is_gt, BIG, A.mult)
         tt(b("MK"), key, b("cap"), A.subtract)
         tt(b("SK"), sK, b("cap"), A.min)
@@ -417,15 +420,19 @@ def rank_program(g, core, T, topo):
         cp(b("ZS", (15, 143, 16)), b("ss", (15, 128, 16)))
         tt(b("mt"), b("sc", (15, 128, 16)), b("wB"), A.max)
         ts(b("hi"), b("mt"), MAGIC, A.add, -MAGIC, A.add)
-        tt(b("m1"), b("mt"), b("t1"), A.add)
+        tt(b("m1"), b("mt"), b("t1"), A.subtract)
         tt(vl, b("m1"), b("hi"), A.subtract)
         mm([(PB(1, 0, 8), Id, b("il"))] + tolist(PB(1, 0, 8), "ZW", "Mv"))
         tt(b("of"), PB(1, 0, 8), b("vo"), A.min)
         cp(o16, b("of"))
-        mm([(PB(5, 384, 8), b("ZL", c_(15 - k, 128)), b("I16", (k, 128, 16))) for k in range(16)])
+        mm(tolist(PB(5, 384, 8), "ZB", "M16"), stop=False)
+        mm([(PB(5, 384, 8), b("ZL", c_(15 - k, 128)), b("I16", (k, 128, 16))) for k in range(16)], start=False)
         cp(b("e2") if last else v16, PB(5, 384, 8))
         if not last:
             ts(b("vo"), PB(5, 384, 8), 128.0, A.add)
+            mm([(PB(1, 8, 8), b("I16"), vl)] + [(PB(1, 8, 8), b("I16"), b("ZB", (3 + 4 * j, 131, 16))) for j in range(4)])
+            act(b("vn"), PB(1, 8, 8), F.Copy)
+            act(b("vB"), PB(1, 8, 8), F.Copy, bias=TOP)
         mm([(PB(2, 0, 128), one, b("c1")), (PB(2, 0, 128), b("cap"), b("NC", (128, 256)))])
         tt(b("mm"), PB(2, 0, 128), b("AA"), A.mult)
         mm([(PB(3, 0, 128), Id, b("T1")), (PB(3, 0, 128), Id, b("T2"))] + [(PB(3, 0, 128), Id, b("P128"))] * t, stop=False)
@@ -470,9 +477,16 @@ def rank_program(g, core, T, topo):
         for n in range(N - 1, -1, -1):
             rest[n] = dur[n] + max([rest[m] + d for m, d in succ[n]] or [calls[n]["lat"]])
 
-        def place(prio):
-            left = [len(c["pre"]) for c in calls]
-            est, at, used = [0.0] * N, [0.0] * N, {k: [] for k in eng}
+        pred = [[] for _ in range(N)]
+        for n in range(N):
+            for m, d in succ[n]:
+                pred[m].append((n, d))
+        tail = [c["lat"] for c in calls]
+
+        def place(prio, back=False):
+            nxt, prv = (pred, succ) if back else (succ, pred)
+            left = [len(p) for p in prv]
+            est, at, used = list(tail) if back else [0.0] * N, [0.0] * N, {k: [] for k in eng}
             ready = [n for n in range(N) if not left[n]]
             while ready:
                 n = max(ready, key=lambda m: prio[m])
@@ -487,21 +501,23 @@ def rank_program(g, core, T, topo):
                 if dur[n]:
                     slots.insert(j, (t0, t0 + dur[n]))
                 at[n] = t0
-                for m, d in succ[n]:
+                for m, d in nxt[n]:
                     est[m] = max(est[m], t0 + dur[n] + d)
                     left[m] -= 1
                     if not left[m]:
                         ready.append(m)
-            return max(at[n] + dur[n] + calls[n]["lat"] for n in range(N)), at
+            return max(at[n] + dur[n] + tail[n] for n in range(N)), at
+
+        def sweep(prio):
+            at = place(prio)[1]
+            at = place([at[n] + dur[n] for n in range(N)], True)[1]
+            prio = [at[n] + dur[n] for n in range(N)]
+            return place(prio) + (prio,)
 
         rng = np.random.RandomState(TUNE["seed"])
-        best, at = place(rest)
-        prio = rest
+        best, at, prio = sweep(rest)
         for _ in range(TUNE["tries"]):
-            new = list(prio)
-            for n in rng.randint(0, N, 12):
-                new[n] += TUNE["noise"] * float(rng.randn())
-            span, at2 = place(new)
+            span, at2, new = sweep([p + TUNE["noise"] * r for p, r in zip(prio, rng.randn(N).tolist())])
             if span <= best:
                 best, at, prio = span, at2, new
         ORDERS["span"] = best

@@ -9,33 +9,37 @@ BIG, TOP, MAGIC = 2.0 ** 22, 2.0 ** 21, 1.5 * 2.0 ** 35
 _S = {
     "spi": (8, I32), "E": (128 + 1280, I32), "EF": (128 + 1280, F32), "X": (XW, BF), "bk": (3 * H, BF), "x": (L, BF), "xT": (L, BF), "nx": (L, BF),
     "wt": (2, BF), "wl": (24, BF), "qs": (8 * STEPS, U16), "ql": (8 * STEPS, U16), "ys": (L * STEPS, BF), "yl": (L * STEPS, BF),
-    "one": (128, BF), "pk": (128, I32), "pa": (128, I32), "Id": (128, BF), "nId": (128, BF), "n2Id": (128, BF), "IF": (128, F32), "IFq": (128, F32),
-    "BD0": (128, BF), "BD": (128, BF), "BDs": (128, BF), "BDf": (32, F32), "P": (128, BF), "Pb": (128, BF), "PJ": (64, BF), "Q4": (32, BF),
-    "Mv": (32, BF), "I16": (128, F16), "il": (8, BF), "Mvf": (32, F32), "rt": (128, F32), "TR": (128, F32), "zer": (128, F32), "wsc": (128, F32), "sg": (16, F32), "CODE": (1024, BF),
-    "col": (16, F32), "KC": (384, BF), "cT": (128, BF), "c1": (128, BF), "cN": (256, BF), "T1": (128, BF), "T2": (128, BF), "P128": (128, BF), "ni": (128, BF),
-    "I4": (128, BF), "I2k": (128, BF), "I256": (128, BF), "c256": (128, BF), "nIs": (128, BF), "FE": (256, BF), "NC": (256, BF), "NW": (256, BF),
-    "RB": (24, BF), "W": (16, BF), "Wz": (192, BF), "spf": (8, F32), "sv": (128, F32),
+    "one": (128, BF), "pk": (128, I32), "pa": (128, I32), "Id": (128, BF), "IF": (128, F32), "IFq": (128, F32),
+    "BD0": (128, BF), "BD": (128, BF), "BDf": (40, F32), "PJ": (64, BF), "Q4": (32, BF),
+    "I16": (128, F16), "il": (8, F16), "cO": (40, BF), "oP": (32, F32), "rt": (128, F32), "TR": (128, F32), "zer": (128, F32), "wsc": (128, F32), "sg": (16, F32), "CODE": (1024, BF),
+    "col": (16, F32), "KC": (384, BF), "cN": (256, BF), "ni": (128, BF),
+    "RB": (24, BF), "W": (64, BF), "ZU": (132, F16), "zb": (288, BF), "Wz": (192, BF), "spf": (8, F32), "sv": (128, F32),
     "lst": (16, U16), "e2": (8, F32), "Ci": (128, I32), "C16": (128, U16), "A1": (128, F32), "Cf": (128, F32), "fe": (128, BF), "AA": (128, F32),
     "Zs": (128, BF), "ZP": (128, BF), "XC": (2048, BF), "D": (2048, BF), "XV": (128, BF), "z": (128, BF),
-    "uz": (64, I32), "uy": (64, I32), "hz": (64, I32), "ZH": (132, F32), "Ui": (256, I32), "U2": (256, I32), "h1": (128, I32), "h2": (128, I32),
+    "uz": (64, I32), "uy": (64, I32), "hz": (64, I32), "ZH": (132, F16), "Ui": (256, I32), "U2": (256, I32), "h1": (128, I32), "h2": (128, I32),
     "H16": (128, U16), "BC": (2048, BF), "CG": (128, BF), "CGm": (256, BF), "EQ": (1024, BF), "WO": (128, BF), "ov": (256, BF),
-    "wr": (128, BF), "cap": (128, BF), "wL": (128, BF), "ZL": (144, F16), "ZS": (144, BF), "ZW": (132, BF), "b1": (32, I32), "b2": (32, I32),
-    "W1": (32, BF), "M16": (32, F16), "ZB": (132, F16),
+    "wr": (128, BF), "cap": (128, BF), "wL": (128, BF), "ZL": (144, F16), "ZS": (144, BF), "ZO": (132, F16), "b1": (32, I32), "b2": (32, I32),
+    "M16": (32, F16), "ZB": (132, F16),
     "MK": (128, F32), "SK": (128, BF), "sc": (128, F32), "ss": (128, BF), "Mh": (128, BF),
     "mm": (128, F32), "VC": (128, F32), "Bq": (128, F32), "YW": (128, BF),
 }
 _IN = {}
-for _buf, _w, _d, _names in (("KB", 128, BF, "nId n2Id BDs P Pb cT c1 T1 T2 P128 I4 I2k I256 c256 nIs"), ("KF", 8, F32, "BDf hi vB vn wB t1 mt m1 of vo")):
+for _buf, _w, _d, _names in (("KB", 128, BF, "nId BDs P cT c1 T1 T2 P128 I4 IB nIr c4 nIs"), ("KF", 8, F32, "hi vB vn wB t1 mt m1")):
     for _j, _k in enumerate(_names.split()):
         _IN[_k] = (_buf, _w * _j, _w)
     _S[_buf] = (_w * len(_names.split()), _d)
 SCRATCH = {k: ("sbuf", [128, w], d) for k, (w, d) in _S.items() if k not in _IN}
-for _k, _s, _d in (("OV", [8, 256], BF), ("IN", [4, 512], BF), ("WI", [4, 32], BF), ("Ex", [128, 16], BF), ("HB0", [18, 8], F32), ("HB1", [18, 8], F32)):
+TUNE = {"wake": 0.15, "remote": 2.3, "load": 2.0, "tries": 5000, "noise": 0.2, "seed": 0, "reach": 4.0, "f": 1.15, "xs": (0, 2), "sb": (2,), "sel": "SS", "xv": "S",
+        "cnt": ((0, 4),), "war": True, "parts": ((0, 2), (2, 2)), "wo": "G", "cf": "G", "ef": "G", "zs": "S", "fe": "S", "vb": "S"}
+for _k, _s, _d in (("OV", [8, 256], BF), ("IN", [4, 512], BF), ("WI", [4, 32], BF), ("Ex", [128, 16], BF)):
     SCRATCH[_k] = ("sbuf", [128] + _s, _d)
+for _k, (_c, _n) in enumerate(TUNE["parts"]):
+    SCRATCH["HB%d" % _k] = ("sbuf", [128, 72 // _n, 4 * _n], F16)
 for _k in range(8):
     SCRATCH["PB%d" % _k] = ("psum", [128, 512], F32)
 SIZE = {BF: 2, F16: 2, U16: 2, F32: 4, I32: 4}
-TUNE = {"wake": 0.15, "remote": 2.5, "load": 2.0, "tries": 1500, "noise": 0.15, "seed": 0, "xs": (0, 2), "sb": (2,), "sel": "SS"}
+CASES = ((1.0, 1.56, 3.8, 0.15, 1.0, 1.0), (1.25, 1.15, 2.5, 0.1, 0.8, 1.2), (1.2, 1.95, 5.0, 0.2, 1.2, 0.85), (1.45, 1.56, 3.0, 0.13, 1.1, 1.1),
+         (1.1, 1.3, 4.5, 0.22, 0.9, 1.3))
 ORDERS = {}
 DMAS = ["spi", "E", "x", "X", "wt", "bk0", "bk1", "bk2", "out", "out0"]
 SEMAPHORES = (["sV", "sS", "sP", "sG", "wloc", "wrem"] + ["d_" + k for k in DMAS]
@@ -99,7 +103,8 @@ def rank_program(g, core, T, topo):
             for k, mask in regs:
                 for m, mk, mw in touched.get(k, ()):
                     if mk & mask and (w or mw):
-                        pre[m] = pre.get(m, False) or not (w and eng == "P" and calls[m]["eng"] == "P")
+                        own = w and eng == calls[m]["eng"] and kind == calls[m]["kind"] == "c" and (eng == "P" or not TUNE["war"])
+                        pre[m] = pre.get(m, False) or not own
         for k, mask in ws:
             touched[k] = [(m, mk & ~mask, mw) for m, mk, mw in touched.get(k, ()) if mk & ~mask] + [(n, mask, True)]
         for k, mask in rs:
@@ -114,20 +119,25 @@ def rank_program(g, core, T, topo):
                 for m in cur[1][-1:]:
                     pre[m] = pre.get(m, False)
             cur[1].append(n)
-        calls.append({"eng": eng, "pre": pre, "fn": fn, "kind": kind, "lat": lat, "tok": tok, "n": n, "dur": dur})
+        calls.append({"eng": eng, "pre": pre, "fn": fn, "kind": kind, "lat": lat, "tok": tok, "n": n, "cost": dur, "to": (ws or rs)[0][0]})
         return n
 
     def cost(eng, out, ins, two=False):
         vs = [out] + ins
         n = ins[0][2] if ins else out[2]
         if out[4]:
-            return 0.05 + 3.8 * n * CYC
+            return (0.05, n * CYC, "scatter")
         if any(v[4] for v in ins):
-            return 0.06 + 1.56 * n * CYC
+            return (0.06, n * CYC, "gather2" if two else "gather")
         if eng == "S":
             return 0.06 + max(64, n) * CYC
         r = (1.0 if any(psum(v) for v in ins) else 2.0) if two else 0.5 if all(SIZE[v[3]] == 2 for v in vs) else 1.0
         return max(64, n * r) * CYC
+
+    def length(c, k):
+        if isinstance(c, float):
+            return c * k[0]
+        return (c[0] + c[1] * {"scatter": k[2], "gather": k[1], "gather2": max(2.0, k[1])}[c[2]]) * k[0]
 
     dcount, loads = {}, {}
 
@@ -168,11 +178,11 @@ def rank_program(g, core, T, topo):
     def act(out, x0, f, bias=0.0, scale=1.0):
         note("S", [x0, bias, scale], [out], lambda: S.activation(out[0], x0[0], f, bias=a_(bias), scale=a_(scale)), cost("S", out, [x0]))
 
-    def mul(eng, out, x0, c):
+    def mul(eng, out, x0, c, add=0.0):
         if eng == "S":
-            act(out, x0, F.Copy, scale=c)
+            act(out, x0, F.Copy, scale=c, bias=add)
         else:
-            ts(out, x0, c, A.mult)
+            ts(out, x0, c, A.mult, add, A.add)
 
     def mm(lst, start=True, stop=True, apart=False, more=()):
         def go():
@@ -188,6 +198,12 @@ def rank_program(g, core, T, topo):
 
     def gp(out, ins, fn):
         note("G", ins, [out], fn, 0.15 + 2 * out[2] * CYC)
+
+    def copy(eng, out, x0):
+        if eng == "G":
+            gp(out, [x0], lambda: g.affine_select(out[0], x0[0], [[0, out[2]]], A.is_ge, 0.0, 0, 0))
+        else:
+            cp(out, x0)
 
     def c_(a, n):
         return (a, a + n)
@@ -232,24 +248,26 @@ def rank_program(g, core, T, topo):
     wcol = b("wsc", (127, 128))
 
     fill(b("X", (M, XW)), 0.0)
-    for k in ("ZS", "ZW", "ZH", "HB0", "HB1"):
+    for k in ("ZS", "zb"):
         fill(b(k), 0.0)
-    cp(b("ZL"), b("ZS"))
+    PARTS = TUNE["parts"]
+    for k in ["ZL", "ZH", "ZU", "ZB", "ZO"] + ["HB%d" % h for h in range(len(PARTS))]:
+        cp(b(k), b("zb", (0, b(k)[2])))
     fill(b("Mh"), 1.0)
     fill(b("Mh", (0, 128, 16)), 0.0)
-    fill(b("KC", (128, 256)), -0.5 / 128)
+    fill(b("KC", (128, 256)), -1.5 / 128)
     fill(b("KC", (256, 384)), 0.0)
-    fill(b("cT"), -BIG / 128)
+    fill(b("cT"), -3 * BIG / 128)
     fill(b("c1"), 1.0 / 128)
-    fill(b("c256"), -2.0)
-    fill(b("cN", (0, 128)), (4096.0 - 2.0 ** 19) / 128)
-    fill(b("cN", (128, 256)), 2.0 / 128)
+    fill(b("c4"), -4096.0 / 128)
+    fill(b("cN", (0, 128)), -2 * BIG / 128)
+    fill(b("cN", (128, 256)), 0.0)
     cp(b("Ex", (0, 128), (0, 1)), Id)
     for n in (1, 2, 4, 8):
         cp(b("Ex", (0, 128), c_(n, n)), b("Ex", (0, 128), (0, n)))
     mul("V", nId, Id, -1.0)
-    mm([(b("PB7", (384, 512)), x, Id)])
-    act(xT, b("PB7", (384, 512)), F.Copy)
+    mm([(b("PB4", (384, 512)), x, Id)])
+    act(xT, b("PB4", (384, 512)), F.Copy)
     ts(b("pa"), b("pk"), 15, A.bitwise_and)
     ts(P, b("pa"), 0, A.is_equal)
     ts(b("uz", (0, 32)), b("pk", (0, 128, 4)), 12, A.bitwise_and)
@@ -257,21 +275,22 @@ def rank_program(g, core, T, topo):
         ts(b("PJ", c_(32 * j, 32)), b("uz", (0, 32)), 0, A.is_equal)
     ts(b("uz", (32, 64)), b("pk", (0, 32)), 3, A.bitwise_and)
     ts(b("Q4"), b("uz", (32, 64)), 0, A.is_equal)
-    tt(b("Mvf"), bd32, b("Q4"), A.mult)
-    ts(b("Pb"), P, -1.0, A.mult, 1.0, A.add)
-    kcol, slot, m0, m1 = (b("col", c_(j, 1)) for j in (0, 2, 6, 8))
-    ts(kcol, b("pa", (0, 1)), -512.0, A.mult, 8192.0, A.add)
+    tt(b("M16"), bd32, b("Q4"), A.mult)
+    ts(b("PB7", (384, 512)), P, -1.0, A.mult, 1.0, A.add)
+    kcol, slot, lane, m0, m1, n0, n1 = (b("col", c_(j, 1)) for j in (0, 2, 4, 6, 8, 10, 12))
+    ts(kcol, b("pa", (0, 1)), -512.0, A.mult, 7680.0, A.add)
     ts(slot, b("pa", (0, 1)), -1.0, A.add)
+    ts(lane, b("pk", (0, 1)), -1.0, A.mult, 144.0, A.add)
     ts(b("il"), b("ni", (0, 128, 16)), slot, A.add)
-    for j, m in enumerate((m0, m1)):
-        note("V", [BD], [m], lambda j=j, m=m: V.tensor_reduce(m[0], T.BD[:, 16 * j:128:32], AX.X, A.add), 64 * CYC)
+    fill(b("cO", (0, 8)), 0.0)
+    ts(b("cO", (8, 40)), b("one", (0, 32)), lane, A.mult)
+    for m, src in ((m0, b("BD", (0, 128, 32))), (m1, b("BD", (16, 128, 32))), (n0, b("P", (0, 8))), (n1, b("P", (8, 16)))):
+        note("V", [src], [m], lambda m=m, src=src: V.tensor_reduce(m[0], src[0], AX.X, A.add), 64 * CYC)
     for eng, out, src, f in (("S", IF, Id, 1.0), ("S", b("IFq"), Id, 1.0 / 4096), ("S", b("KC", (0, 128)), P, kcol), ("S", b("BDs"), BD, 2 * BIG),
-                             ("V", b("n2Id"), Id, -2.0), ("V", b("I4"), Id, 4096.0), ("V", b("I2k"), Id, 2048.0), ("V", b("I256"), Id, 256.0),
-                             ("V", b("nIs"), Id, -2 * BIG), ("V", b("FE", (0, 128)), Id, -TOP), ("V", b("FE", (128, 256)), Id, -4096.0),
-                             ("V", b("NC", (0, 128)), Id, 2.0 ** 18 / BIG), ("V", b("NC", (128, 256)), Id, -1.0 / BIG),
-                             ("V", b("NW", (0, 128)), Id, 2.0 ** 18), ("V", b("NW", (128, 256)), Id, -1.0), ("V", b("P128"), P, 128.0),
-                             ("S", b("BDf"), bd8, 1.0), ("V", b("I16"), Id, 1.0), ("V", b("Mv"), b("Mvf"), 4096.0), ("V", b("RB", (0, 8)), bd8, 65536.0), ("V", b("RB", (8, 16)), bd8, 1.0),
-                             ("V", b("RB", (16, 24)), bd8, 1.0)):
+                             ("V", b("I4"), Id, 4096.0), ("V", b("nIs"), Id, -2 * BIG), ("V", b("IB"), Id, BIG), ("V", b("nIr"), Id, -1.0 / BIG),
+                             ("V", b("P128"), P, 128.0),
+                             ("S", b("BDf", (0, 8)), bd8, 1.0), ("S", b("BDf", (8, 40)), bd32, 1.0), ("V", b("I16"), Id, 1.0),
+                             ("V", b("RB", (0, 8)), bd8, 65536.0), ("V", b("RB", (8, 16)), bd8, 1.0), ("V", b("RB", (16, 24)), bd8, 1.0)):
         mul(eng, out, src, f)
     ts(b("T1"), P, M - 4096.0, A.mult, 4096.0, A.add)
     tt(b("YW"), P, b("ni"), A.mult)
@@ -281,7 +300,7 @@ def rank_program(g, core, T, topo):
     for j in range(10):
         ts(b("CODE", c_(2 ** j, 2 ** j)), b("CODE", (0, 2 ** j)), b("sg", c_(j, 1)), A.mult)
     for u in range(2):
-        ts(b("W", c_(8 * u, 8)), bd8, b("wt", c_(u, 1)), A.mult)
+        ts(b("W", c_(32 * u, 32)), bd32, b("wt", c_(u, 1)), A.mult)
     for j in range(3):
         for u in range(2):
             ts(b("Wz", c_(64 * j + 32 * u, 32)), bd32, b("wl", c_(8 * j + u, 1)), A.mult)
@@ -290,17 +309,17 @@ def rank_program(g, core, T, topo):
     cp(b("spf"), b("spi"))
     for c in range(8):
         mul("S", b("sv", c_(16 * c, 16)), b("P", (0, 16)), b("spf", c_(c, 1)))
-    mm([(b("PB7", (0, 8)), b("sv"), b("BDf"))])
-    vl = b("ZL", (15, 143, 16))
-    act(b("vn"), b("PB7", (0, 8)), F.Copy)
-    act(b("vB"), b("PB7", (0, 8)), F.Copy, bias=TOP)
-    ts(b("W1"), bd32, b("wt", (0, 1)), A.mult)
-    cp(b("M16"), b("Mvf"))
-    cp(b("ZB"), b("ZW"))
-    ts(b("vo"), b("spi"), 128.0, A.add)
 
     def PB(k, a=0, n=512, s=1):
         return b("PB%d" % k, (a, a + n, s))
+
+    def nodes():
+        tt(b("oP"), PB(7, 16, 32), pj, A.mult)
+        cp(b("vn"), PB(7, 8, 8))
+        mul(TUNE["vb"], b("vB"), b("vn"), 1.0, TOP)
+    mm([(PB(7, 8, 40), Id, b("cO")), (PB(7, 8, 40), b("sv"), b("BDf"))])
+    vl = b("ZL", (15, 143, 16))
+    nodes()
 
     def ch(k, c):
         return b(k, c_(512 * c, 512))
@@ -308,30 +327,40 @@ def rank_program(g, core, T, topo):
     def ch3(k, c):
         return b(k, c_(2 * c, 2))
 
+    def halves(t, h1, h2, u1, u2, tmp, f, u):
+        tt(h1, u1, u2, A.mult)
+        ts(h2, h1, 5, A.logical_shift_right, H - 1, A.bitwise_and)
+        cp(f, h2)
+        if t:
+            ts(u, u2, -float(H), A.add)
+            return float(H)
+        ts(tmp, u2, H - 1, A.bitwise_and)
+        cp(u, tmp)
+        return 0.0
+
     for t in range(STEPS):
         last = t == STEPS - 1
         wg = M + L * max(0, t - 1)
         asked, asker = T.cores[(rank + 1 + t) % NB], T.cores[(rank - 1 - t) % NB]
         Ev = ind(b("E", c_(128, wg)), v16)
-        bk = b("bk") if t else b("bk", (0, H))
+        bk = b("bk") if t else b("bk", (0, 2 * H))
         yl = b("yl", c_(L * t, L))
         ts(b("Ci"), Ev, 4095, A.bitwise_and)
         ts(b("C16"), b("Ci"), 1280.0, A.min)
-        tt(b("XV"), ind(b("X", (0, wg)), v16), x, A.subtract)
-        act(b("z"), b("XV"), F.Abs)
-        mm([(PB(7, 384, 64), b("z"), b("Wz", c_(64 * t, 64)))])
-        tt(b("uz"), PB(7, 384, 64), PJ, A.mult)
-        ts(b("uy"), b("uz"), 4095, A.bitwise_and)
-        tt(b("hz", (0, 32)), b("uy", (0, 32)), b("uy", (32, 64)), A.mult)
-        ts(b("hz", (32, 64)), b("hz", (0, 32)), 5, A.logical_shift_right, H - 1, A.bitwise_and)
-        if t:
-            tt(pad("ZH"), b("hz", (32, 64)), b("uy", (32, 64)), A.add)
+        if TUNE["xv"] == "V":
+            tt(b("XV"), ind(b("X", (0, wg)), v16), x, A.subtract)
+            act(b("z"), b("XV"), F.Abs)
         else:
-            tt(b("hz", (0, 32)), b("hz", (32, 64)), b("uy", (32, 64)), A.add)
-            ts(b("hz", (32, 64)), b("hz", (0, 32)), H - 1, A.bitwise_and)
-            cp(pad("ZH"), b("hz", (32, 64)))
-        mm(tolist(PB(7, 448, 8), "ZH", "Mvf"))
-        cp(b("qs", c_(8 * t, 8)), PB(7, 448, 8))
+            act(b("XV"), ind(b("X", (0, wg)), v16), F.Copy)
+            mm([(PB(7, 128, 128), nId, x), (PB(7, 128, 128), Id, b("XV"))])
+            act(b("z"), PB(7, 128, 128), F.Abs)
+        mm([(PB(7, 64, 64), b("z"), b("Wz", c_(64 * t, 64)))])
+        tt(b("uz"), PB(7, 64, 64), PJ, A.mult)
+        ts(b("uy"), b("uz"), 4095, A.bitwise_and)
+        off = halves(t, b("hz", (0, 32)), b("hz", (32, 64)), b("uy", (0, 32)), b("uy", (32, 64)), b("uz", (0, 32)), pad("ZH"), pad("ZU"))
+        mm(tolist(PB(7, 128, 8), "ZU", "M16"), stop=False)
+        mm(tolist(PB(7, 128, 8), "ZH", "M16"), start=False)
+        ts(b("qs", c_(8 * t, 8)), PB(7, 128, 8), 4 * off, A.add)
         send(b("ql", c_(8 * t, 8)), b("qs", c_(8 * t, 8)), asked, asker, "qa%d" % t, "qo%d" % t)
         for c in range(4):
             mm([(PB(c), xT, b("Ex", c_(32 * c, 32)))], stop=False)
@@ -344,44 +373,44 @@ def rank_program(g, core, T, topo):
             act(ch("D", c), PB(c), F.Abs)
             act(ch3("OV", c), PB(c), F.Sign, bias=0.5)
         ts(b("A1"), Ev, -1.0, A.mult, 4095.0, A.add)
-        ts(b("Cf"), b("Ci"), -4096.0, A.add)
-        act(b("fe"), b("Cf"), F.Relu, bias=2.0)
-        tt(b("AA"), b("A1"), b("Pb"), A.mult)
-        mm([(PB(7, 256, 128), b("IFq"), b("A1")), (PB(7, 256, 128), b("IFq"), b("Cf")), (PB(7, 256, 128), b("I2k"), b("fe"))])
-        act(b("Zs"), PB(7, 256, 128), F.Copy)
+        copy(TUNE["cf"], b("Cf"), b("Ci"))
+        if TUNE["fe"] == "S":
+            act(b("fe"), b("Cf"), F.Relu, bias=-4094.0)
+        else:
+            ts(b("fe"), b("Ci"), 4095.0, A.is_ge)
+        mm([(PB(7, 256, 128), b("IFq"), b("A1")), (PB(7, 256, 128), b("IFq"), b("Cf")), (PB(7, 256, 128), b("I4"), b("fe"))])
+        if TUNE["zs"] == "S":
+            act(b("Zs"), PB(7, 256, 128), F.Copy)
         tt(b("ZP"), PB(7, 256, 128), P, A.mult)
+        tt(b("AA"), PB(7, 384, 128), b("A1"), A.mult)
         act(b("CG"), ind(b("CODE"), v16), F.Copy)
         for j, m in enumerate((m0, m1)):
             ts(b("CGm", c_(128 * j, 128)), b("CG"), m, A.mult)
-        for h in range(2):
-            u, hb = 4 + h, "HB%d" % h
-            mm([(PB(u, k, 128 - k, 8), b("D", (1024 * h + k, 1024 * h + 1024, 8)), b("W")) for k in range(8)], apart=True)
-            u1, u2, h1, h2 = b("U2", c_(128 * h, 64)), b("U2", c_(128 * h + 64, 64)), b("h1", c_(64 * h, 64)), b("h2", c_(64 * h, 64))
-            cp(b("Ui", c_(128 * h, 128)), PB(u, 0, 128))
-            ts(b("U2", c_(128 * h, 128)), b("Ui", c_(128 * h, 128)), 4095, A.bitwise_and)
-            tt(h1, u1, u2, A.mult)
-            ts(h2, h1, 5, A.logical_shift_right, H - 1, A.bitwise_and)
-            if t:
-                tt(b(hb, (1, 17, 2)), h2, u2, A.add)
-            else:
-                tt(h1, h2, u2, A.add)
-                ts(h2, h1, H - 1, A.bitwise_and)
-                cp(b(hb, (1, 17, 2)), h2)
-            mm([(PB(u, 128, 64), b(hb, c_(1 - kk, 16)), b("IF", (kk, 128, 2))) for kk in range(2)])
-            cp(b("H16", c_(64 * h, 64)), PB(u, 128, 64))
+        for h, (c, n) in enumerate(PARTS):
+            u, hb, w, r = 4 + h % 2, "HB%d" % h, 32 * n, 4 // n
+            h1, h2 = b("h1", c_(32 * c, w)), b("h2", c_(32 * c, w))
+            mm([(PB(u, k, 2 * w - k, 16 // r), b("D", (512 * c + k, 512 * (c + n), 16 // r)), b("W", (0, 64, 4))) for k in range(16 // r)], apart=True)
+            u1, u2 = b("U2", c_(64 * c, w)), b("U2", c_(64 * c + w, w))
+            cp(b("Ui", c_(64 * c, 2 * w)), PB(u, 0, 2 * w))
+            ts(b("U2", c_(64 * c, 2 * w)), b("Ui", c_(64 * c, 2 * w)), 4095, A.bitwise_and)
+            off = halves(t, h1, h2, u1, u2, b("Ui", c_(64 * c, w)), b(hb, (r - 1, 9 * r - 1, r)), b(hb, (10 * r - 1, 18 * r - 1, r)))
+            for j in range(2):
+                mm([(PB(u, 128, w), b(hb, c_(9 * r * (1 - j) + r - 1 - kk, 8 * r)), b("I16", (kk, 128, r))) for kk in range(r)], start=j == 0, stop=j == 1)
+            ts(b("H16", c_(32 * c, w)), PB(u, 128, w), off, A.add)
         act(b("ys", c_(L * t, L)), ind(bk, b("ql", c_(8 * t, 8))), F.Copy)
         send(yl, b("ys", c_(L * t, L)), asker, asked, "ya%d" % t, "yo%d" % t)
         mm([(PB(7, k, 128 - k, 16), b("OV", (0, 8), (k, 256, 16)), bd8) for k in range(16)], apart=True)
-        cp(b("WO"), b("OV", (0, 8), (0, 256, 17)))
+        copy(TUNE["wo"], b("WO"), b("OV", (0, 8), (0, 256, 17)))
         mm([(PB(7, 128, 128), b("WO"), BD)])
         act(b("ov"), PB(7, 0, 256), F.Relu, scale=-64.0, bias=128.0)
         for h in range(2):
             more = ()
             for a in (2 * h, 2 * h + 1):
                 more = (mm([(PB(h, 256 * (a % 2), 256), b("CG", p=c_(32 * a, 32)), b("CGm", p=c_(32 * a, 32)))], more=more),)
-            act(ch("EQ", h), PB(h), F.Relu, bias=-15.0)
+            act(ch("EQ", h), PB(h), F.Relu, scale=0.5, bias=-7.5)
         key, TT, sK, Tp = PB(6, 0, 128), PB(6, 128, 128), PB(6, 256, 128), PB(4, 256, 128)
-        mm([(PB(6, 0, 384), one, b("KC")), (key, b("Cf"), IF), (PB(6, 0, 256), b("fe"), b("FE")), (TT, b("Zs"), Id)], stop=False)
+        mm([(PB(6, 0, 384), one, b("KC")), (key, b("Cf"), IF), (key, b("fe"), b("nIs")), (TT, b("fe"), b("nIs"))]
+           + ([(TT, b("Zs"), Id)] if TUNE["zs"] == "S" else [(TT, b("A1"), b("IFq")), (TT, b("Cf"), b("IFq"))]), stop=False)
         mm([(TT, nId, b("ov", (0, 128)))], start=False, stop=False)
         mm([(Tp, one, b("cT")), (Tp, b("ZP"), b("BDs")), (Tp, b("nIs"), b("ov", (128, 256)))], stop=False)
         for c in range(4):
@@ -395,21 +424,24 @@ def rank_program(g, core, T, topo):
         for j in range(2):
             cp(b("WI", (0, 4), c_(16 * j, 16)), b("IN", (0, 4), (256 * j, 256 * j + 256, 17)))
         mm([(Tp, b("WI"), b("BDs"))], start=False)
-        mm([(PB(6, k, 384 - k, 16), b("IN", (0, 4), (k, 512, 16)), b("RB")) for k in range(16)], start=False)
+        for c0, c1 in TUNE["cnt"]:
+            mm([(b("PB6", (k, 384, 16), p=(32 * c0, 32 * c1)), b("IN", (c0, c1), (k, 512, 16)), b("RB")) for k in range(16)], start=False,
+               stop=(c0, c1) == TUNE["cnt"][-1])
         mm([(PB(5, 256, 128), Id, x), (PB(5, 256, 128), nId, yl)])
         act(b("nx"), PB(5, 256, 128), F.Abs)
-        mm([(PB(5, 256, 32), b("nx"), b("W1"))])
+        mm([(PB(5, 256, 32), b("nx"), b("W", (0, 32)))])
         tt(b("b1"), PB(5, 256, 32), pj, A.mult)
         ts(b("b2"), b("b1"), R - 1, A.bitwise_and)
         if last:
-            cp(b("EF", c_(128 + wg, L)), b("E", c_(128 + wg, L)))
-            cp(b("EF", c_(128, wg)), b("E", c_(128, wg)))
+            copy(TUNE["ef"], b("EF", c_(128 + wg, L)), b("E", c_(128 + wg, L)))
+            for j in range(2):
+                copy(TUNE["ef"], b("EF", c_(128 + wg // 2 * j, wg // 2)), b("E", c_(128 + wg // 2 * j, wg // 2)))
             dma("Y", "out0", T.ykids[:, wg:wg + L], b("EF", c_(128 + wg, L)), 1.5)
         ts(b("wr"), Tp, 0.0, A.is_gt, wcol, A.mult)
         tt(b("wB"), PB(4, 256, 128, 16), b("vB"), A.min)
-        mm([(PB(0, 0, 128), b("n2Id"), b("wr"))] + [(PB(0, 16 * k, 16), b("EQ", c_(128 * k, 128)), b("wr", c_(16 * k, 16))) for k in range(8)])
-        ts(b("wL"), PB(0, 0, 128), 0.0, A.is_lt)
-        tt(pad("ZW"), b("wL", (0, 128, 4)), pj, A.mult)
+        mm([(PB(0, 16 * k, 16), b("EQ", c_(128 * k, 128)), b("wr", c_(16 * k, 16))) for k in range(8)], apart=True)
+        tt(b("wL"), PB(0, 0, 128), b("wr"), A.is_lt)
+        tt(pad("ZO"), b("wL", (0, 128, 4)), b("oP"), A.mult)
         tt(pad("ZB"), b("wL", (0, 128, 4)), b("b2"), A.mult)
         tt(b("t1"), b("wL", (0, 128, 16)), b("vn"), A.mult)
         ts(b("cap"), TT, 0.0, A.is_gt, BIG, A.mult)
@@ -417,26 +449,25 @@ def rank_program(g, core, T, topo):
         tt(b("SK"), sK, b("cap"), A.min)
         scan(b("sc"), b("Mh"), b("MK"), 0.0, A.mult, A.max)
         scan(b("ss"), b("Mh"), b("SK"), 0.0, A.mult, A.max)
-        cp(b("ZS", (15, 143, 16)), b("ss", (15, 128, 16)))
+        for j in range(2):
+            ts(b("ZS", (7 + 8 * j, 135, 16)), b("ss", (15, 128, 16)), b("col", c_(10 + 2 * j, 1)), A.mult)
         tt(b("mt"), b("sc", (15, 128, 16)), b("wB"), A.max)
         ts(b("hi"), b("mt"), MAGIC, A.add, -MAGIC, A.add)
         tt(b("m1"), b("mt"), b("t1"), A.subtract)
         tt(vl, b("m1"), b("hi"), A.subtract)
-        mm([(PB(1, 0, 8), Id, b("il"))] + tolist(PB(1, 0, 8), "ZW", "Mv"))
-        tt(b("of"), PB(1, 0, 8), b("vo"), A.min)
-        cp(o16, b("of"))
-        mm(tolist(PB(5, 384, 8), "ZB", "M16"), stop=False)
-        mm([(PB(5, 384, 8), b("ZL", c_(15 - k, 128)), b("I16", (k, 128, 16))) for k in range(16)], start=False)
-        cp(b("e2") if last else v16, PB(5, 384, 8))
+        mm([(PB(7, 0, 8), b("I16"), b("il"))] + tolist(PB(7, 0, 8), "ZO", "M16"))
+        cp(o16, PB(7, 0, 8))
+        mm([(PB(1, 16, 8), b("ZL", c_(15 - k, 128)), b("I16", (k, 128, 16))) for k in range(16)], stop=False)
+        mm(tolist(PB(1, 16, 8), "ZB", "M16"), start=False)
+        cp(b("e2") if last else v16, PB(1, 16, 8))
         if not last:
-            ts(b("vo"), PB(5, 384, 8), 128.0, A.add)
-            mm([(PB(1, 8, 8), b("I16"), vl)] + [(PB(1, 8, 8), b("I16"), b("ZB", (3 + 4 * j, 131, 16))) for j in range(4)])
-            act(b("vn"), PB(1, 8, 8), F.Copy)
-            act(b("vB"), PB(1, 8, 8), F.Copy, bias=TOP)
-        mm([(PB(2, 0, 128), one, b("c1")), (PB(2, 0, 128), b("cap"), b("NC", (128, 256)))])
+            mm([(PB(7, 8, 40), Id, b("cO")), (PB(7, 8, 8), b("I16"), vl), (PB(7, 16, 32), b("I16"), pad("ZB"))]
+               + [(PB(7, 8, 8), b("I16"), b("ZB", (3 + 4 * j, 131, 16))) for j in range(4)] + [(PB(7, 16 + j, 32 - j, 4), b("I16"), vl) for j in range(4)])
+            nodes()
+        mm([(PB(2, 0, 128), one, b("c1")), (PB(2, 0, 128), b("cap"), b("nIr"))])
         tt(b("mm"), PB(2, 0, 128), b("AA"), A.mult)
         mm([(PB(3, 0, 128), Id, b("T1")), (PB(3, 0, 128), Id, b("T2"))] + [(PB(3, 0, 128), Id, b("P128"))] * t, stop=False)
-        mm([(PB(3, k, 128 - k, 16), b("ZS", c_(15 - k, 128)), b("I4", (k, 128, 16))) for k in range(16)], start=False)
+        mm([(PB(3, k, 128 - k, 8), b("ZS", c_(7 - k, 128)), b("I4", (k, 128, 8))) for k in range(8)], start=False)
         tt(b("VC"), PB(3, 0, 128), b("mm"), A.subtract)
         ek = "EF" if last else "E"
         cp(ind(b(ek, (0, 128 + wg)), o16), b("VC"))
@@ -445,7 +476,7 @@ def rank_program(g, core, T, topo):
         new = b("X", c_(M + L * t, L))
         for out, src, k, eng in ((b("YW"), yl, 4, TUNE["sel"][0]), (new, x, 0, TUNE["sel"][1])):
             if eng == "S":
-                mm([(PB(k, 384, 128), Id, src), (PB(k, 384, 128), one, b("c256")), (PB(k, 384, 128), b("wL"), b("I256"))])
+                mm([(PB(k, 384, 128), Id, src), (PB(k, 384, 128), one, b("c4")), (PB(k, 384, 128), b("wL"), b("I4"))])
                 act(out, PB(k, 384, 128), F.Relu)
             else:
                 mm([(PB(k, 384, 128), b("wL"), Id)])
@@ -456,8 +487,8 @@ def rank_program(g, core, T, topo):
         mm([(PB(5, 0, 128), Id, x), (PB(5, 0, 128), nId, b("YW"))])
         act(x, PB(5, 0, 128), F.Abs)
         mm([(PB(6, 0, 256), one, b("cN")), (PB(6, 0, 128), IF, b("Cf")), (PB(6, 0, 128), b("SK"), b("I4")),
-            (PB(6, 0, 256), b("cap"), b("NC")), (PB(6, 0, 256), b("wL"), b("NW"))])
-        ts(b("Bq"), PB(6, 128, 128), 4095.0, A.mult, 4095.0, A.min)
+            (PB(6, 0, 128), b("cap"), Id), (PB(6, 128, 128), b("cap"), b("nIr")), (PB(6, 0, 128), b("wL"), b("IB")), (PB(6, 128, 128), b("wL"), nId)])
+        ts(b("Bq"), PB(6, 128, 128), -1.5, A.is_gt, 4095.0, A.mult)
         tt(b(ek, c_(128 + M + L * t, L)), PB(6, 0, 128), b("Bq"), A.max)
         if last:
             dma("Y", "out", T.ykids[:, M + L * t:M + L * t + L], b("EF", c_(128 + M + L * t, L)), 1.5)
@@ -468,6 +499,8 @@ def rank_program(g, core, T, topo):
     def schedule():
         N = len(calls)
         WAKE = TUNE["wake"]
+        for c in calls:
+            c["dur"] = length(c["cost"], (TUNE["f"], 1.56, 3.8))
         succ = [[] for _ in range(N)]
         for c in calls:
             for m, w in c["pre"].items():
@@ -514,13 +547,35 @@ def rank_program(g, core, T, topo):
             prio = [at[n] + dur[n] for n in range(N)]
             return place(prio) + (prio,)
 
+        cases = []
+        for k in CASES:
+            cases.append(([length(c["cost"], k) for c in calls],
+                          [[(m, k[3] + calls[m]["lat"] * (k[4] if eng[m] == "A" else k[5]) if w else 0.0) for m, w in c["pre"].items()] for c in calls]))
+
+        def spans(at):
+            order, total = sorted(range(N), key=lambda n: (at[n], n)), 0.0
+            for d, pre in cases:
+                end, free = [0.0] * N, {k: 0.0 for k in eng}
+                for n in order:
+                    t0 = 0.0 if eng[n] == "A" else free[eng[n]]
+                    for m, e in pre[n]:
+                        if end[m] + e > t0:
+                            t0 = end[m] + e
+                    end[n] = free[eng[n]] = t0 + d[n]
+                total += float(np.log(max(end[n] + tail[n] for n in range(N))))
+            return float(np.exp(total / len(cases)))
+
         rng = np.random.RandomState(TUNE["seed"])
-        best, at, prio = sweep(rest)
+        span, at, prio = sweep(rest)
+        best = spans(at)
         for _ in range(TUNE["tries"]):
-            span, at2, new = sweep([p + TUNE["noise"] * r for p, r in zip(prio, rng.randn(N).tolist())])
-            if span <= best:
-                best, at, prio = span, at2, new
-        ORDERS["span"] = best
+            mid = span * float(rng.rand())
+            span2, at2, new = sweep([p + TUNE["noise"] * r if abs(a - mid) < TUNE["reach"] else p for p, r, a in zip(prio, rng.randn(N).tolist(), at)])
+            if span2 <= span * 1.01:
+                mean = spans(at2)
+                if mean <= best:
+                    best, span, at, prio = mean, span2, at2, new
+        ORDERS.update(span=span, mean=best, at=at, calls=calls)
         return sorted(range(N), key=lambda n: (at[n], n))
 
     if "order" not in ORDERS:

import numpy as np
from concourse.bass import DstId, RemoteDMATransfer
from concourse.mybir import AluOpType as A, ActivationFunctionType as F, AxisListType as AX

M, L, STEPS, H, R, NB = 896, 128, 3, 2048, 512, 4
XW = 1296
BF, F32, I32, U16, F16 = "bfloat16", "float32", "int32", "uint16", "float16"
BIG, TOP, MAGIC = 2.0 ** 22, 2.0 ** 21, 1.5 * 2.0 ** 35
_S = {
    "spi": (8, I32), "E": (128 + 1280, I32), "EF": (128 + 1280, F32), "X": (XW, BF), "bk": (3 * H, BF), "x": (L, BF), "xT": (L, BF), "nx": (L, BF),
    "wt": (2, BF), "wl": (24, BF), "qs": (8 * STEPS, U16), "ql": (8 * STEPS, U16), "ys": (L * STEPS, BF), "yl": (L * STEPS, BF),
    "one": (128, BF), "pk": (128, I32), "pa": (128, I32), "Id": (128, BF), "IF": (128, F32), "IFq": (128, F32),
    "BD0": (128, BF), "BD": (128, BF), "BDf": (40, F32), "PJ": (64, BF), "Q4": (32, BF),
    "I16": (128, F16), "il": (8, F16), "cO": (40, BF), "oP": (32, F32), "rt": (128, F32), "TR": (128, F32), "zer": (128, F32), "wsc": (128, F32), "sg": (16, F32), "CODE": (1024, BF),
    "col": (16, F32), "KC": (384, BF), "cN": (256, BF), "ni": (128, BF),
    "RB": (24, BF), "W": (64, BF), "ZU": (132, F16), "zb": (288, BF), "Wz": (192, BF), "spf": (8, F32), "sv": (128, F32),
    "lst": (16, U16), "e2": (8, F32), "Ci": (128, I32), "C16": (128, U16), "A1": (128, F32), "Cf": (128, F32), "fe": (128, BF), "AA": (128, F32),
    "Zs": (128, BF), "ZP": (128, BF), "XC": (2048, BF), "D": (2048, BF), "XV": (128, BF), "z": (128, BF),
    "uz": (64, I32), "uy": (64, I32), "hz": (64, I32), "ZH": (132, F16), "Ui": (256, I32), "U2": (256, I32), "h1": (128, I32), "h2": (128, I32),
    "H16": (128, U16), "BC": (2048, BF), "CG": (128, BF), "CGm": (256, BF), "EQ": (1024, BF), "WO": (128, BF), "ov": (256, BF),
    "wr": (128, BF), "cap": (128, BF), "wL": (128, BF), "ZL": (144, F16), "ZS": (144, BF), "ZO": (132, F16), "b1": (32, I32), "b2": (32, I32),
    "M16": (32, F16), "ZB": (132, F16),
    "MK": (128, F32), "SK": (128, BF), "sc": (128, F32), "ss": (128, BF), "Mh": (128, BF),
    "mm": (128, F32), "VC": (128, F32), "Bq": (128, F32), "YW": (128, BF),
}
_IN = {}
for _buf, _w, _d, _names in (("KB", 128, BF, "nId BDs P cT c1 T1 T2 P128 I4 IB nIr c4 nIs"), ("KF", 8, F32, "hi vB vn wB t1 mt m1")):
    for _j, _k in enumerate(_names.split()):
        _IN[_k] = (_buf, _w * _j, _w)
    _S[_buf] = (_w * len(_names.split()), _d)
SCRATCH = {k: ("sbuf", [128, w], d) for k, (w, d) in _S.items() if k not in _IN}
TUNE = {"wake": 0.15, "remote": 2.3, "load": 2.0, "tries": 5000, "noise": 0.2, "seed": 0, "reach": 4.0, "f": 1.15, "xs": (0, 2), "sb": (2,), "sel": "SS", "xv": "S",
        "cnt": ((0, 4),), "war": True, "parts": ((0, 2), (2, 2)), "wo": "G", "cf": "G", "ef": "G", "zs": "S", "fe": "S", "vb": "S"}
for _k, _s, _d in (("OV", [8, 256], BF), ("IN", [4, 512], BF), ("WI", [4, 32], BF), ("Ex", [128, 16], BF)):
    SCRATCH[_k] = ("sbuf", [128] + _s, _d)
for _k, (_c, _n) in enumerate(TUNE["parts"]):
    SCRATCH["HB%d" % _k] = ("sbuf", [128, 72 // _n, 4 * _n], F16)
for _k in range(8):
    SCRATCH["PB%d" % _k] = ("psum", [128, 512], F32)
SIZE = {BF: 2, F16: 2, U16: 2, F32: 4, I32: 4}
CASES = ((1.0, 1.56, 3.8, 0.15, 1.0, 1.0), (1.25, 1.15, 2.5, 0.1, 0.8, 1.2), (1.2, 1.95, 5.0, 0.2, 1.2, 0.85), (1.45, 1.56, 3.0, 0.13, 1.1, 1.1),
         (1.1, 1.3, 4.5, 0.22, 0.9, 1.3))
ORDERS = {}
DMAS = ["spi", "E", "x", "X", "wt", "bk0", "bk1", "bk2", "out", "out0"]
SEMAPHORES = (["sV", "sS", "sP", "sG", "wloc", "wrem"] + ["d_" + k for k in DMAS]
              + [k + str(t) for k in ("qa", "qo", "ya", "yo") for t in range(STEPS)])
CYC, PEC = 0.00083, 0.00042


def rank_program(g, core, T, topo):
    rank = T.rank_of(core)
    if rank is None:
        return
    Q = {"V": g.vector, "S": g.scalar, "P": g.tensor, "G": g, "Y": g.sync}
    V, S, PE = g.vector, g.scalar, g.tensor
    cnt = {k: 0 for k in "VSPG"}
    known = {k: {} for k in Q}
    snap = {}

    def b(name, *idx, p=None):
        if name in _IN:
            name, o, w = _IN[name]
            i = idx[0] if idx else (0, w)
            idx = ((o + i[0], o + i[1]) + i[2:],)
        shape = SCRATCH[name][1]
        ix = tuple(slice(*i) if isinstance(i, tuple) else i for i in idx)
        cols = np.arange(int(np.prod(shape[1:]))).reshape(shape[1:])[ix].reshape(-1)
        bits = np.zeros(int(np.prod(shape[1:])), np.uint8)
        bits[cols] = 1
        mask = int.from_bytes(np.packbits(bits, bitorder="little").tobytes(), "little")
        return (T[name][(slice(*p) if p else slice(None),) + ix], [(name, mask)], len(cols), SCRATCH[name][2], False)

    def ind(win, off):
        return (win[0].indirect(off[0]), win[1], 16 * off[2], win[3], off[1])

    def a_(v):
        return v[0] if isinstance(v, tuple) else v

    def psum(v):
        return v[1][0][0][:2] == "PB"

    def wait(eng, toks):
        best = {}
        for s, v in toks:
            if known[eng].get(s, 0) < v:
                best[s] = max(best.get(s, 0), v)
        for s, v in sorted(best.items(), key=lambda a: -len(snap.get(a, ()))):
            if known[eng].get(s, 0) >= v:
                continue
            Q[eng].wait_ge(T.sem[s], v)
            known[eng][s] = v
            for k, n in snap.get((s, v), {}).items():
                known[eng][k] = max(known[eng].get(k, 0), n)

    calls, touched, banks = [], {}, {}

    def note(eng, rd, wr, fn, dur, kind="c", lat=0.0, tok=None):
        n, pre = len(calls), {}
        rd = [v for v in rd if isinstance(v, tuple)]
        rs = [r for v in rd for r in v[1]] + [r for v in rd + wr if v[4] for r in v[4]]
        ws = [r for v in wr for r in v[1]]
        for regs, w in ((rs, False), (ws, True)):
            for k, mask in regs:
                for m, mk, mw in touched.get(k, ()):
                    if mk & mask and (w or mw):
                        own = w and eng == calls[m]["eng"] and kind == calls[m]["kind"] == "c" and (eng == "P" or not TUNE["war"])
                        pre[m] = pre.get(m, False) or not own
        for k, mask in ws:
            touched[k] = [(m, mk & ~mask, mw) for m, mk, mw in touched.get(k, ()) if mk & ~mask] + [(n, mask, True)]
        for k, mask in rs:
            touched.setdefault(k, []).append((n, mask, False))
        for k in sorted(set(k for k, _ in rs + ws if k[:2] == "PB")):
            cur = banks.get(k, (None, [], []))
            if cur[0] != eng:
                banks[k] = cur = (eng, [], cur[1])
            for m in cur[2]:
                pre[m] = True
            if eng == "P":
                for m in cur[1][-1:]:
                    pre[m] = pre.get(m, False)
            cur[1].append(n)
        calls.append({"eng": eng, "pre": pre, "fn": fn, "kind": kind, "lat": lat, "tok": tok, "n": n, "cost": dur, "to": (ws or rs)[0][0]})
        return n

    def cost(eng, out, ins, two=False):
        vs = [out] + ins
        n = ins[0][2] if ins else out[2]
        if out[4]:
            return (0.05, n * CYC, "scatter")
        if any(v[4] for v in ins):
            return (0.06, n * CYC, "gather2" if two else "gather")
        if eng == "S":
            return 0.06 + max(64, n) * CYC
        r = (1.0 if any(psum(v) for v in ins) else 2.0) if two else 0.5 if all(SIZE[v[3]] == 2 for v in vs) else 1.0
        return max(64, n * r) * CYC

    def length(c, k):
        if isinstance(c, float):
            return c * k[0]
        return (c[0] + c[1] * {"scatter": k[2], "gather": k[1], "gather2": max(2.0, k[1])}[c[2]]) * k[0]

    dcount, loads = {}, {}

    def dma(eng, sem, out, in_, lat):
        dcount[sem] = dcount.get(sem, 0) + 16
        n = note(eng, [in_], [out] if isinstance(out, tuple) else [], lambda: Q[eng].dma_start(a_(out), a_(in_)).then_inc(T.sem["d_" + sem], 16),
                 0.06, "d", lat, ("d_" + sem, dcount[sem]))
        if isinstance(out, tuple):
            if eng in loads:
                calls[n]["pre"][loads[eng]] = False
            loads[eng] = n

    def lands(m, out, arrive, n):
        k = note("A", [], out, None, 0.0, "a", TUNE["remote"], (arrive, n))
        calls[k]["pre"][m] = True

    def send(out, in_, dst, src, arrive, left):
        rid, pid = topo.addr(dst, core)
        m = note("G", [in_], [], lambda: g.remote_dma(out[0], in_[0], T.sem[arrive], T.sem[left], pid, rid, topo.mask(core, dst)), 0.3, "r")
        lands(m, [out], arrive, len(topo.engines(src, core)))

    def tt(out, x0, x1, o):
        note("V", [x0, x1], [out], lambda: V.tensor_tensor(out[0], x0[0], x1[0], o), cost("V", out, [x0, x1], True))

    def ts(out, x0, s1, o0, s2=None, o1=None):
        more = () if o1 is None else (o1,)
        note("V", [x0, s1, s2], [out], lambda: V.tensor_scalar(out[0], x0[0], a_(s1), a_(s2), o0, *more), cost("V", out, [x0]))

    def cp(out, x0):
        note("V", [x0], [out], lambda: V.tensor_copy(out[0], x0[0]), cost("V", out, [x0]))

    def scan(out, d0, d1, init, o0, o1):
        note("V", [d0, d1], [out], lambda: V.tensor_tensor_scan(out[0], d0[0], d1[0], init, o0, o1), cost("V", out, [d0, d1]))

    def fill(out, c):
        note("V", [], [out], lambda: V.memset(out[0], c), cost("V", out, []))

    def act(out, x0, f, bias=0.0, scale=1.0):
        note("S", [x0, bias, scale], [out], lambda: S.activation(out[0], x0[0], f, bias=a_(bias), scale=a_(scale)), cost("S", out, [x0]))

    def mul(eng, out, x0, c, add=0.0):
        if eng == "S":
            act(out, x0, F.Copy, scale=c, bias=add)
        else:
            ts(out, x0, c, A.mult, add, A.add)

    def mm(lst, start=True, stop=True, apart=False, more=()):
        def go():
            i = None
            for n, (o, l, r) in enumerate(lst):
                i = PE.matmul(o[0], l[0], r[0], apart or (start and n == 0), apart or (stop and n == len(lst) - 1))
            return i
        m = note("P", [v for _, l, r in lst for v in (l, r)], [o for o, _, _ in lst], go,
                 sum(max(min(64, l[2]), r[2]) * SIZE[l[3]] ** 2 / 4 * PEC for _, l, r in lst))
        for k in more:
            calls[m]["pre"][k] = True
        return m

    def gp(out, ins, fn):
        note("G", ins, [out], fn, 0.15 + 2 * out[2] * CYC)

    def copy(eng, out, x0):
        if eng == "G":
            gp(out, [x0], lambda: g.affine_select(out[0], x0[0], [[0, out[2]]], A.is_ge, 0.0, 0, 0))
        else:
            cp(out, x0)

    def c_(a, n):
        return (a, a + n)

    one, Id, nId, IF, BD, P, PJ = (b(k) for k in ("one", "Id", "nId", "IF", "BD", "P", "PJ"))
    x, xT = b("x"), b("xT")
    bd8, bd32, pj = b("BD", (0, 128, 16)), b("BD", (0, 128, 4)), b("PJ", (0, 32))

    def pad(k):
        return b(k, (3, 131, 4))

    def tolist(out, k, mv):
        return [(out, b(k, c_(3 - kk, 128)), b(mv, (kk, 32, 4))) for kk in range(4)]

    ld = TUNE["load"]
    dma("Y", "spi", b("spi"), T.spot[:], ld - 0.6)
    dma("Y", "E", b("E", c_(128, M)), T.kids[:], ld + 0.6)
    dma("S", "wt", b("wt"), T.wts[:], ld - 0.6)
    dma("S", "x", x, T.cand[:], ld - 0.5)
    dma("Y", "X", b("X", (0, M)), T.nodes[:], ld + 1.4)
    for j in range(3):
        dma("Y", "bk%d" % j, b("bk", c_(H * j, H)), T.book[:], ld + 3.2 + 1.8 * j)

    fill(one, 1.0)
    gp(b("pk"), [], lambda: g.iota(T.pk[:], [[0, 8], [-1, 16]], 16, 1))
    gp(Id, [one], lambda: g.affine_select(T.Id[:], T.one[:], [[-1, 128]], A.is_equal, 0.0, 0, 1))
    gp(b("BD0"), [one], lambda: g.affine_select(T.BD0[:], T.one[:], [[-16, 8], [0, 16]], A.is_ge, 0.0, 0, 1))
    gp(BD, [b("BD0")], lambda: g.affine_select(T.BD[:], T.BD0[:], [[16, 8], [0, 16]], A.is_ge, 0.0, 15, -1))
    others = [T.cores[(rank - 1 - j) % NB] for j in range(NB - 1)]
    neng = len(topo.engines(core, others[0]))

    def weights():
        ids = [DstId(rid=topo.addr(d, core)[0], pnc=topo.addr(d, core)[1]) for d in others]
        return g.remote_dma_fused([RemoteDMATransfer(dst_ids=ids, dma_engine_mask=topo.mask(core, others[0]), remote_sem=T.sem.wrem, srcs=[T.wt[:]],
                                                     dsts=[T.wl[:, 8 * j:8 * j + 2] for j in range(NB - 1)])], local_sem=T.sem.wloc)
    lands(note("G", [b("wt")], [], weights, 0.5, "r"), [b("wl")], "wrem", neng * (NB - 1))
    fill(b("rt"), 0.35)
    fill(b("zer"), 0.0)
    gp(b("TR"), [b("rt")], lambda: g.affine_select(T.TR[:], T.rt[:], [[-1, 128]], A.is_gt, 1.0, 0, 1))
    gp(b("ni"), [], lambda: g.iota(T.ni[:], [[1, 128]], 1, 0, allow_small_or_imprecise_dtypes=True))
    scan(b("wsc"), b("TR"), b("zer"), 2.0 ** 96, A.mult, A.add)
    wcol = b("wsc", (127, 128))

    fill(b("X", (M, XW)), 0.0)
    for k in ("ZS", "zb"):
        fill(b(k), 0.0)
    PARTS = TUNE["parts"]
    for k in ["ZL", "ZH", "ZU", "ZB", "ZO"] + ["HB%d" % h for h in range(len(PARTS))]:
        cp(b(k), b("zb", (0, b(k)[2])))
    fill(b("Mh"), 1.0)
    fill(b("Mh", (0, 128, 16)), 0.0)
    fill(b("KC", (128, 256)), -1.5 / 128)
    fill(b("KC", (256, 384)), 0.0)
    fill(b("cT"), -3 * BIG / 128)
    fill(b("c1"), 1.0 / 128)
    fill(b("c4"), -4096.0 / 128)
    fill(b("cN", (0, 128)), -2 * BIG / 128)
    fill(b("cN", (128, 256)), 0.0)
    cp(b("Ex", (0, 128), (0, 1)), Id)
    for n in (1, 2, 4, 8):
        cp(b("Ex", (0, 128), c_(n, n)), b("Ex", (0, 128), (0, n)))
    mul("V", nId, Id, -1.0)
    mm([(b("PB4", (384, 512)), x, Id)])
    act(xT, b("PB4", (384, 512)), F.Copy)
    ts(b("pa"), b("pk"), 15, A.bitwise_and)
    ts(P, b("pa"), 0, A.is_equal)
    ts(b("uz", (0, 32)), b("pk", (0, 128, 4)), 12, A.bitwise_and)
    for j in range(2):
        ts(b("PJ", c_(32 * j, 32)), b("uz", (0, 32)), 0, A.is_equal)
    ts(b("uz", (32, 64)), b("pk", (0, 32)), 3, A.bitwise_and)
    ts(b("Q4"), b("uz", (32, 64)), 0, A.is_equal)
    tt(b("M16"), bd32, b("Q4"), A.mult)
    ts(b("PB7", (384, 512)), P, -1.0, A.mult, 1.0, A.add)
    kcol, slot, lane, m0, m1, n0, n1 = (b("col", c_(j, 1)) for j in (0, 2, 4, 6, 8, 10, 12))
    ts(kcol, b("pa", (0, 1)), -512.0, A.mult, 7680.0, A.add)
    ts(slot, b("pa", (0, 1)), -1.0, A.add)
    ts(lane, b("pk", (0, 1)), -1.0, A.mult, 144.0, A.add)
    ts(b("il"), b("ni", (0, 128, 16)), slot, A.add)
    fill(b("cO", (0, 8)), 0.0)
    ts(b("cO", (8, 40)), b("one", (0, 32)), lane, A.mult)
    for m, src in ((m0, b("BD", (0, 128, 32))), (m1, b("BD", (16, 128, 32))), (n0, b("P", (0, 8))), (n1, b("P", (8, 16)))):
        note("V", [src], [m], lambda m=m, src=src: V.tensor_reduce(m[0], src[0], AX.X, A.add), 64 * CYC)
    for eng, out, src, f in (("S", IF, Id, 1.0), ("S", b("IFq"), Id, 1.0 / 4096), ("S", b("KC", (0, 128)), P, kcol), ("S", b("BDs"), BD, 2 * BIG),
                             ("V", b("I4"), Id, 4096.0), ("V", b("nIs"), Id, -2 * BIG), ("V", b("IB"), Id, BIG), ("V", b("nIr"), Id, -1.0 / BIG),
                             ("V", b("P128"), P, 128.0),
                             ("S", b("BDf", (0, 8)), bd8, 1.0), ("S", b("BDf", (8, 40)), bd32, 1.0), ("V", b("I16"), Id, 1.0),
                             ("V", b("RB", (0, 8)), bd8, 65536.0), ("V", b("RB", (8, 16)), bd8, 1.0), ("V", b("RB", (16, 24)), bd8, 1.0)):
        mul(eng, out, src, f)
    ts(b("T1"), P, M - 4096.0, A.mult, 4096.0, A.add)
    tt(b("YW"), P, b("ni"), A.mult)
    ts(b("T2"), b("YW"), -1.0, A.add)
    ts(b("sg"), b("P", (0, 16)), -2.0, A.mult, 1.0, A.add)
    fill(b("CODE", (0, 1)), -1.0)
    for j in range(10):
        ts(b("CODE", c_(2 ** j, 2 ** j)), b("CODE", (0, 2 ** j)), b("sg", c_(j, 1)), A.mult)
    for u in range(2):
        ts(b("W", c_(32 * u, 32)), bd32, b("wt", c_(u, 1)), A.mult)
    for j in range(3):
        for u in range(2):
            ts(b("Wz", c_(64 * j + 32 * u, 32)), bd32, b("wl", c_(8 * j + u, 1)), A.mult)
    v16, o16 = b("lst", (8, 16)), b("lst", (0, 8))
    cp(v16, b("spi"))
    cp(b("spf"), b("spi"))
    for c in range(8):
        mul("S", b("sv", c_(16 * c, 16)), b("P", (0, 16)), b("spf", c_(c, 1)))

    def PB(k, a=0, n=512, s=1):
        return b("PB%d" % k, (a, a + n, s))

    def nodes():
        tt(b("oP"), PB(7, 16, 32), pj, A.mult)
        cp(b("vn"), PB(7, 8, 8))
        mul(TUNE["vb"], b("vB"), b("vn"), 1.0, TOP)
    mm([(PB(7, 8, 40), Id, b("cO")), (PB(7, 8, 40), b("sv"), b("BDf"))])
    vl = b("ZL", (15, 143, 16))
    nodes()

    def ch(k, c):
        return b(k, c_(512 * c, 512))

    def ch3(k, c):
        return b(k, c_(2 * c, 2))

    def halves(t, h1, h2, u1, u2, tmp, f, u):
        tt(h1, u1, u2, A.mult)
        ts(h2, h1, 5, A.logical_shift_right, H - 1, A.bitwise_and)
        cp(f, h2)
        if t:
            ts(u, u2, -float(H), A.add)
            return float(H)
        ts(tmp, u2, H - 1, A.bitwise_and)
        cp(u, tmp)
        return 0.0

    for t in range(STEPS):
        last = t == STEPS - 1
        wg = M + L * max(0, t - 1)
        asked, asker = T.cores[(rank + 1 + t) % NB], T.cores[(rank - 1 - t) % NB]
        Ev = ind(b("E", c_(128, wg)), v16)
        bk = b("bk") if t else b("bk", (0, 2 * H))
        yl = b("yl", c_(L * t, L))
        ts(b("Ci"), Ev, 4095, A.bitwise_and)
        ts(b("C16"), b("Ci"), 1280.0, A.min)
        if TUNE["xv"] == "V":
            tt(b("XV"), ind(b("X", (0, wg)), v16), x, A.subtract)
            act(b("z"), b("XV"), F.Abs)
        else:
            act(b("XV"), ind(b("X", (0, wg)), v16), F.Copy)
            mm([(PB(7, 128, 128), nId, x), (PB(7, 128, 128), Id, b("XV"))])
            act(b("z"), PB(7, 128, 128), F.Abs)
        mm([(PB(7, 64, 64), b("z"), b("Wz", c_(64 * t, 64)))])
        tt(b("uz"), PB(7, 64, 64), PJ, A.mult)
        ts(b("uy"), b("uz"), 4095, A.bitwise_and)
        off = halves(t, b("hz", (0, 32)), b("hz", (32, 64)), b("uy", (0, 32)), b("uy", (32, 64)), b("uz", (0, 32)), pad("ZH"), pad("ZU"))
        mm(tolist(PB(7, 128, 8), "ZU", "M16"), stop=False)
        mm(tolist(PB(7, 128, 8), "ZH", "M16"), start=False)
        ts(b("qs", c_(8 * t, 8)), PB(7, 128, 8), 4 * off, A.add)
        send(b("ql", c_(8 * t, 8)), b("qs", c_(8 * t, 8)), asked, asker, "qa%d" % t, "qo%d" % t)
        for c in range(4):
            mm([(PB(c), xT, b("Ex", c_(32 * c, 32)))], stop=False)
            src = ind(b("X"), b("C16", c_(32 * c, 32)))
            if c in TUNE["xs"]:
                act(ch("XC", c), src, F.Copy)
            else:
                cp(ch("XC", c), src)
            mm([(PB(c), nId, ch("XC", c))], start=False)
            act(ch("D", c), PB(c), F.Abs)
            act(ch3("OV", c), PB(c), F.Sign, bias=0.5)
        ts(b("A1"), Ev, -1.0, A.mult, 4095.0, A.add)
        copy(TUNE["cf"], b("Cf"), b("Ci"))
        if TUNE["fe"] == "S":
            act(b("fe"), b("Cf"), F.Relu, bias=-4094.0)
        else:
            ts(b("fe"), b("Ci"), 4095.0, A.is_ge)
        mm([(PB(7, 256, 128), b("IFq"), b("A1")), (PB(7, 256, 128), b("IFq"), b("Cf")), (PB(7, 256, 128), b("I4"), b("fe"))])
        if TUNE["zs"] == "S":
            act(b("Zs"), PB(7, 256, 128), F.Copy)
        tt(b("ZP"), PB(7, 256, 128), P, A.mult)
        tt(b("AA"), PB(7, 384, 128), b("A1"), A.mult)
        act(b("CG"), ind(b("CODE"), v16), F.Copy)
        for j, m in enumerate((m0, m1)):
            ts(b("CGm", c_(128 * j, 128)), b("CG"), m, A.mult)
        for h, (c, n) in enumerate(PARTS):
            u, hb, w, r = 4 + h % 2, "HB%d" % h, 32 * n, 4 // n
            h1, h2 = b("h1", c_(32 * c, w)), b("h2", c_(32 * c, w))
            mm([(PB(u, k, 2 * w - k, 16 // r), b("D", (512 * c + k, 512 * (c + n), 16 // r)), b("W", (0, 64, 4))) for k in range(16 // r)], apart=True)
            u1, u2 = b("U2", c_(64 * c, w)), b("U2", c_(64 * c + w, w))
            cp(b("Ui", c_(64 * c, 2 * w)), PB(u, 0, 2 * w))
            ts(b("U2", c_(64 * c, 2 * w)), b("Ui", c_(64 * c, 2 * w)), 4095, A.bitwise_and)
            off = halves(t, h1, h2, u1, u2, b("Ui", c_(64 * c, w)), b(hb, (r - 1, 9 * r - 1, r)), b(hb, (10 * r - 1, 18 * r - 1, r)))
            for j in range(2):
                mm([(PB(u, 128, w), b(hb, c_(9 * r * (1 - j) + r - 1 - kk, 8 * r)), b("I16", (kk, 128, r))) for kk in range(r)], start=j == 0, stop=j == 1)
            ts(b("H16", c_(32 * c, w)), PB(u, 128, w), off, A.add)
        act(b("ys", c_(L * t, L)), ind(bk, b("ql", c_(8 * t, 8))), F.Copy)
        send(yl, b("ys", c_(L * t, L)), asker, asked, "ya%d" % t, "yo%d" % t)
        mm([(PB(7, k, 128 - k, 16), b("OV", (0, 8), (k, 256, 16)), bd8) for k in range(16)], apart=True)
        copy(TUNE["wo"], b("WO"), b("OV", (0, 8), (0, 256, 17)))
        mm([(PB(7, 128, 128), b("WO"), BD)])
        act(b("ov"), PB(7, 0, 256), F.Relu, scale=-64.0, bias=128.0)
        for h in range(2):
            more = ()
            for a in (2 * h, 2 * h + 1):
                more = (mm([(PB(h, 256 * (a % 2), 256), b("CG", p=c_(32 * a, 32)), b("CGm", p=c_(32 * a, 32)))], more=more),)
            act(ch("EQ", h), PB(h), F.Relu, scale=0.5, bias=-7.5)
        key, TT, sK, Tp = PB(6, 0, 128), PB(6, 128, 128), PB(6, 256, 128), PB(4, 256, 128)
        mm([(PB(6, 0, 384), one, b("KC")), (key, b("Cf"), IF), (key, b("fe"), b("nIs")), (TT, b("fe"), b("nIs"))]
           + ([(TT, b("Zs"), Id)] if TUNE["zs"] == "S" else [(TT, b("A1"), b("IFq")), (TT, b("Cf"), b("IFq"))]), stop=False)
        mm([(TT, nId, b("ov", (0, 128)))], start=False, stop=False)
        mm([(Tp, one, b("cT")), (Tp, b("ZP"), b("BDs")), (Tp, b("nIs"), b("ov", (128, 256)))], stop=False)
        for c in range(4):
            src = ind(bk, b("H16", c_(32 * c, 32)))
            if c in TUNE["sb"]:
                act(ch("BC", c), src, F.Copy)
                mm([(PB(c), Id, ch("BC", c)), (PB(c), nId, ch("D", c))])
                ts(b("IN", c), PB(c), 0.0, A.is_ge)
            else:
                tt(b("IN", c), src, ch("D", c), A.is_ge)
        for j in range(2):
            cp(b("WI", (0, 4), c_(16 * j, 16)), b("IN", (0, 4), (256 * j, 256 * j + 256, 17)))
        mm([(Tp, b("WI"), b("BDs"))], start=False)
        for c0, c1 in TUNE["cnt"]:
            mm([(b("PB6", (k, 384, 16), p=(32 * c0, 32 * c1)), b("IN", (c0, c1), (k, 512, 16)), b("RB")) for k in range(16)], start=False,
               stop=(c0, c1) == TUNE["cnt"][-1])
        mm([(PB(5, 256, 128), Id, x), (PB(5, 256, 128), nId, yl)])
        act(b("nx"), PB(5, 256, 128), F.Abs)
        mm([(PB(5, 256, 32), b("nx"), b("W", (0, 32)))])
        tt(b("b1"), PB(5, 256, 32), pj, A.mult)
        ts(b("b2"), b("b1"), R - 1, A.bitwise_and)
        if last:
            copy(TUNE["ef"], b("EF", c_(128 + wg, L)), b("E", c_(128 + wg, L)))
            for j in range(2):
                copy(TUNE["ef"], b("EF", c_(128 + wg // 2 * j, wg // 2)), b("E", c_(128 + wg // 2 * j, wg // 2)))
            dma("Y", "out0", T.ykids[:, wg:wg + L], b("EF", c_(128 + wg, L)), 1.5)
        ts(b("wr"), Tp, 0.0, A.is_gt, wcol, A.mult)
        tt(b("wB"), PB(4, 256, 128, 16), b("vB"), A.min)
        mm([(PB(0, 16 * k, 16), b("EQ", c_(128 * k, 128)), b("wr", c_(16 * k, 16))) for k in range(8)], apart=True)
        tt(b("wL"), PB(0, 0, 128), b("wr"), A.is_lt)
        tt(pad("ZO"), b("wL", (0, 128, 4)), b("oP"), A.mult)
        tt(pad("ZB"), b("wL", (0, 128, 4)), b("b2"), A.mult)
        tt(b("t1"), b("wL", (0, 128, 16)), b("vn"), A.mult)
        ts(b("cap"), TT, 0.0, A.is_gt, BIG, A.mult)
        tt(b("MK"), key, b("cap"), A.subtract)
        tt(b("SK"), sK, b("cap"), A.min)
        scan(b("sc"), b("Mh"), b("MK"), 0.0, A.mult, A.max)
        scan(b("ss"), b("Mh"), b("SK"), 0.0, A.mult, A.max)
        for j in range(2):
            ts(b("ZS", (7 + 8 * j, 135, 16)), b("ss", (15, 128, 16)), b("col", c_(10 + 2 * j, 1)), A.mult)
        tt(b("mt"), b("sc", (15, 128, 16)), b("wB"), A.max)
        ts(b("hi"), b("mt"), MAGIC, A.add, -MAGIC, A.add)
        tt(b("m1"), b("mt"), b("t1"), A.subtract)
        tt(vl, b("m1"), b("hi"), A.subtract)
        mm([(PB(7, 0, 8), b("I16"), b("il"))] + tolist(PB(7, 0, 8), "ZO", "M16"))
        cp(o16, PB(7, 0, 8))
        mm([(PB(1, 16, 8), b("ZL", c_(15 - k, 128)), b("I16", (k, 128, 16))) for k in range(16)], stop=False)
        mm(tolist(PB(1, 16, 8), "ZB", "M16"), start=False)
        cp(b("e2") if last else v16, PB(1, 16, 8))
        if not last:
            mm([(PB(7, 8, 40), Id, b("cO")), (PB(7, 8, 8), b("I16"), vl), (PB(7, 16, 32), b("I16"), pad("ZB"))]
               + [(PB(7, 8, 8), b("I16"), b("ZB", (3 + 4 * j, 131, 16))) for j in range(4)] + [(PB(7, 16 + j, 32 - j, 4), b("I16"), vl) for j in range(4)])
            nodes()
        mm([(PB(2, 0, 128), one, b("c1")), (PB(2, 0, 128), b("cap"), b("nIr"))])
        tt(b("mm"), PB(2, 0, 128), b("AA"), A.mult)
        mm([(PB(3, 0, 128), Id, b("T1")), (PB(3, 0, 128), Id, b("T2"))] + [(PB(3, 0, 128), Id, b("P128"))] * t, stop=False)
        mm([(PB(3, k, 128 - k, 8), b("ZS", c_(7 - k, 128)), b("I4", (k, 128, 8))) for k in range(8)], start=False)
        tt(b("VC"), PB(3, 0, 128), b("mm"), A.subtract)
        ek = "EF" if last else "E"
        cp(ind(b(ek, (0, 128 + wg)), o16), b("VC"))
        if last:
            dma("Y", "out", T.ykids[:, 0:wg], b("EF", c_(128, wg)), 3.0)
        new = b("X", c_(M + L * t, L))
        for out, src, k, eng in ((b("YW"), yl, 4, TUNE["sel"][0]), (new, x, 0, TUNE["sel"][1])):
            if eng == "S":
                mm([(PB(k, 384, 128), Id, src), (PB(k, 384, 128), one, b("c4")), (PB(k, 384, 128), b("wL"), b("I4"))])
                act(out, PB(k, 384, 128), F.Relu)
            else:
                mm([(PB(k, 384, 128), b("wL"), Id)])
                tt(out, PB(k, 384, 128), src, A.mult)
        if not last:
            mm([(PB(4, 0, 128), x, Id), (PB(4, 0, 128), b("YW"), nId)])
            act(xT, PB(4, 0, 128), F.Abs)
        mm([(PB(5, 0, 128), Id, x), (PB(5, 0, 128), nId, b("YW"))])
        act(x, PB(5, 0, 128), F.Abs)
        mm([(PB(6, 0, 256), one, b("cN")), (PB(6, 0, 128), IF, b("Cf")), (PB(6, 0, 128), b("SK"), b("I4")),
            (PB(6, 0, 128), b("cap"), Id), (PB(6, 128, 128), b("cap"), b("nIr")), (PB(6, 0, 128), b("wL"), b("IB")), (PB(6, 128, 128), b("wL"), nId)])
        ts(b("Bq"), PB(6, 128, 128), -1.5, A.is_gt, 4095.0, A.mult)
        tt(b(ek, c_(128 + M + L * t, L)), PB(6, 0, 128), b("Bq"), A.max)
        if last:
            dma("Y", "out", T.ykids[:, M + L * t:M + L * t + L], b("EF", c_(128 + M + L * t, L)), 1.5)
            dma("S", "out", T.ynodes[:], b("X", c_(M, L * STEPS)), 1.5)
            dma("S", "out", T.ycand[:], x, 1.5)
            dma("S", "out", T.yspot[:], b("e2"), 1.5)

    def schedule():
        N = len(calls)
        WAKE = TUNE["wake"]
        for c in calls:
            c["dur"] = length(c["cost"], (TUNE["f"], 1.56, 3.8))
        succ = [[] for _ in range(N)]
        for c in calls:
            for m, w in c["pre"].items():
                succ[m].append((c["n"], WAKE + calls[m]["lat"] if w else 0.0))
        dur, eng = [c["dur"] for c in calls], [c["eng"] for c in calls]
        rest = [0.0] * N
        for n in range(N - 1, -1, -1):
            rest[n] = dur[n] + max([rest[m] + d for m, d in succ[n]] or [calls[n]["lat"]])

        pred = [[] for _ in range(N)]
        for n in range(N):
            for m, d in succ[n]:
                pred[m].append((n, d))
        tail = [c["lat"] for c in calls]

        def place(prio, back=False):
            nxt, prv = (pred, succ) if back else (succ, pred)
            left = [len(p) for p in prv]
            est, at, used = list(tail) if back else [0.0] * N, [0.0] * N, {k: [] for k in eng}
            ready = [n for n in range(N) if not left[n]]
            while ready:
                n = max(ready, key=lambda m: prio[m])
                ready.remove(n)
                t0, slots = est[n], used[eng[n]]
                j = len(slots)
                while j and slots[j - 1][1] > t0:
                    j -= 1
                while j < len(slots) and slots[j][0] < t0 + dur[n]:
                    t0 = max(t0, slots[j][1])
                    j += 1
                if dur[n]:
                    slots.insert(j, (t0, t0 + dur[n]))
                at[n] = t0
                for m, d in nxt[n]:
                    est[m] = max(est[m], t0 + dur[n] + d)
                    left[m] -= 1
                    if not left[m]:
                        ready.append(m)
            return max(at[n] + dur[n] + tail[n] for n in range(N)), at

        def sweep(prio):
            at = place(prio)[1]
            at = place([at[n] + dur[n] for n in range(N)], True)[1]
            prio = [at[n] + dur[n] for n in range(N)]
            return place(prio) + (prio,)

        cases = []
        for k in CASES:
            cases.append(([length(c["cost"], k) for c in calls],
                          [[(m, k[3] + calls[m]["lat"] * (k[4] if eng[m] == "A" else k[5]) if w else 0.0) for m, w in c["pre"].items()] for c in calls]))

        def spans(at):
            order, total = sorted(range(N), key=lambda n: (at[n], n)), 0.0
            for d, pre in cases:
                end, free = [0.0] * N, {k: 0.0 for k in eng}
                for n in order:
                    t0 = 0.0 if eng[n] == "A" else free[eng[n]]
                    for m, e in pre[n]:
                        if end[m] + e > t0:
                            t0 = end[m] + e
                    end[n] = free[eng[n]] = t0 + d[n]
                total += float(np.log(max(end[n] + tail[n] for n in range(N))))
            return float(np.exp(total / len(cases)))

        rng = np.random.RandomState(TUNE["seed"])
        span, at, prio = sweep(rest)
        best = spans(at)
        for _ in range(TUNE["tries"]):
            mid = span * float(rng.rand())
            span2, at2, new = sweep([p + TUNE["noise"] * r if abs(a - mid) < TUNE["reach"] else p for p, r, a in zip(prio, rng.randn(N).tolist(), at)])
            if span2 <= span * 1.01:
                mean = spans(at2)
                if mean <= best:
                    best, span, at, prio = mean, span2, at2, new
        ORDERS.update(span=span, mean=best, at=at, calls=calls)
        return sorted(range(N), key=lambda n: (at[n], n))

    if "order" not in ORDERS:
        ORDERS["order"] = schedule()
    for n in ORDERS["order"]:
        c = calls[n]
        eng = c["eng"]
        if eng == "A":
            snap[c["tok"]] = {}
            continue
        wait(eng, [calls[m]["tok"] for m, w in c["pre"].items() if w])
        i = c["fn"]()
        if c["kind"] == "c":
            cnt[eng] += 1
            i.then_inc(T.sem["s" + eng], 1)
            c["tok"] = ("s" + eng, cnt[eng])
        if c["tok"]:
            snap[c["tok"]] = dict(known[eng])
    for t in range(STEPS):
        for s in ("qo", "yo"):
            g.wait_ge(T.sem[s + str(t)], neng)
    g.wait_ge(T.sem.wloc, neng)
    wait("G", [("sV", cnt["V"]), ("sS", cnt["S"]), ("sP", cnt["P"]), ("sG", cnt["G"])] + [("d_" + k, n) for k, n in dcount.items()]
         + [("wrem", neng * (NB - 1))] + [(k + str(t), neng) for k in ("qa", "ya") for t in range(STEPS)])
